import numpy as np
import ml_dtypes


def mxq(x, axis, fmt="e4m3"):
    dtype, down = {"e4m3": (ml_dtypes.float8_e4m3fn, 7), "e5m2": (ml_dtypes.float8_e5m2, 14)}[fmt]
    v = np.moveaxis(np.asarray(x, np.float32).astype(ml_dtypes.bfloat16).astype(np.float64), axis, -1)
    blocks = v.reshape(v.shape[:-1] + (-1, 32))
    amax = np.abs(blocks).max(-1, keepdims=True)
    byte = np.maximum(np.where(amax > 0, np.frexp(amax)[1] - 1 + 127, 0) - down, 1)
    scale = np.exp2(byte - 127.0)
    codes = (blocks / scale).astype(np.float32).astype(dtype).astype(np.float64)
    return np.moveaxis((codes * scale).reshape(v.shape), -1, axis)


WIDE = False


def mx_kscale(k):
    if not WIDE:
        return np.ones(k)
    levels = np.array([10, -10, 5, -5, 0])
    if k % 512:
        return np.exp2(np.random.permutation(np.resize(levels, k // 32))).repeat(32)
    a = np.empty((k // 512, 16))
    for p in range(k // 512):
        a[p, :8] = np.random.permutation(np.resize(levels, 8))
        for g in range(8):
            far = levels[np.abs(levels - a[p, g]) >= 10]
            a[p, g + 8] = far[np.random.randint(len(far))]
    return np.exp2(a.ravel()).repeat(32)


def f64(x):
    return np.asarray(x).astype(np.float64)


def striped(idx):
    return np.tile(idx.reshape(-1, 16).T, (8, 1)).astype(np.uint16)


def unstriped(offs):
    return offs[:16].T.reshape(-1).astype(np.int64)


E2M1 = np.array([0.0, 0.5, 1.0, 1.5, 2.0, 3.0, 4.0, 6.0, -0.0, -0.5, -1.0, -1.5, -2.0, -3.0, -4.0, -6.0])


def pack_weight(w, fmt):
    k, n = w.shape
    w = f64(np.asarray(w, np.float32).astype(ml_dtypes.bfloat16)).reshape(k // 32, 32, n)
    amax = np.abs(w).max(1)
    if fmt == "e4m3":
        byte = np.frexp(amax)[1] - 1 + 127 - 7
    else:
        mant, ex = np.frexp(amax / 6.0)
        byte = np.where(mant > 0.5, ex, ex - 1) + 127
    byte = np.clip(np.where(amax > 0, byte, 1), 1, 254)
    scaled = (w * np.exp2(127.0 - byte)[:, None, :]).reshape(k, n).astype(np.float32)
    by_word = np.ascontiguousarray(scaled.reshape(k // 512, 128, 4, n).transpose(0, 1, 3, 2))
    if fmt == "e4m3":
        words = by_word.astype(ml_dtypes.float8_e4m3fn).view(np.uint8)
    else:
        c = by_word.astype(ml_dtypes.float4_e2m1fn).view(np.uint8) & 0xF
        words = (c[..., 0::2] | (c[..., 1::2] << 4)).reshape(k // 512, 128, 2 * n)
    return np.ascontiguousarray(words), np.ascontiguousarray(byte.astype(np.uint8).reshape(k // 512, 16, n))


def unpack_weight(words, scales, fmt):
    g, _, n = scales.shape
    words = np.ascontiguousarray(words).reshape(g, 128, n, -1)
    if fmt == "e4m3":
        vals = words.view(ml_dtypes.float8_e4m3fn).astype(np.float64)
    else:
        nib = np.empty((g, 128, n, 4), np.uint8)
        nib[..., 0::2] = words & 0xF
        nib[..., 1::2] = words >> 4
        vals = E2M1[nib]
    vals = vals * np.repeat(np.exp2(scales.astype(np.float64) - 127.0), 8, axis=1)[..., None]
    return vals.transpose(0, 1, 3, 2).reshape(g * 512, n)


def gelu(v):
    return 0.5 * v * (1.0 + np.tanh(np.sqrt(2.0 / np.pi) * (v + 0.044715 * v**3)))


K, T, S, T2, S2, N = 1024, 4096, 1536, 2048, 1024, 256

def setup_inputs():
    n = np.random.standard_normal
    s = mx_kscale(K)[:, None]
    u = mx_kscale(S)[:, None]
    tab_words, tab_scales = pack_weight(n((K, T)) * s, "e4m3")
    tab2_words, tab2_scales = pack_weight(n((K, T2)) / s / np.sqrt(K), "e4m3")
    w4_words, w4_scales = pack_weight(2.0 * n((S, N)) / u / np.sqrt(S), "e2m1")
    w = (1.2 * n((S, N)) / u / np.sqrt(S)).astype(np.float32)
    th = (0.5 + 0.2 * n(S2)).astype(np.float32)
    g = (np.exp(0.3 * n(S)) * u[:, 0]).astype(np.float32)
    return {"tab_words": tab_words, "tab_scales": tab_scales,
            "offs": striped(np.random.permutation(T)[:S]),
            "tab2_words": tab2_words, "tab2_scales": tab2_scales,
            "offs2": striped(np.random.permutation(T2)[:S2]),
            "th": th, "g": g, "w4_words": w4_words, "w4_scales": w4_scales, "w": w}

def reference(tab_words, tab_scales, offs, tab2_words, tab2_scales, offs2, th, g, w4_words, w4_scales, w):
    v = unpack_weight(tab_words, tab_scales, "e4m3")[:, unstriped(offs)]
    v2 = unpack_weight(tab2_words, tab2_scales, "e4m3")[:, unstriped(offs2)]
    a = v.T @ v2
    z = np.maximum(a - f64(th)[None, :], 0.0) * f64(g)[:, None]
    zq = mxq(z, 0, "e4m3")
    w4 = unpack_weight(w4_words, w4_scales, "e2m1")
    wq = mxq(f64(w), 0, "e4m3")
    return w4.T @ zq + wq.T @ zq

@@ -1,0 +1,233 @@
+from contextlib import ExitStack
+
+import concourse.mybir as mybir
+from concourse.masks import make_identity
+
+K, T, S, T2, S2, N = 1024, 4096, 1536, 2048, 1024, 256
+FLOPS = 2 * K * S * S2 + 2 * 2 * S * N * S2
+
+F32 = mybir.dt.float32
+BF16 = mybir.dt.bfloat16
+I32 = mybir.dt.int32
+U32 = mybir.dt.uint32
+U16 = mybir.dt.uint16
+U8 = mybir.dt.uint8
+FP8X4 = mybir.dt.float8_e4m3fn_x4
+FP4X4 = mybir.dt.float4_e2m1fn_x4
+ACT = mybir.ActivationFunctionType
+ALU = mybir.AluOpType
+
+P = 128
+PACK = 4
+PASS = P * PACK
+BANK = 512
+K_PASSES = K // PASS
+I_PASSES = S // PASS
+J_HALVES = S2 // BANK
+N_TILES = N // P
+QUADRANTS = 4
+LIST_ROWS = 16
+LAST_SPLIT = 176
+
+
+def tile_list_similarity_join_aggregate_kernel(
+    tc, tab_words, tab_scales, offs, tab2_words, tab2_scales, offs2, th, g, w4_words, w4_scales, w, out
+):
+    nc = tc.nc
+    with ExitStack() as ctx:
+        keep = ctx.enter_context(tc.tile_pool(name="keep", bufs=1))
+        work = ctx.enter_context(tc.tile_pool(name="work", bufs=3))
+        sim_psum = ctx.enter_context(tc.psum_pool(name="sim_psum", bufs=4))
+        out_psum = ctx.enter_context(tc.psum_pool(name="out_psum", bufs=4))
+
+        th_sb = keep.tile([P, J_HALVES, PACK], F32, name="th_sb")
+        g_sb = keep.tile([P, I_PASSES, PACK], F32, name="g_sb")
+
+        s2_tab = keep.tile([P, T2 // 4], I32, name="s2_tab", align_bytes=64)
+        s1_tab = keep.tile([P, T // 4], I32, name="s1_tab", align_bytes=64)
+        w4_s = keep.tile([P, I_PASSES, N // 4], I32, name="w4_s", align_bytes=64)
+        nc.gpsimd.memset(s2_tab[:], 0)
+        nc.vector.memset(s1_tab[:], 0)
+        nc.vector.memset(w4_s[:], 0)
+        ident = keep.tile([P, P], F32, name="ident")
+        make_identity(nc, ident[:])
+
+        list2 = keep.tile([P, S2 // LIST_ROWS], U16, name="list2")
+        list1 = keep.tile([P, S // LIST_ROWS], U16, name="list1")
+        t2 = [keep.tile([P, T2], I32, name=f"t2_{a}", align_bytes=64) for a in range(K_PASSES)]
+        t1 = [keep.tile([P, T], I32, name=f"t1_{a}", align_bytes=64) for a in range(K_PASSES)]
+        nc.sync.dma_start(list2[:], offs2)
+        nc.sync.dma_start(t2[0][:], tab2_words[0].rearrange("p t i -> p (t i)").bitcast(I32))
+        nc.sync.dma_start(th_sb[:], th.rearrange("(h p c) -> p h c", h=J_HALVES, c=PACK))
+        nc.sync.dma_start(g_sb[:], g.rearrange("(b p t) -> p b t", b=I_PASSES, t=PACK))
+        nc.sync.dma_start(t2[1][:], tab2_words[1].rearrange("p t i -> p (t i)").bitcast(I32))
+        nc.sync.dma_start(list1[:], offs)
+        for tile, scales in ((s2_tab, tab2_scales), (s1_tab, tab_scales)):
+            for q in range(QUADRANTS):
+                nc.sync.dma_start(
+                    tile[32 * q : 32 * q + 4 * K_PASSES, :], scales[:, 4 * q : 4 * q + 4, :].bitcast(I32)
+                )
+        for a in range(K_PASSES):
+            nc.sync.dma_start(t1[a][:], tab_words[a].rearrange("p t i -> p (t i)").bitcast(I32))
+        w_raw = [keep.tile([P, PACK, N], F32, name=f"w_raw{b}") for b in range(I_PASSES)]
+        w4_c = keep.tile([P, I_PASSES, 2 * N // 4], I32, name="w4_c", align_bytes=64)
+        nc.sync.dma_start(w_raw[0][:], w[0:PASS, :].rearrange("(p t) n -> p t n", t=PACK))
+        nc.sync.dma_start(w4_c[:], w4_words.rearrange("b p c -> p b c").bitcast(I32))
+        for q in range(QUADRANTS):
+            nc.gpsimd.dma_start(
+                w4_s[32 * q : 32 * q + 4, :, :],
+                w4_scales[:, 4 * q : 4 * q + 4, :].rearrange("b r n -> r b n").bitcast(I32),
+            )
+        for b in range(1, I_PASSES):
+            nc.sync.dma_start(w_raw[b][:], w[b * PASS : (b + 1) * PASS, :].rearrange("(p t) n -> p t n", t=PACK))
+
+        th_all = keep.tile([P, J_HALVES, P, PACK], F32, name="th_all")
+        for h in range(J_HALVES):
+            spread = out_psum.tile([P, PACK, P], F32, name="spread", tag="acc")
+            for c in range(PACK):
+                nc.tensor.transpose(spread[:, c, :], th_sb[:, h, c : c + 1].to_broadcast([P, P]), ident[:])
+            nc.scalar.copy(th_all[:, h, :, :], spread[:].rearrange("m c p -> m p c"))
+        gth = []
+        for b in range(I_PASSES):
+            for t in range(PACK):
+                tile = keep.tile([P, S2], F32, name=f"gth{b}_{t}")
+                nc.scalar.activation(
+                    tile[:], th_all[:].rearrange("m h p c -> m (h p c)"), ACT.Copy, scale=g_sb[:, b, t : t + 1]
+                )
+                gth.append(tile)
+
+        v2 = [keep.tile([P, S2], U32, name=f"v2_{a}", align_bytes=64) for a in range(K_PASSES)]
+        v2_s = keep.tile([P, S2], U8, name="v2_s", align_bytes=64)
+        for a in range(K_PASSES):
+            nc.vector.tensor_copy(v2[a][:], t2[a][:].bitcast(U32).indirect(list2[:]))
+        nc.vector.tensor_copy(v2_s[:], s2_tab[:].bitcast(U8).indirect(list2[:]))
+
+        cols = PASS // LIST_ROWS
+        v1 = [[keep.tile([P, PASS], U32, name=f"v1_{a}_{b}", align_bytes=64) for b in range(I_PASSES)] for a in range(K_PASSES)]
+        s1_raw = [keep.tile([P, PASS], U8, name=f"s1_raw{b}", align_bytes=64) for b in range(I_PASSES)]
+        v1_s = [keep.tile([P, PASS], U8, name=f"v1_s{b}", align_bytes=64) for b in range(I_PASSES)]
+
+        def gather_words(a, b):
+            nc.vector.tensor_copy(
+                v1[a][b][:].rearrange("p (t m) -> p m t", t=PACK),
+                t1[a][:].bitcast(U32).indirect(list1[:, b * cols : (b + 1) * cols]),
+            )
+
+        def gather_scales(b):
+            nc.vector.tensor_copy(s1_raw[b][:], s1_tab[:].bitcast(U8).indirect(list1[:, b * cols : (b + 1) * cols]))
+
+        def permute_scales(b):
+            nc.vector.tensor_copy(
+                v1_s[b][:].rearrange("p (t m) -> p t m", t=PACK), s1_raw[b][:].rearrange("p (m t) -> p t m", t=PACK)
+            )
+
+        wq = [keep.tile([P, N], U32, name=f"wq{b}", align_bytes=64) for b in range(I_PASSES)]
+        wq_s = [keep.tile([P, N], U8, name=f"wq_s{b}", align_bytes=64) for b in range(I_PASSES)]
+
+        def quantize_w(b):
+            grouped = work.tile([P, N, PACK], BF16, name="w_grouped", align_bytes=64)
+            nc.scalar.copy(
+                grouped[:].rearrange("p (c i) t -> p c t i", i=4), w_raw[b][:].rearrange("p t (c i) -> p c t i", i=4)
+            )
+            nc.vector.quantize_mx(
+                out=wq[b][:].bitcast(FP8X4), scales=wq_s[b][:], in_=grouped[:].rearrange("p n t -> p (n t)")
+            )
+
+        acc = {}
+
+        def excess(b, h):
+            x = work.tile([P, PACK, BANK], BF16, name="x", align_bytes=64)
+            j = slice(h * BANK, (h + 1) * BANK)
+            for t in range(PACK):
+                sim = sim_psum.tile([P, BANK], F32, name="sim")
+                m = slice(t * P, (t + 1) * P)
+                for a in range(K_PASSES):
+                    nc.tensor.matmul_mx(
+                        out=sim[:],
+                        lhsT=v1[a][b][:, m].bitcast(FP8X4),
+                        lhsT_scale=v1_s[b][4 * a : P, m],
+                        rhs=v2[a][:, j].bitcast(FP8X4),
+                        rhs_scale=v2_s[4 * a : P, j],
+                        start=(a == 0),
+                        stop=(a == K_PASSES - 1),
+                    )
+                nc.vector.scalar_tensor_tensor(
+                    out=x[:, t, :],
+                    in0=sim[:],
+                    scalar=g_sb[:, b, t : t + 1],
+                    in1=gth[PACK * b + t][:, j],
+                    op0=ALU.mult,
+                    op1=ALU.subtract,
+                )
+            z = work.tile([P, BANK, PACK], BF16, name="z", align_bytes=64)
+            split = LAST_SPLIT if (b, h) == (I_PASSES - 1, J_HALVES - 1) else BANK
+            nc.scalar.activation(
+                z[:, 0:split, :].rearrange("p (c i) t -> p c t i", i=4),
+                x[:, :, 0:split].rearrange("p t (c i) -> p c t i", i=4),
+                ACT.Relu,
+            )
+            if split < BANK:
+                nc.vector.tensor_scalar(
+                    out=z[:, split:BANK, :].rearrange("p (c i) t -> p c t i", i=4),
+                    in0=x[:, :, split:BANK].rearrange("p t (c i) -> p c t i", i=4),
+                    scalar1=0.0,
+                    scalar2=None,
+                    op0=ALU.max,
+                )
+            return z
+
+        def aggregate(b, h, z):
+            zq = work.tile([P, BANK], U32, name="zq", align_bytes=64)
+            zq_s = work.tile([P, BANK], U8, name="zq_s", align_bytes=64)
+            nc.vector.quantize_mx(out=zq[:].bitcast(FP8X4), scales=zq_s[:], in_=z[:].rearrange("p j t -> p (j t)"))
+            for n in range(N_TILES):
+                if b == 0:
+                    acc[n, h] = out_psum.tile([P, BANK], F32, name="acc", tag="acc")
+                m = slice(n * P, (n + 1) * P)
+                nc.tensor.matmul_mx(
+                    out=acc[n, h][:],
+                    lhsT=w4_c[:, b, :].bitcast(U8)[:, 2 * n * P : 2 * (n + 1) * P].bitcast(FP4X4),
+                    lhsT_scale=w4_s[:, b, :].bitcast(U8)[:, m],
+                    rhs=zq[:].bitcast(FP8X4),
+                    rhs_scale=zq_s[:],
+                    start=(b == 0),
+                    stop=False,
+                )
+                nc.tensor.matmul_mx(
+                    out=acc[n, h][:],
+                    lhsT=wq[b][:, m].bitcast(FP8X4),
+                    lhsT_scale=wq_s[b][:, m],
+                    rhs=zq[:].bitcast(FP8X4),
+                    rhs_scale=zq_s[:],
+                    start=False,
+                    stop=(b == I_PASSES - 1),
+                )
+                if b == I_PASSES - 1:
+                    result = keep.tile([P, BANK], F32, name=f"result{n}_{h}")
+                    if n == 0 or h < J_HALVES - 1:
+                        nc.scalar.copy(result[:], acc[n, h][:])
+                    else:
+                        nc.vector.tensor_copy(result[:], acc[n, h][:])
+                    nc.sync.dma_start(out[m, h * BANK : (h + 1) * BANK], result[:])
+
+        gather_scales(0)
+        gather_words(0, 0)
+        permute_scales(0)
+        gather_words(1, 0)
+        for b in range(1, I_PASSES):
+            gather_scales(b)
+            gather_words(0, b)
+            permute_scales(b)
+
+        units = [(b, h) for b in range(I_PASSES) for h in range(J_HALVES)]
+        pending = None
+        for b, h in units:
+            z = excess(b, h)
+            if h == 0:
+                quantize_w(b)
+                if b + 1 < I_PASSES:
+                    gather_words(1, b + 1)
+            if pending is not None:
+                aggregate(*pending)
+            pending = (b, h, z)
+        aggregate(*pending)

@@ -27,7 +27,7 @@ J_HALVES = S2 // BANK
 N_TILES = N // P
 QUADRANTS = 4
 LIST_ROWS = 16
-LAST_SPLIT = 176
+LAST_SPLIT = 80
 
 
 def tile_list_similarity_join_aggregate_kernel(
@@ -36,7 +36,7 @@ def tile_list_similarity_join_aggregate_kernel(
     nc = tc.nc
     with ExitStack() as ctx:
         keep = ctx.enter_context(tc.tile_pool(name="keep", bufs=1))
-        work = ctx.enter_context(tc.tile_pool(name="work", bufs=3))
+        work = ctx.enter_context(tc.tile_pool(name="work", bufs=4))
         sim_psum = ctx.enter_context(tc.psum_pool(name="sim_psum", bufs=4))
         out_psum = ctx.enter_context(tc.psum_pool(name="out_psum", bufs=4))
 
@@ -58,7 +58,7 @@ def tile_list_similarity_join_aggregate_kernel(
         t1 = [keep.tile([P, T], I32, name=f"t1_{a}", align_bytes=64) for a in range(K_PASSES)]
         nc.sync.dma_start(list2[:], offs2)
         nc.sync.dma_start(t2[0][:], tab2_words[0].rearrange("p t i -> p (t i)").bitcast(I32))
-        nc.sync.dma_start(th_sb[:], th.rearrange("(h p c) -> p h c", h=J_HALVES, c=PACK))
+        nc.scalar.dma_start(th_sb[:], th.rearrange("(h p c) -> p h c", h=J_HALVES, c=PACK))
         nc.sync.dma_start(g_sb[:], g.rearrange("(b p t) -> p b t", b=I_PASSES, t=PACK))
         nc.sync.dma_start(t2[1][:], tab2_words[1].rearrange("p t i -> p (t i)").bitcast(I32))
         nc.sync.dma_start(list1[:], offs)
@@ -74,7 +74,7 @@ def tile_list_similarity_join_aggregate_kernel(
         nc.sync.dma_start(w_raw[0][:], w[0:PASS, :].rearrange("(p t) n -> p t n", t=PACK))
         nc.sync.dma_start(w4_c[:], w4_words.rearrange("b p c -> p b c").bitcast(I32))
         for q in range(QUADRANTS):
-            nc.gpsimd.dma_start(
+            nc.sync.dma_start(
                 w4_s[32 * q : 32 * q + 4, :, :],
                 w4_scales[:, 4 * q : 4 * q + 4, :].rearrange("b r n -> r b n").bitcast(I32),
             )
@@ -135,51 +135,52 @@ def tile_list_similarity_join_aggregate_kernel(
 
         acc = {}
 
-        def excess(b, h):
-            x = work.tile([P, PACK, BANK], BF16, name="x", align_bytes=64)
-            j = slice(h * BANK, (h + 1) * BANK)
-            for t in range(PACK):
-                sim = sim_psum.tile([P, BANK], F32, name="sim")
-                m = slice(t * P, (t + 1) * P)
-                for a in range(K_PASSES):
-                    nc.tensor.matmul_mx(
-                        out=sim[:],
-                        lhsT=v1[a][b][:, m].bitcast(FP8X4),
-                        lhsT_scale=v1_s[b][4 * a : P, m],
-                        rhs=v2[a][:, j].bitcast(FP8X4),
-                        rhs_scale=v2_s[4 * a : P, j],
-                        start=(a == 0),
-                        stop=(a == K_PASSES - 1),
-                    )
-                nc.vector.scalar_tensor_tensor(
-                    out=x[:, t, :],
-                    in0=sim[:],
-                    scalar=g_sb[:, b, t : t + 1],
-                    in1=gth[PACK * b + t][:, j],
-                    op0=ALU.mult,
-                    op1=ALU.subtract,
+        def excess(b, h, t, x, c0, c1):
+            j = slice(h * BANK + c0, h * BANK + c1)
+            sim = sim_psum.tile([P, c1 - c0], F32, name="sim")
+            m = slice(t * P, (t + 1) * P)
+            for a in range(K_PASSES):
+                nc.tensor.matmul_mx(
+                    out=sim[:],
+                    lhsT=v1[a][b][:, m].bitcast(FP8X4),
+                    lhsT_scale=v1_s[b][4 * a : P, m],
+                    rhs=v2[a][:, j].bitcast(FP8X4),
+                    rhs_scale=v2_s[4 * a : P, j],
+                    start=(a == 0),
+                    stop=(a == K_PASSES - 1),
                 )
-            z = work.tile([P, BANK, PACK], BF16, name="z", align_bytes=64)
-            split = LAST_SPLIT if (b, h) == (I_PASSES - 1, J_HALVES - 1) else BANK
+            nc.vector.scalar_tensor_tensor(
+                out=x[:, t, c0:c1],
+                in0=sim[:],
+                scalar=g_sb[:, b, t : t + 1],
+                in1=gth[PACK * b + t][:, j],
+                op0=ALU.mult,
+                op1=ALU.subtract,
+            )
+
+        def rectify(x, z, c0, split, c1):
             nc.scalar.activation(
-                z[:, 0:split, :].rearrange("p (c i) t -> p c t i", i=4),
-                x[:, :, 0:split].rearrange("p t (c i) -> p c t i", i=4),
+                z[:, c0:split, :].rearrange("p (c i) t -> p c t i", i=4),
+                x[:, :, c0:split].rearrange("p t (c i) -> p c t i", i=4),
                 ACT.Relu,
             )
-            if split < BANK:
+            if split < c1:
                 nc.vector.tensor_scalar(
-                    out=z[:, split:BANK, :].rearrange("p (c i) t -> p c t i", i=4),
-                    in0=x[:, :, split:BANK].rearrange("p t (c i) -> p c t i", i=4),
+                    out=z[:, split:c1, :].rearrange("p (c i) t -> p c t i", i=4),
+                    in0=x[:, :, split:c1].rearrange("p t (c i) -> p c t i", i=4),
                     scalar1=0.0,
                     scalar2=None,
                     op0=ALU.max,
                 )
-            return z
 
-        def aggregate(b, h, z):
+        def aggregate(b, h, z, pieces=1):
             zq = work.tile([P, BANK], U32, name="zq", align_bytes=64)
             zq_s = work.tile([P, BANK], U8, name="zq_s", align_bytes=64)
-            nc.vector.quantize_mx(out=zq[:].bitcast(FP8X4), scales=zq_s[:], in_=z[:].rearrange("p j t -> p (j t)"))
+            for piece in range(pieces):
+                c = slice(piece * BANK // pieces, (piece + 1) * BANK // pieces)
+                nc.vector.quantize_mx(
+                    out=zq[:, c].bitcast(FP8X4), scales=zq_s[:, c], in_=z[:, c, :].rearrange("p j t -> p (j t)")
+                )
             for n in range(N_TILES):
                 if b == 0:
                     acc[n, h] = out_psum.tile([P, BANK], F32, name="acc", tag="acc")
@@ -220,14 +221,30 @@ def tile_list_similarity_join_aggregate_kernel(
             permute_scales(b)
 
         units = [(b, h) for b in range(I_PASSES) for h in range(J_HALVES)]
-        pending = None
-        for b, h in units:
-            z = excess(b, h)
-            if h == 0:
-                quantize_w(b)
-                if b + 1 < I_PASSES:
-                    gather_words(1, b + 1)
-            if pending is not None:
-                aggregate(*pending)
-            pending = (b, h, z)
-        aggregate(*pending)
+        last = len(units) - 1
+        half = BANK // 2
+        zs = []
+        for u, (b, h) in enumerate(units):
+            x = work.tile([P, PACK, BANK], BF16, name="x", align_bytes=64)
+            z = work.tile([P, BANK, PACK], BF16, name="z", align_bytes=64)
+            zs.append(z)
+            if u < last:
+                for t in range(PACK):
+                    if t == PACK // 2 and u >= 2:
+                        aggregate(*units[u - 2], zs[u - 2])
+                    excess(b, h, t, x, 0, BANK)
+                rectify(x, z, 0, BANK, BANK)
+            else:
+                for t in range(PACK):
+                    excess(b, h, t, x, 0, half)
+                rectify(x, z, 0, half, half)
+                aggregate(*units[u - 2], zs[u - 2])
+                for t in range(PACK):
+                    excess(b, h, t, x, half, BANK)
+                aggregate(*units[u - 1], zs[u - 1])
+                rectify(x, z, half, half + LAST_SPLIT, BANK)
+            if u < I_PASSES:
+                quantize_w(u)
+            if h == 0 and b + 1 < I_PASSES:
+                gather_words(1, b + 1)
+        aggregate(*units[last], zs[last], pieces=2)

@@ -60,13 +60,17 @@ def tile_list_similarity_join_aggregate_kernel(
         nc.sync.dma_start(t2[0][:], tab2_words[0].rearrange("p t i -> p (t i)").bitcast(I32))
         nc.scalar.dma_start(th_sb[:], th.rearrange("(h p c) -> p h c", h=J_HALVES, c=PACK))
         nc.sync.dma_start(g_sb[:], g.rearrange("(b p t) -> p b t", b=I_PASSES, t=PACK))
-        nc.sync.dma_start(t2[1][:], tab2_words[1].rearrange("p t i -> p (t i)").bitcast(I32))
         nc.sync.dma_start(list1[:], offs)
-        for tile, scales in ((s2_tab, tab2_scales), (s1_tab, tab_scales)):
-            for q in range(QUADRANTS):
-                nc.sync.dma_start(
-                    tile[32 * q : 32 * q + 4 * K_PASSES, :], scales[:, 4 * q : 4 * q + 4, :].bitcast(I32)
-                )
+        for q in range(QUADRANTS):
+            nc.sync.dma_start(
+                s2_tab[32 * q : 32 * q + 4 * K_PASSES, :], tab2_scales[:, 4 * q : 4 * q + 4, :].bitcast(I32)
+            )
+        nc.sync.dma_start(t2[1][:], tab2_words[1].rearrange("p t i -> p (t i)").bitcast(I32))
+        for q in range(QUADRANTS):
+            queue = nc.gpsimd if q < 2 else nc.sync
+            queue.dma_start(
+                s1_tab[32 * q : 32 * q + 4 * K_PASSES, :], tab_scales[:, 4 * q : 4 * q + 4, :].bitcast(I32)
+            )
         for a in range(K_PASSES):
             nc.sync.dma_start(t1[a][:], tab_words[a].rearrange("p t i -> p (t i)").bitcast(I32))
         w_raw = [keep.tile([P, PACK, N], F32, name=f"w_raw{b}") for b in range(I_PASSES)]
@@ -98,9 +102,9 @@ def tile_list_similarity_join_aggregate_kernel(
 
         v2 = [keep.tile([P, S2], U32, name=f"v2_{a}", align_bytes=64) for a in range(K_PASSES)]
         v2_s = keep.tile([P, S2], U8, name="v2_s", align_bytes=64)
-        for a in range(K_PASSES):
-            nc.vector.tensor_copy(v2[a][:], t2[a][:].bitcast(U32).indirect(list2[:]))
+        nc.vector.tensor_copy(v2[0][:], t2[0][:].bitcast(U32).indirect(list2[:]))
         nc.vector.tensor_copy(v2_s[:], s2_tab[:].bitcast(U8).indirect(list2[:]))
+        nc.vector.tensor_copy(v2[1][:], t2[1][:].bitcast(U32).indirect(list2[:]))
 
         cols = PASS // LIST_ROWS
         v1 = [[keep.tile([P, PASS], U32, name=f"v1_{a}_{b}", align_bytes=64) for b in range(I_PASSES)] for a in range(K_PASSES)]
@@ -137,7 +141,10 @@ def tile_list_similarity_join_aggregate_kernel(
 
         def excess(b, h, t, x, c0, c1):
             j = slice(h * BANK + c0, h * BANK + c1)
-            sim = sim_psum.tile([P, c1 - c0], F32, name="sim")
+            if (b, h) == (0, 1):
+                sim = out_psum.tile([P, c1 - c0], F32, name="sim", tag="acc")
+            else:
+                sim = sim_psum.tile([P, c1 - c0], F32, name="sim")
             m = slice(t * P, (t + 1) * P)
             for a in range(K_PASSES):
                 nc.tensor.matmul_mx(
@@ -207,18 +214,21 @@ def tile_list_similarity_join_aggregate_kernel(
                     result = keep.tile([P, BANK], F32, name=f"result{n}_{h}")
                     if n == 0 or h < J_HALVES - 1:
                         nc.scalar.copy(result[:], acc[n, h][:])
+                        nc.sync.dma_start(out[m, h * BANK : (h + 1) * BANK], result[:])
                     else:
-                        nc.vector.tensor_copy(result[:], acc[n, h][:])
-                    nc.sync.dma_start(out[m, h * BANK : (h + 1) * BANK], result[:])
+                        for c0 in range(0, BANK, BANK // 2):
+                            c = slice(c0, c0 + BANK // 2)
+                            nc.vector.tensor_copy(result[:, c], acc[n, h][:, c])
+                            nc.sync.dma_start(out[m, h * BANK + c0 : h * BANK + c0 + BANK // 2], result[:, c])
 
-        gather_scales(0)
+        for b in range(I_PASSES):
+            gather_scales(b)
+        for b in range(I_PASSES):
+            permute_scales(b)
         gather_words(0, 0)
-        permute_scales(0)
         gather_words(1, 0)
         for b in range(1, I_PASSES):
-            gather_scales(b)
             gather_words(0, b)
-            permute_scales(b)
 
         units = [(b, h) for b in range(I_PASSES) for h in range(J_HALVES)]
         last = len(units) - 1

@@ -60,30 +60,27 @@ def tile_list_similarity_join_aggregate_kernel(
         nc.sync.dma_start(t2[0][:], tab2_words[0].rearrange("p t i -> p (t i)").bitcast(I32))
         nc.scalar.dma_start(th_sb[:], th.rearrange("(h p c) -> p h c", h=J_HALVES, c=PACK))
         nc.sync.dma_start(g_sb[:], g.rearrange("(b p t) -> p b t", b=I_PASSES, t=PACK))
-        nc.sync.dma_start(list1[:], offs)
-        for q in range(QUADRANTS):
-            nc.sync.dma_start(
-                s2_tab[32 * q : 32 * q + 4 * K_PASSES, :], tab2_scales[:, 4 * q : 4 * q + 4, :].bitcast(I32)
-            )
         nc.sync.dma_start(t2[1][:], tab2_words[1].rearrange("p t i -> p (t i)").bitcast(I32))
-        for q in range(QUADRANTS):
-            queue = nc.gpsimd if q < 2 else nc.sync
-            queue.dma_start(
-                s1_tab[32 * q : 32 * q + 4 * K_PASSES, :], tab_scales[:, 4 * q : 4 * q + 4, :].bitcast(I32)
-            )
+        nc.sync.dma_start(list1[:], offs)
+        for tile, scales in ((s2_tab, tab2_scales), (s1_tab, tab_scales)):
+            for q in range(QUADRANTS):
+                nc.sync.dma_start(
+                    tile[32 * q : 32 * q + 4 * K_PASSES, :], scales[:, 4 * q : 4 * q + 4, :].bitcast(I32)
+                )
         for a in range(K_PASSES):
             nc.sync.dma_start(t1[a][:], tab_words[a].rearrange("p t i -> p (t i)").bitcast(I32))
-        w_raw = [keep.tile([P, PACK, N], F32, name=f"w_raw{b}") for b in range(I_PASSES)]
+        w_raw = [
+            keep.tile([P, PACK, N], F32, name=f"w_raw{b}", tag=f"w_raw{b}", align_bytes=64) for b in range(I_PASSES)
+        ]
         w4_c = keep.tile([P, I_PASSES, 2 * N // 4], I32, name="w4_c", align_bytes=64)
-        nc.sync.dma_start(w_raw[0][:], w[0:PASS, :].rearrange("(p t) n -> p t n", t=PACK))
+        for b in range(I_PASSES):
+            nc.sync.dma_start(w_raw[b][:], w[b * PASS : (b + 1) * PASS, :].rearrange("(p t) n -> p t n", t=PACK))
         nc.sync.dma_start(w4_c[:], w4_words.rearrange("b p c -> p b c").bitcast(I32))
         for q in range(QUADRANTS):
             nc.sync.dma_start(
                 w4_s[32 * q : 32 * q + 4, :, :],
                 w4_scales[:, 4 * q : 4 * q + 4, :].rearrange("b r n -> r b n").bitcast(I32),
             )
-        for b in range(1, I_PASSES):
-            nc.sync.dma_start(w_raw[b][:], w[b * PASS : (b + 1) * PASS, :].rearrange("(p t) n -> p t n", t=PACK))
 
         th_all = keep.tile([P, J_HALVES, P, PACK], F32, name="th_all")
         for h in range(J_HALVES):
@@ -103,8 +100,8 @@ def tile_list_similarity_join_aggregate_kernel(
         v2 = [keep.tile([P, S2], U32, name=f"v2_{a}", align_bytes=64) for a in range(K_PASSES)]
         v2_s = keep.tile([P, S2], U8, name="v2_s", align_bytes=64)
         nc.vector.tensor_copy(v2[0][:], t2[0][:].bitcast(U32).indirect(list2[:]))
-        nc.vector.tensor_copy(v2_s[:], s2_tab[:].bitcast(U8).indirect(list2[:]))
         nc.vector.tensor_copy(v2[1][:], t2[1][:].bitcast(U32).indirect(list2[:]))
+        nc.vector.tensor_copy(v2_s[:], s2_tab[:].bitcast(U8).indirect(list2[:]))
 
         cols = PASS // LIST_ROWS
         v1 = [[keep.tile([P, PASS], U32, name=f"v1_{a}_{b}", align_bytes=64) for b in range(I_PASSES)] for a in range(K_PASSES)]
@@ -128,11 +125,15 @@ def tile_list_similarity_join_aggregate_kernel(
         wq = [keep.tile([P, N], U32, name=f"wq{b}", align_bytes=64) for b in range(I_PASSES)]
         wq_s = [keep.tile([P, N], U8, name=f"wq_s{b}", align_bytes=64) for b in range(I_PASSES)]
 
-        def quantize_w(b):
-            grouped = work.tile([P, N, PACK], BF16, name="w_grouped", align_bytes=64)
+        w_grouped = [keep.tile([P, N, PACK], BF16, name=f"w_grouped{b}", align_bytes=64) for b in range(I_PASSES)]
+        for b in range(I_PASSES):
             nc.scalar.copy(
-                grouped[:].rearrange("p (c i) t -> p c t i", i=4), w_raw[b][:].rearrange("p t (c i) -> p c t i", i=4)
+                w_grouped[b][:].rearrange("p (c i) t -> p c t i", i=4),
+                w_raw[b][:].rearrange("p t (c i) -> p c t i", i=4),
             )
+
+        def quantize_w(b):
+            grouped = w_grouped[b]
             nc.vector.quantize_mx(
                 out=wq[b][:].bitcast(FP8X4), scales=wq_s[b][:], in_=grouped[:].rearrange("p n t -> p (n t)")
             )
@@ -236,7 +237,10 @@ def tile_list_similarity_join_aggregate_kernel(
         zs = []
         for u, (b, h) in enumerate(units):
             x = work.tile([P, PACK, BANK], BF16, name="x", align_bytes=64)
-            z = work.tile([P, BANK, PACK], BF16, name="z", align_bytes=64)
+            if u == 0:
+                z = keep.tile([P, BANK, PACK], BF16, name="z", tag=f"w_raw{I_PASSES - 1}", align_bytes=64)
+            else:
+                z = work.tile([P, BANK, PACK], BF16, name="z", align_bytes=64)
             zs.append(z)
             if u < last:
                 for t in range(PACK):

@@ -28,6 +28,7 @@ N_TILES = N // P
 QUADRANTS = 4
 LIST_ROWS = 16
 LAST_SPLIT = 80
+SHARED = (0, 1, 1, 1, 1, 0)
 
 
 def tile_list_similarity_join_aggregate_kernel(
@@ -157,14 +158,21 @@ def tile_list_similarity_join_aggregate_kernel(
                     start=(a == 0),
                     stop=(a == K_PASSES - 1),
                 )
-            nc.vector.scalar_tensor_tensor(
-                out=x[:, t, c0:c1],
-                in0=sim[:],
-                scalar=g_sb[:, b, t : t + 1],
-                in1=gth[PACK * b + t][:, j],
-                op0=ALU.mult,
-                op1=ALU.subtract,
-            )
+            if t < SHARED[J_HALVES * b + h]:
+                scaled = work.tile([P, BANK], F32, name="scaled")
+                nc.scalar.activation(scaled[:], sim[:], ACT.Copy, scale=g_sb[:, b, t : t + 1])
+                for d0 in range(0, BANK, BANK // 2):
+                    d = slice(d0, d0 + BANK // 2)
+                    nc.gpsimd.tensor_tensor(x[:, t, d], scaled[:, d], gth[PACK * b + t][:, j][:, d], ALU.subtract)
+            else:
+                nc.vector.scalar_tensor_tensor(
+                    out=x[:, t, c0:c1],
+                    in0=sim[:],
+                    scalar=g_sb[:, b, t : t + 1],
+                    in1=gth[PACK * b + t][:, j],
+                    op0=ALU.mult,
+                    op1=ALU.subtract,
+                )
 
         def rectify(x, z, c0, split, c1):
             nc.scalar.activation(
@@ -234,19 +242,29 @@ def tile_list_similarity_join_aggregate_kernel(
         units = [(b, h) for b in range(I_PASSES) for h in range(J_HALVES)]
         last = len(units) - 1
         half = BANK // 2
+        xs = []
         zs = []
-        for u, (b, h) in enumerate(units):
+
+        def open_unit(u):
             x = work.tile([P, PACK, BANK], BF16, name="x", align_bytes=64)
+            xs.append(x)
+            for t in range(SHARED[u]):
+                excess(*units[u], t, x, 0, BANK)
+
+        open_unit(0)
+        for u, (b, h) in enumerate(units):
+            x = xs[u]
             if u == 0:
                 z = keep.tile([P, BANK, PACK], BF16, name="z", tag=f"w_raw{I_PASSES - 1}", align_bytes=64)
             else:
                 z = work.tile([P, BANK, PACK], BF16, name="z", align_bytes=64)
             zs.append(z)
             if u < last:
-                for t in range(PACK):
+                for t in range(SHARED[u], PACK):
                     if t == PACK // 2 and u >= 2:
                         aggregate(*units[u - 2], zs[u - 2])
                     excess(b, h, t, x, 0, BANK)
+                open_unit(u + 1)
                 rectify(x, z, 0, BANK, BANK)
             else:
                 for t in range(PACK):

@@ -27,8 +27,8 @@ J_HALVES = S2 // BANK
 N_TILES = N // P
 QUADRANTS = 4
 LIST_ROWS = 16
-LAST_SPLIT = 80
-SHARED = (0, 1, 1, 1, 1, 0)
+LAST_SPLIT = 160
+SHARED = (0, 4, 0, 0, 0, 0)
 
 
 def tile_list_similarity_join_aggregate_kernel(
@@ -92,7 +92,7 @@ def tile_list_similarity_join_aggregate_kernel(
         gth = []
         for b in range(I_PASSES):
             for t in range(PACK):
-                tile = keep.tile([P, S2], F32, name=f"gth{b}_{t}")
+                tile = keep.tile([P, S2], F32, name=f"gth{b}_{t}", align_bytes=64)
                 nc.scalar.activation(
                     tile[:], th_all[:].rearrange("m h p c -> m (h p c)"), ACT.Copy, scale=g_sb[:, b, t : t + 1]
                 )
@@ -123,23 +123,33 @@ def tile_list_similarity_join_aggregate_kernel(
                 v1_s[b][:].rearrange("p (t m) -> p t m", t=PACK), s1_raw[b][:].rearrange("p (m t) -> p t m", t=PACK)
             )
 
-        wq = [keep.tile([P, N], U32, name=f"wq{b}", align_bytes=64) for b in range(I_PASSES)]
+        wq = {}
         wq_s = [keep.tile([P, N], U8, name=f"wq_s{b}", align_bytes=64) for b in range(I_PASSES)]
 
-        w_grouped = [keep.tile([P, N, PACK], BF16, name=f"w_grouped{b}", align_bytes=64) for b in range(I_PASSES)]
-        for b in range(I_PASSES):
+        w_grouped = {}
+
+        def round_w(b, tag):
+            w_grouped[b] = keep.tile([P, N, PACK], BF16, name=f"w_grouped{b}", tag=tag, align_bytes=64)
             nc.scalar.copy(
                 w_grouped[b][:].rearrange("p (c i) t -> p c t i", i=4),
                 w_raw[b][:].rearrange("p t (c i) -> p c t i", i=4),
             )
 
+        for b in range(I_PASSES - 1):
+            round_w(b, f"w_grouped{b}")
+
         def quantize_w(b):
             grouped = w_grouped[b]
+            if b == 0:
+                codes = keep.tile([P, I_PASSES * N], U32, name="wq", tag="w_raw1", align_bytes=64)
+                for c in range(I_PASSES):
+                    wq[c] = codes[:, c * N : (c + 1) * N]
             nc.vector.quantize_mx(
-                out=wq[b][:].bitcast(FP8X4), scales=wq_s[b][:], in_=grouped[:].rearrange("p n t -> p (n t)")
+                out=wq[b].bitcast(FP8X4), scales=wq_s[b][:], in_=grouped[:].rearrange("p n t -> p (n t)")
             )
 
         acc = {}
+        held = {}
 
         def excess(b, h, t, x, c0, c1):
             j = slice(h * BANK + c0, h * BANK + c1)
@@ -159,14 +169,15 @@ def tile_list_similarity_join_aggregate_kernel(
                     stop=(a == K_PASSES - 1),
                 )
             if t < SHARED[J_HALVES * b + h]:
-                scaled = work.tile([P, BANK], F32, name="scaled")
-                nc.scalar.activation(scaled[:], sim[:], ACT.Copy, scale=g_sb[:, b, t : t + 1])
-                for d0 in range(0, BANK, BANK // 2):
-                    d = slice(d0, d0 + BANK // 2)
-                    nc.gpsimd.tensor_tensor(x[:, t, d], scaled[:, d], gth[PACK * b + t][:, j][:, d], ALU.subtract)
+                if t == 0:
+                    shared = SHARED[J_HALVES * b + h]
+                    held[b, h] = keep.tile([P, shared, BANK], F32, name=f"scaled{b}{h}", tag="w_raw1", align_bytes=64)
+                scaled = held[b, h][:, t, :]
+                nc.scalar.activation(scaled, sim[:], ACT.Copy, scale=g_sb[:, b, t : t + 1])
+                nc.gpsimd.tensor_tensor(x[:, t, :], scaled, gth[PACK * b + t][:, j], ALU.subtract)
             else:
                 nc.vector.scalar_tensor_tensor(
-                    out=x[:, t, c0:c1],
+                    out=x[:, t, :],
                     in0=sim[:],
                     scalar=g_sb[:, b, t : t + 1],
                     in1=gth[PACK * b + t][:, j],
@@ -189,46 +200,49 @@ def tile_list_similarity_join_aggregate_kernel(
                     op0=ALU.max,
                 )
 
-        def aggregate(b, h, z, pieces=1):
-            zq = work.tile([P, BANK], U32, name="zq", align_bytes=64)
-            zq_s = work.tile([P, BANK], U8, name="zq_s", align_bytes=64)
-            for piece in range(pieces):
-                c = slice(piece * BANK // pieces, (piece + 1) * BANK // pieces)
-                nc.vector.quantize_mx(
-                    out=zq[:, c].bitcast(FP8X4), scales=zq_s[:, c], in_=z[:, c, :].rearrange("p j t -> p (j t)")
-                )
+        def aggregate(b, h, z, c0=0, c1=BANK):
+            width = c1 - c0
+            zq = work.tile([P, width], U32, name="zq", align_bytes=64)
+            zq_s = work.tile([P, width], U8, name="zq_s", align_bytes=64)
+            nc.vector.quantize_mx(
+                out=zq[:].bitcast(FP8X4), scales=zq_s[:], in_=z[:].rearrange("p j t -> p (j t)")
+            )
+            closes = b == I_PASSES - 1 and c1 == BANK
+            fp4_width = BANK if width == BANK else P
             for n in range(N_TILES):
                 if b == 0:
                     acc[n, h] = out_psum.tile([P, BANK], F32, name="acc", tag="acc")
                 m = slice(n * P, (n + 1) * P)
+                for d0 in range(0, width, fp4_width):
+                    d = slice(d0, d0 + fp4_width)
+                    nc.tensor.matmul_mx(
+                        out=acc[n, h][:, c0 + d0 : c0 + d0 + fp4_width],
+                        lhsT=w4_c[:, b, :].bitcast(U8)[:, 2 * n * P : 2 * (n + 1) * P].bitcast(FP4X4),
+                        lhsT_scale=w4_s[:, b, :].bitcast(U8)[:, m],
+                        rhs=zq[:, d].bitcast(FP8X4),
+                        rhs_scale=zq_s[:, d],
+                        start=(b == 0),
+                        stop=False,
+                    )
                 nc.tensor.matmul_mx(
-                    out=acc[n, h][:],
-                    lhsT=w4_c[:, b, :].bitcast(U8)[:, 2 * n * P : 2 * (n + 1) * P].bitcast(FP4X4),
-                    lhsT_scale=w4_s[:, b, :].bitcast(U8)[:, m],
-                    rhs=zq[:].bitcast(FP8X4),
-                    rhs_scale=zq_s[:],
-                    start=(b == 0),
-                    stop=False,
-                )
-                nc.tensor.matmul_mx(
-                    out=acc[n, h][:],
+                    out=acc[n, h][:, c0:c1],
                     lhsT=wq[b][:, m].bitcast(FP8X4),
                     lhsT_scale=wq_s[b][:, m],
                     rhs=zq[:].bitcast(FP8X4),
                     rhs_scale=zq_s[:],
                     start=False,
-                    stop=(b == I_PASSES - 1),
+                    stop=closes,
                 )
-                if b == I_PASSES - 1:
+                if closes:
                     result = keep.tile([P, BANK], F32, name=f"result{n}_{h}")
                     if n == 0 or h < J_HALVES - 1:
                         nc.scalar.copy(result[:], acc[n, h][:])
                         nc.sync.dma_start(out[m, h * BANK : (h + 1) * BANK], result[:])
                     else:
-                        for c0 in range(0, BANK, BANK // 2):
-                            c = slice(c0, c0 + BANK // 2)
-                            nc.vector.tensor_copy(result[:, c], acc[n, h][:, c])
-                            nc.sync.dma_start(out[m, h * BANK + c0 : h * BANK + c0 + BANK // 2], result[:, c])
+                        for d0 in range(0, BANK, BANK // 2):
+                            d = slice(d0, d0 + BANK // 2)
+                            nc.vector.tensor_copy(result[:, d], acc[n, h][:, d])
+                            nc.sync.dma_start(out[m, h * BANK + d0 : h * BANK + d0 + BANK // 2], result[:, d])
 
         for b in range(I_PASSES):
             gather_scales(b)
@@ -239,44 +253,46 @@ def tile_list_similarity_join_aggregate_kernel(
         for b in range(1, I_PASSES):
             gather_words(0, b)
 
-        units = [(b, h) for b in range(I_PASSES) for h in range(J_HALVES)]
-        last = len(units) - 1
         half = BANK // 2
+        pieces = [(b, h, 0, BANK) for b in range(I_PASSES) for h in range(J_HALVES)]
+        pieces[-1:] = [(I_PASSES - 1, J_HALVES - 1, 0, half), (I_PASSES - 1, J_HALVES - 1, half, BANK)]
+        last = len(pieces) - 1
         xs = []
         zs = []
 
-        def open_unit(u):
-            x = work.tile([P, PACK, BANK], BF16, name="x", align_bytes=64)
+        def open_piece(u):
+            b, h, c0, c1 = pieces[u]
+            x = work.tile([P, PACK, c1 - c0], BF16, name="x", align_bytes=64, bufs=4)
             xs.append(x)
-            for t in range(SHARED[u]):
-                excess(*units[u], t, x, 0, BANK)
+            for t in range(SHARED[J_HALVES * b + h]):
+                excess(b, h, t, x, c0, c1)
 
-        open_unit(0)
-        for u, (b, h) in enumerate(units):
+        def finish(u):
+            b, h, c0, c1 = pieces[u]
+            aggregate(b, h, zs[u], c0, c1)
+
+        open_piece(0)
+        for u, (b, h, c0, c1) in enumerate(pieces):
             x = xs[u]
+            width = c1 - c0
             if u == 0:
-                z = keep.tile([P, BANK, PACK], BF16, name="z", tag=f"w_raw{I_PASSES - 1}", align_bytes=64)
+                z = keep.tile([P, width, PACK], BF16, name="z", tag=f"w_raw{I_PASSES - 1}", align_bytes=64)
             else:
-                z = work.tile([P, BANK, PACK], BF16, name="z", align_bytes=64)
+                z = work.tile([P, width, PACK], BF16, name="z", align_bytes=64)
             zs.append(z)
+            for t in range(SHARED[J_HALVES * b + h], PACK):
+                excess(b, h, t, x, c0, c1)
             if u < last:
-                for t in range(SHARED[u], PACK):
-                    if t == PACK // 2 and u >= 2:
-                        aggregate(*units[u - 2], zs[u - 2])
-                    excess(b, h, t, x, 0, BANK)
-                open_unit(u + 1)
-                rectify(x, z, 0, BANK, BANK)
-            else:
-                for t in range(PACK):
-                    excess(b, h, t, x, 0, half)
-                rectify(x, z, 0, half, half)
-                aggregate(*units[u - 2], zs[u - 2])
-                for t in range(PACK):
-                    excess(b, h, t, x, half, BANK)
-                aggregate(*units[u - 1], zs[u - 1])
-                rectify(x, z, half, half + LAST_SPLIT, BANK)
-            if u < I_PASSES:
-                quantize_w(u)
+                open_piece(u + 1)
+            if u == 2:
+                for c in range(I_PASSES):
+                    quantize_w(c)
+            if u >= 2:
+                finish(u - 2)
+            if u == 0:
+                round_w(I_PASSES - 1, "gth0_0")
+            rectify(x, z, 0, width if u < last else LAST_SPLIT, width)
             if h == 0 and b + 1 < I_PASSES:
                 gather_words(1, b + 1)
-        aggregate(*units[last], zs[last], pieces=2)
+        for u in range(last + 1 - 2, last + 1):
+            finish(u)

@@ -28,7 +28,7 @@ N_TILES = N // P
 QUADRANTS = 4
 LIST_ROWS = 16
 LAST_SPLIT = 160
-SHARED = (0, 4, 0, 0, 0, 0)
+SHARED = (4, 0, 0, 0, 0, 0)
 
 
 def tile_list_similarity_join_aggregate_kernel(
@@ -61,15 +61,15 @@ def tile_list_similarity_join_aggregate_kernel(
         nc.sync.dma_start(t2[0][:], tab2_words[0].rearrange("p t i -> p (t i)").bitcast(I32))
         nc.scalar.dma_start(th_sb[:], th.rearrange("(h p c) -> p h c", h=J_HALVES, c=PACK))
         nc.sync.dma_start(g_sb[:], g.rearrange("(b p t) -> p b t", b=I_PASSES, t=PACK))
-        nc.sync.dma_start(t2[1][:], tab2_words[1].rearrange("p t i -> p (t i)").bitcast(I32))
         nc.sync.dma_start(list1[:], offs)
         for tile, scales in ((s2_tab, tab2_scales), (s1_tab, tab_scales)):
             for q in range(QUADRANTS):
                 nc.sync.dma_start(
                     tile[32 * q : 32 * q + 4 * K_PASSES, :], scales[:, 4 * q : 4 * q + 4, :].bitcast(I32)
                 )
-        for a in range(K_PASSES):
+        for a in reversed(range(K_PASSES)):
             nc.sync.dma_start(t1[a][:], tab_words[a].rearrange("p t i -> p (t i)").bitcast(I32))
+        nc.sync.dma_start(t2[1][:], tab2_words[1].rearrange("p t i -> p (t i)").bitcast(I32))
         w_raw = [
             keep.tile([P, PACK, N], F32, name=f"w_raw{b}", tag=f"w_raw{b}", align_bytes=64) for b in range(I_PASSES)
         ]
@@ -101,7 +101,6 @@ def tile_list_similarity_join_aggregate_kernel(
         v2 = [keep.tile([P, S2], U32, name=f"v2_{a}", align_bytes=64) for a in range(K_PASSES)]
         v2_s = keep.tile([P, S2], U8, name="v2_s", align_bytes=64)
         nc.vector.tensor_copy(v2[0][:], t2[0][:].bitcast(U32).indirect(list2[:]))
-        nc.vector.tensor_copy(v2[1][:], t2[1][:].bitcast(U32).indirect(list2[:]))
         nc.vector.tensor_copy(v2_s[:], s2_tab[:].bitcast(U8).indirect(list2[:]))
 
         cols = PASS // LIST_ROWS
@@ -153,7 +152,7 @@ def tile_list_similarity_join_aggregate_kernel(
 
         def excess(b, h, t, x, c0, c1):
             j = slice(h * BANK + c0, h * BANK + c1)
-            if (b, h) == (0, 1):
+            if (b, h) == (0, 0):
                 sim = out_psum.tile([P, c1 - c0], F32, name="sim", tag="acc")
             else:
                 sim = sim_psum.tile([P, c1 - c0], F32, name="sim")
@@ -233,37 +232,47 @@ def tile_list_similarity_join_aggregate_kernel(
                     start=False,
                     stop=closes,
                 )
-                if closes:
-                    result = keep.tile([P, BANK], F32, name=f"result{n}_{h}")
-                    if n == 0 or h < J_HALVES - 1:
-                        nc.scalar.copy(result[:], acc[n, h][:])
-                        nc.sync.dma_start(out[m, h * BANK : (h + 1) * BANK], result[:])
-                    else:
-                        for d0 in range(0, BANK, BANK // 2):
-                            d = slice(d0, d0 + BANK // 2)
-                            nc.vector.tensor_copy(result[:, d], acc[n, h][:, d])
-                            nc.sync.dma_start(out[m, h * BANK + d0 : h * BANK + d0 + BANK // 2], result[:, d])
+
+        def store_early(h):
+            result = keep.tile([P, N_TILES, BANK], F32, name="early", tag=f"x{last}", align_bytes=64)
+            for n in range(N_TILES):
+                nc.scalar.copy(result[:, n, :], acc[n, h][:])
+                nc.sync.dma_start(out[n * P : (n + 1) * P, h * BANK : (h + 1) * BANK], result[:, n, :])
+
+        def store_last(h):
+            first = keep.tile([P, BANK], F32, name="first")
+            nc.scalar.copy(first[:], acc[0, h][:])
+            nc.sync.dma_start(out[0:P, h * BANK : (h + 1) * BANK], first[:])
+            second = keep.tile([P, BANK], F32, name="second")
+            for d0 in range(0, BANK, BANK // 2):
+                d = slice(d0, d0 + BANK // 2)
+                nc.vector.tensor_copy(second[:, d], acc[1, h][:, d])
+                nc.sync.dma_start(out[P : 2 * P, h * BANK + d0 : h * BANK + d0 + BANK // 2], second[:, d])
 
         for b in range(I_PASSES):
             gather_scales(b)
         for b in range(I_PASSES):
             permute_scales(b)
-        gather_words(0, 0)
-        gather_words(1, 0)
-        for b in range(1, I_PASSES):
-            gather_words(0, b)
+        for a in reversed(range(K_PASSES)):
+            for b in range(I_PASSES):
+                gather_words(a, b)
+        for h in range(J_HALVES):
+            nc.vector.tensor_copy(
+                v2[1][:, h * BANK : (h + 1) * BANK], t2[1][:].bitcast(U32).indirect(list2[:, h * cols : (h + 1) * cols])
+            )
 
         half = BANK // 2
         pieces = [(b, h, 0, BANK) for b in range(I_PASSES) for h in range(J_HALVES)]
         pieces[-1:] = [(I_PASSES - 1, J_HALVES - 1, 0, half), (I_PASSES - 1, J_HALVES - 1, half, BANK)]
+        pieces[0:2] = [pieces[1], pieces[0]]
         last = len(pieces) - 1
-        xs = []
+        xs = {}
         zs = []
 
         def open_piece(u):
             b, h, c0, c1 = pieces[u]
-            x = work.tile([P, PACK, c1 - c0], BF16, name="x", align_bytes=64, bufs=4)
-            xs.append(x)
+            x = keep.tile([P, PACK, c1 - c0], BF16, name=f"x{u}", align_bytes=64)
+            xs[u] = x
             for t in range(SHARED[J_HALVES * b + h]):
                 excess(b, h, t, x, c0, c1)
 
@@ -271,18 +280,17 @@ def tile_list_similarity_join_aggregate_kernel(
             b, h, c0, c1 = pieces[u]
             aggregate(b, h, zs[u], c0, c1)
 
+        open_piece(1)
         open_piece(0)
         for u, (b, h, c0, c1) in enumerate(pieces):
             x = xs[u]
             width = c1 - c0
-            if u == 0:
-                z = keep.tile([P, width, PACK], BF16, name="z", tag=f"w_raw{I_PASSES - 1}", align_bytes=64)
-            else:
-                z = work.tile([P, width, PACK], BF16, name="z", align_bytes=64)
+            tag = f"x{u - 2}" if u > 1 else ("gth0_1", "z1")[u]
+            z = keep.tile([P, width, PACK], BF16, name=f"z{u}", tag=tag, align_bytes=64)
             zs.append(z)
             for t in range(SHARED[J_HALVES * b + h], PACK):
                 excess(b, h, t, x, c0, c1)
-            if u < last:
+            if 0 < u < last:
                 open_piece(u + 1)
             if u == 2:
                 for c in range(I_PASSES):
@@ -292,7 +300,7 @@ def tile_list_similarity_join_aggregate_kernel(
             if u == 0:
                 round_w(I_PASSES - 1, "gth0_0")
             rectify(x, z, 0, width if u < last else LAST_SPLIT, width)
-            if h == 0 and b + 1 < I_PASSES:
-                gather_words(1, b + 1)
-        for u in range(last + 1 - 2, last + 1):
-            finish(u)
+        finish(last - 1)
+        store_early(0)
+        finish(last)
+        store_last(1)

@@ -27,8 +27,8 @@ J_HALVES = S2 // BANK
 N_TILES = N // P
 QUADRANTS = 4
 LIST_ROWS = 16
-LAST_SPLIT = 160
-SHARED = (4, 0, 0, 0, 0, 0)
+LAST_SPLIT = 128
+SHARED = (4, 0, 1, 0, 0, 0)
 
 
 def tile_list_similarity_join_aggregate_kernel(
@@ -59,8 +59,8 @@ def tile_list_similarity_join_aggregate_kernel(
         t1 = [keep.tile([P, T], I32, name=f"t1_{a}", align_bytes=64) for a in range(K_PASSES)]
         nc.sync.dma_start(list2[:], offs2)
         nc.sync.dma_start(t2[0][:], tab2_words[0].rearrange("p t i -> p (t i)").bitcast(I32))
-        nc.scalar.dma_start(th_sb[:], th.rearrange("(h p c) -> p h c", h=J_HALVES, c=PACK))
-        nc.sync.dma_start(g_sb[:], g.rearrange("(b p t) -> p b t", b=I_PASSES, t=PACK))
+        nc.scalar.dma_start(th_sb[:], th.rearrange("(p h c) -> p h c", h=J_HALVES, c=PACK))
+        nc.scalar.dma_start(g_sb[:], g.rearrange("(b p t) -> p b t", b=I_PASSES, t=PACK))
         nc.sync.dma_start(list1[:], offs)
         for tile, scales in ((s2_tab, tab2_scales), (s1_tab, tab_scales)):
             for q in range(QUADRANTS):
@@ -83,18 +83,18 @@ def tile_list_similarity_join_aggregate_kernel(
                 w4_scales[:, 4 * q : 4 * q + 4, :].rearrange("b r n -> r b n").bitcast(I32),
             )
 
-        th_all = keep.tile([P, J_HALVES, P, PACK], F32, name="th_all")
+        th_all = keep.tile([P, P, J_HALVES, PACK], F32, name="th_all")
         for h in range(J_HALVES):
             spread = out_psum.tile([P, PACK, P], F32, name="spread", tag="acc")
             for c in range(PACK):
                 nc.tensor.transpose(spread[:, c, :], th_sb[:, h, c : c + 1].to_broadcast([P, P]), ident[:])
-            nc.scalar.copy(th_all[:, h, :, :], spread[:].rearrange("m c p -> m p c"))
+            nc.scalar.copy(th_all[:, :, h, :], spread[:].rearrange("m c p -> m p c"))
         gth = []
         for b in range(I_PASSES):
             for t in range(PACK):
                 tile = keep.tile([P, S2], F32, name=f"gth{b}_{t}", align_bytes=64)
                 nc.scalar.activation(
-                    tile[:], th_all[:].rearrange("m h p c -> m (h p c)"), ACT.Copy, scale=g_sb[:, b, t : t + 1]
+                    tile[:], th_all[:].rearrange("m p h c -> m (p h c)"), ACT.Copy, scale=g_sb[:, b, t : t + 1]
                 )
                 gth.append(tile)
 
@@ -148,7 +148,7 @@ def tile_list_similarity_join_aggregate_kernel(
             )
 
         acc = {}
-        held = {}
+        held = keep.tile([P, sum(SHARED), BANK], F32, name="held", tag="w_raw1", align_bytes=64)
 
         def excess(b, h, t, x, c0, c1):
             j = slice(h * BANK + c0, h * BANK + c1)
@@ -168,10 +168,7 @@ def tile_list_similarity_join_aggregate_kernel(
                     stop=(a == K_PASSES - 1),
                 )
             if t < SHARED[J_HALVES * b + h]:
-                if t == 0:
-                    shared = SHARED[J_HALVES * b + h]
-                    held[b, h] = keep.tile([P, shared, BANK], F32, name=f"scaled{b}{h}", tag="w_raw1", align_bytes=64)
-                scaled = held[b, h][:, t, :]
+                scaled = held[:, sum(SHARED[: J_HALVES * b + h]) + t, :]
                 nc.scalar.activation(scaled, sim[:], ACT.Copy, scale=g_sb[:, b, t : t + 1])
                 nc.gpsimd.tensor_tensor(x[:, t, :], scaled, gth[PACK * b + t][:, j], ALU.subtract)
             else:
@@ -290,7 +287,9 @@ def tile_list_similarity_join_aggregate_kernel(
             zs.append(z)
             for t in range(SHARED[J_HALVES * b + h], PACK):
                 excess(b, h, t, x, c0, c1)
-            if 0 < u < last:
+            if u == 0:
+                open_piece(2)
+            if 1 < u < last:
                 open_piece(u + 1)
             if u == 2:
                 for c in range(I_PASSES):

@@ -130,8 +130,8 @@ def tile_list_similarity_join_aggregate_kernel(
         def round_w(b, tag):
             w_grouped[b] = keep.tile([P, N, PACK], BF16, name=f"w_grouped{b}", tag=tag, align_bytes=64)
             nc.scalar.copy(
-                w_grouped[b][:].rearrange("p (c i) t -> p c t i", i=4),
-                w_raw[b][:].rearrange("p t (c i) -> p c t i", i=4),
+                w_grouped[b][:].rearrange("p (c i) t -> p c t i", i=8),
+                w_raw[b][:].rearrange("p t (c i) -> p c t i", i=8),
             )
 
         for b in range(I_PASSES - 1):
@@ -183,14 +183,14 @@ def tile_list_similarity_join_aggregate_kernel(
 
         def rectify(x, z, c0, split, c1):
             nc.scalar.activation(
-                z[:, c0:split, :].rearrange("p (c i) t -> p c t i", i=4),
-                x[:, :, c0:split].rearrange("p t (c i) -> p c t i", i=4),
+                z[:, c0:split, :].rearrange("p (c i) t -> p c t i", i=8),
+                x[:, :, c0:split].rearrange("p t (c i) -> p c t i", i=8),
                 ACT.Relu,
             )
             if split < c1:
                 nc.vector.tensor_scalar(
-                    out=z[:, split:c1, :].rearrange("p (c i) t -> p c t i", i=4),
-                    in0=x[:, :, split:c1].rearrange("p t (c i) -> p c t i", i=4),
+                    out=z[:, split:c1, :].rearrange("p (c i) t -> p c t i", i=8),
+                    in0=x[:, :, split:c1].rearrange("p t (c i) -> p c t i", i=8),
                     scalar1=0.0,
                     scalar2=None,
                     op0=ALU.max,

@@ -58,15 +58,17 @@ def tile_list_similarity_join_aggregate_kernel(
         t2 = [keep.tile([P, T2], I32, name=f"t2_{a}", align_bytes=64) for a in range(K_PASSES)]
         t1 = [keep.tile([P, T], I32, name=f"t1_{a}", align_bytes=64) for a in range(K_PASSES)]
         nc.sync.dma_start(list2[:], offs2)
-        nc.sync.dma_start(t2[0][:], tab2_words[0].rearrange("p t i -> p (t i)").bitcast(I32))
         nc.scalar.dma_start(th_sb[:], th.rearrange("(p h c) -> p h c", h=J_HALVES, c=PACK))
-        nc.scalar.dma_start(g_sb[:], g.rearrange("(b p t) -> p b t", b=I_PASSES, t=PACK))
+        nc.sync.dma_start(g_sb[:], g.rearrange("(b p t) -> p b t", b=I_PASSES, t=PACK))
+        for q in range(QUADRANTS):
+            nc.sync.dma_start(
+                s2_tab[32 * q : 32 * q + 4 * K_PASSES, :], tab2_scales[:, 4 * q : 4 * q + 4, :].bitcast(I32)
+            )
+        nc.sync.dma_start(t2[0][:], tab2_words[0].rearrange("p t i -> p (t i)").bitcast(I32))
         nc.sync.dma_start(list1[:], offs)
-        for tile, scales in ((s2_tab, tab2_scales), (s1_tab, tab_scales)):
-            for q in range(QUADRANTS):
-                nc.sync.dma_start(
-                    tile[32 * q : 32 * q + 4 * K_PASSES, :], scales[:, 4 * q : 4 * q + 4, :].bitcast(I32)
-                )
+        for r in range(4):
+            for a in range(K_PASSES):
+                nc.sync.dma_start(s1_tab[4 * a + r : P : 32, :], tab_scales[a, r:16:4, :].bitcast(I32))
         for a in reversed(range(K_PASSES)):
             nc.sync.dma_start(t1[a][:], tab_words[a].rearrange("p t i -> p (t i)").bitcast(I32))
         nc.sync.dma_start(t2[1][:], tab2_words[1].rearrange("p t i -> p (t i)").bitcast(I32))
@@ -100,8 +102,8 @@ def tile_list_similarity_join_aggregate_kernel(
 
         v2 = [keep.tile([P, S2], U32, name=f"v2_{a}", align_bytes=64) for a in range(K_PASSES)]
         v2_s = keep.tile([P, S2], U8, name="v2_s", align_bytes=64)
-        nc.vector.tensor_copy(v2[0][:], t2[0][:].bitcast(U32).indirect(list2[:]))
         nc.vector.tensor_copy(v2_s[:], s2_tab[:].bitcast(U8).indirect(list2[:]))
+        nc.vector.tensor_copy(v2[0][:], t2[0][:].bitcast(U32).indirect(list2[:]))
 
         cols = PASS // LIST_ROWS
         v1 = [[keep.tile([P, PASS], U32, name=f"v1_{a}_{b}", align_bytes=64) for b in range(I_PASSES)] for a in range(K_PASSES)]

@@ -27,7 +27,7 @@ J_HALVES = S2 // BANK
 N_TILES = N // P
 QUADRANTS = 4
 LIST_ROWS = 16
-LAST_SPLIT = 128
+LAST_SPLIT = 192
 SHARED = (4, 0, 1, 0, 0, 0)
 
 

@@ -27,8 +27,7 @@ J_HALVES = S2 // BANK
 N_TILES = N // P
 QUADRANTS = 4
 LIST_ROWS = 16
-LAST_SPLIT = 192
-SHARED = (4, 0, 1, 0, 0, 0)
+HALF = BANK // 2
 
 
 def tile_list_similarity_join_aggregate_kernel(
@@ -37,9 +36,8 @@ def tile_list_similarity_join_aggregate_kernel(
     nc = tc.nc
     with ExitStack() as ctx:
         keep = ctx.enter_context(tc.tile_pool(name="keep", bufs=1))
-        work = ctx.enter_context(tc.tile_pool(name="work", bufs=4))
-        sim_psum = ctx.enter_context(tc.psum_pool(name="sim_psum", bufs=4))
-        out_psum = ctx.enter_context(tc.psum_pool(name="out_psum", bufs=4))
+        psum = ctx.enter_context(tc.psum_pool(name="psum", bufs=1))
+        banks = [psum.tile([P, BANK], F32, name=f"bank{i}") for i in range(8)]
 
         th_sb = keep.tile([P, J_HALVES, PACK], F32, name="th_sb")
         g_sb = keep.tile([P, I_PASSES, PACK], F32, name="g_sb")
@@ -55,8 +53,8 @@ def tile_list_similarity_join_aggregate_kernel(
 
         list2 = keep.tile([P, S2 // LIST_ROWS], U16, name="list2")
         list1 = keep.tile([P, S // LIST_ROWS], U16, name="list1")
-        t2 = [keep.tile([P, T2], I32, name=f"t2_{a}", align_bytes=64) for a in range(K_PASSES)]
-        t1 = [keep.tile([P, T], I32, name=f"t1_{a}", align_bytes=64) for a in range(K_PASSES)]
+        t2 = [keep.tile([P, T2], I32, name=f"t2_{a}", tag=f"t2_{a}", align_bytes=64) for a in range(K_PASSES)]
+        t1 = [keep.tile([P, T], I32, name=f"t1_{a}", tag=f"t1_{a}", align_bytes=64) for a in range(K_PASSES)]
         nc.sync.dma_start(list2[:], offs2)
         nc.scalar.dma_start(th_sb[:], th.rearrange("(p h c) -> p h c", h=J_HALVES, c=PACK))
         nc.sync.dma_start(g_sb[:], g.rearrange("(b p t) -> p b t", b=I_PASSES, t=PACK))
@@ -69,147 +67,132 @@ def tile_list_similarity_join_aggregate_kernel(
         for r in range(4):
             for a in range(K_PASSES):
                 nc.sync.dma_start(s1_tab[4 * a + r : P : 32, :], tab_scales[a, r:16:4, :].bitcast(I32))
-        for a in reversed(range(K_PASSES)):
-            nc.sync.dma_start(t1[a][:], tab_words[a].rearrange("p t i -> p (t i)").bitcast(I32))
         nc.sync.dma_start(t2[1][:], tab2_words[1].rearrange("p t i -> p (t i)").bitcast(I32))
+        nc.sync.dma_start(t1[1][:], tab_words[1].rearrange("p t i -> p (t i)").bitcast(I32))
+        nc.sync.dma_start(t1[0][:], tab_words[0].rearrange("p t i -> p (t i)").bitcast(I32))
+        arena = keep.tile([P, 26 * BANK], BF16, name="arena", align_bytes=64)
+
+        def slots(first, count):
+            return arena[:, first * BANK : (first + count) * BANK]
+
         w_raw = [
-            keep.tile([P, PACK, N], F32, name=f"w_raw{b}", tag=f"w_raw{b}", align_bytes=64) for b in range(I_PASSES)
+            keep.tile([P, PACK, N], F32, name=f"w_raw{b}", tag=f"w_raw{b}", align_bytes=64)[:] for b in range(I_PASSES)
         ]
         w4_c = keep.tile([P, I_PASSES, 2 * N // 4], I32, name="w4_c", align_bytes=64)
-        for b in range(I_PASSES):
-            nc.sync.dma_start(w_raw[b][:], w[b * PASS : (b + 1) * PASS, :].rearrange("(p t) n -> p t n", t=PACK))
+
+        def load_w(b):
+            nc.sync.dma_start(w_raw[b], w[b * PASS : (b + 1) * PASS, :].rearrange("(p t) n -> p t n", t=PACK))
+
+        load_w(0)
+        load_w(1)
         nc.sync.dma_start(w4_c[:], w4_words.rearrange("b p c -> p b c").bitcast(I32))
         for q in range(QUADRANTS):
             nc.sync.dma_start(
                 w4_s[32 * q : 32 * q + 4, :, :],
                 w4_scales[:, 4 * q : 4 * q + 4, :].rearrange("b r n -> r b n").bitcast(I32),
             )
+        load_w(2)
 
         th_all = keep.tile([P, P, J_HALVES, PACK], F32, name="th_all")
         for h in range(J_HALVES):
-            spread = out_psum.tile([P, PACK, P], F32, name="spread", tag="acc")
+            spread = banks[6 + h][:].rearrange("m (c p) -> m c p", c=PACK)
             for c in range(PACK):
                 nc.tensor.transpose(spread[:, c, :], th_sb[:, h, c : c + 1].to_broadcast([P, P]), ident[:])
-            nc.scalar.copy(th_all[:, :, h, :], spread[:].rearrange("m c p -> m p c"))
-        gth = []
+            nc.scalar.copy(th_all[:, :, h, :], spread.rearrange("m c p -> m p c"))
+        th_row = th_all[:].rearrange("m p h c -> m (p h c)")
+        gth = {}
         for b in range(I_PASSES):
             for t in range(PACK):
                 tile = keep.tile([P, S2], F32, name=f"gth{b}_{t}", align_bytes=64)
-                nc.scalar.activation(
-                    tile[:], th_all[:].rearrange("m p h c -> m (p h c)"), ACT.Copy, scale=g_sb[:, b, t : t + 1]
-                )
-                gth.append(tile)
+                nc.scalar.activation(tile[:], th_row, ACT.Copy, scale=g_sb[:, b, t : t + 1])
+                for h in range(J_HALVES):
+                    gth[b, t, h] = tile[:, h * BANK : (h + 1) * BANK]
 
+        cols = PASS // LIST_ROWS
         v2 = [keep.tile([P, S2], U32, name=f"v2_{a}", align_bytes=64) for a in range(K_PASSES)]
         v2_s = keep.tile([P, S2], U8, name="v2_s", align_bytes=64)
         nc.vector.tensor_copy(v2_s[:], s2_tab[:].bitcast(U8).indirect(list2[:]))
         nc.vector.tensor_copy(v2[0][:], t2[0][:].bitcast(U32).indirect(list2[:]))
 
-        cols = PASS // LIST_ROWS
         v1 = [[keep.tile([P, PASS], U32, name=f"v1_{a}_{b}", align_bytes=64) for b in range(I_PASSES)] for a in range(K_PASSES)]
         s1_raw = [keep.tile([P, PASS], U8, name=f"s1_raw{b}", align_bytes=64) for b in range(I_PASSES)]
         v1_s = [keep.tile([P, PASS], U8, name=f"v1_s{b}", align_bytes=64) for b in range(I_PASSES)]
 
-        def gather_words(a, b):
+        def gather_rows(a, b):
             nc.vector.tensor_copy(
                 v1[a][b][:].rearrange("p (t m) -> p m t", t=PACK),
                 t1[a][:].bitcast(U32).indirect(list1[:, b * cols : (b + 1) * cols]),
             )
 
-        def gather_scales(b):
+        for b in range(I_PASSES):
             nc.vector.tensor_copy(s1_raw[b][:], s1_tab[:].bitcast(U8).indirect(list1[:, b * cols : (b + 1) * cols]))
-
-        def permute_scales(b):
+        for b in range(I_PASSES):
             nc.vector.tensor_copy(
                 v1_s[b][:].rearrange("p (t m) -> p t m", t=PACK), s1_raw[b][:].rearrange("p (m t) -> p t m", t=PACK)
             )
+        nc.vector.tensor_copy(v2[1][:], t2[1][:].bitcast(U32).indirect(list2[:]))
+        for b in range(I_PASSES):
+            gather_rows(1, b)
+
+        units = [(b, h) for h in range(J_HALVES) for b in range(I_PASSES)]
+        sim_bank = {}
+        for u, row in enumerate(((4, 5, 6, 7), (4, 0, 5, 6), (7, 1, 2, 4), (0, 1, 2, 3), (0, 5, 6, 7), (3, 0, 5, 4))):
+            for t in range(PACK):
+                sim_bank[u, t] = banks[row[t]]
+        acc = {(0, 0): banks[1], (1, 0): banks[2], (0, 1): banks[6], (1, 1): banks[7]}
+
+        def sim_pass(u, t, a):
+            b, h = units[u]
+            m = slice(t * P, (t + 1) * P)
+            nc.tensor.matmul_mx(
+                out=sim_bank[u, t][:],
+                lhsT=v1[a][b][:, m].bitcast(FP8X4),
+                lhsT_scale=v1_s[b][4 * a : P, m],
+                rhs=v2[a][:, h * BANK : (h + 1) * BANK].bitcast(FP8X4),
+                rhs_scale=v2_s[4 * a : P, h * BANK : (h + 1) * BANK],
+                start=(a == 1),
+                stop=(a == 0),
+            )
+
+        def sim(u, t):
+            sim_pass(u, t, 1)
+            sim_pass(u, t, 0)
+
+        xs = {u: slots(first, PACK).rearrange("p (t j) -> p t j", t=PACK) for u, first in ((0, 12), (1, 8), (2, 16), (3, 20), (4, 0), (5, 8))}
+
+        def excess(u, t):
+            b, h = units[u]
+            nc.vector.scalar_tensor_tensor(
+                out=xs[u][:, t, :],
+                in0=sim_bank[u, t][:],
+                scalar=g_sb[:, b, t : t + 1],
+                in1=gth[b, t, h],
+                op0=ALU.mult,
+                op1=ALU.subtract,
+            )
+
+        def rectify(u, c0, c1, z, on_scalar):
+            dst = z.rearrange("p (c i t) -> p c t i", i=8, t=PACK)
+            src = xs[u][:, :, c0:c1].rearrange("p t (c i) -> p c t i", i=8)
+            if on_scalar:
+                nc.scalar.activation(dst, src, ACT.Relu)
+            else:
+                nc.vector.tensor_scalar(out=dst, in0=src, scalar1=0.0, scalar2=None, op0=ALU.max)
 
         wq = {}
-        wq_s = [keep.tile([P, N], U8, name=f"wq_s{b}", align_bytes=64) for b in range(I_PASSES)]
+        wq_s = {}
 
-        w_grouped = {}
+        def quantize(name, src, width, tag):
+            codes = keep.tile([P, width], U32, name=name, tag=tag, align_bytes=64)
+            scales = keep.tile([P, width], U8, name=name + "_s", align_bytes=64)
+            nc.vector.quantize_mx(out=codes[:].bitcast(FP8X4), scales=scales[:], in_=src)
+            return codes[:], scales[:]
 
-        def round_w(b, tag):
-            w_grouped[b] = keep.tile([P, N, PACK], BF16, name=f"w_grouped{b}", tag=tag, align_bytes=64)
-            nc.scalar.copy(
-                w_grouped[b][:].rearrange("p (c i) t -> p c t i", i=8),
-                w_raw[b][:].rearrange("p t (c i) -> p c t i", i=8),
-            )
-
-        for b in range(I_PASSES - 1):
-            round_w(b, f"w_grouped{b}")
-
-        def quantize_w(b):
-            grouped = w_grouped[b]
-            if b == 0:
-                codes = keep.tile([P, I_PASSES * N], U32, name="wq", tag="w_raw1", align_bytes=64)
-                for c in range(I_PASSES):
-                    wq[c] = codes[:, c * N : (c + 1) * N]
-            nc.vector.quantize_mx(
-                out=wq[b].bitcast(FP8X4), scales=wq_s[b][:], in_=grouped[:].rearrange("p n t -> p (n t)")
-            )
-
-        acc = {}
-        held = keep.tile([P, sum(SHARED), BANK], F32, name="held", tag="w_raw1", align_bytes=64)
-
-        def excess(b, h, t, x, c0, c1):
-            j = slice(h * BANK + c0, h * BANK + c1)
-            if (b, h) == (0, 0):
-                sim = out_psum.tile([P, c1 - c0], F32, name="sim", tag="acc")
-            else:
-                sim = sim_psum.tile([P, c1 - c0], F32, name="sim")
-            m = slice(t * P, (t + 1) * P)
-            for a in range(K_PASSES):
-                nc.tensor.matmul_mx(
-                    out=sim[:],
-                    lhsT=v1[a][b][:, m].bitcast(FP8X4),
-                    lhsT_scale=v1_s[b][4 * a : P, m],
-                    rhs=v2[a][:, j].bitcast(FP8X4),
-                    rhs_scale=v2_s[4 * a : P, j],
-                    start=(a == 0),
-                    stop=(a == K_PASSES - 1),
-                )
-            if t < SHARED[J_HALVES * b + h]:
-                scaled = held[:, sum(SHARED[: J_HALVES * b + h]) + t, :]
-                nc.scalar.activation(scaled, sim[:], ACT.Copy, scale=g_sb[:, b, t : t + 1])
-                nc.gpsimd.tensor_tensor(x[:, t, :], scaled, gth[PACK * b + t][:, j], ALU.subtract)
-            else:
-                nc.vector.scalar_tensor_tensor(
-                    out=x[:, t, :],
-                    in0=sim[:],
-                    scalar=g_sb[:, b, t : t + 1],
-                    in1=gth[PACK * b + t][:, j],
-                    op0=ALU.mult,
-                    op1=ALU.subtract,
-                )
-
-        def rectify(x, z, c0, split, c1):
-            nc.scalar.activation(
-                z[:, c0:split, :].rearrange("p (c i) t -> p c t i", i=8),
-                x[:, :, c0:split].rearrange("p t (c i) -> p c t i", i=8),
-                ACT.Relu,
-            )
-            if split < c1:
-                nc.vector.tensor_scalar(
-                    out=z[:, split:c1, :].rearrange("p (c i) t -> p c t i", i=8),
-                    in0=x[:, :, split:c1].rearrange("p t (c i) -> p c t i", i=8),
-                    scalar1=0.0,
-                    scalar2=None,
-                    op0=ALU.max,
-                )
-
-        def aggregate(b, h, z, c0=0, c1=BANK):
+        def aggregate(u, zq, zq_s, c0, c1, opens, closes):
+            b, h = units[u]
             width = c1 - c0
-            zq = work.tile([P, width], U32, name="zq", align_bytes=64)
-            zq_s = work.tile([P, width], U8, name="zq_s", align_bytes=64)
-            nc.vector.quantize_mx(
-                out=zq[:].bitcast(FP8X4), scales=zq_s[:], in_=z[:].rearrange("p j t -> p (j t)")
-            )
-            closes = b == I_PASSES - 1 and c1 == BANK
             fp4_width = BANK if width == BANK else P
             for n in range(N_TILES):
-                if b == 0:
-                    acc[n, h] = out_psum.tile([P, BANK], F32, name="acc", tag="acc")
                 m = slice(n * P, (n + 1) * P)
                 for d0 in range(0, width, fp4_width):
                     d = slice(d0, d0 + fp4_width)
@@ -219,89 +202,128 @@ def tile_list_similarity_join_aggregate_kernel(
                         lhsT_scale=w4_s[:, b, :].bitcast(U8)[:, m],
                         rhs=zq[:, d].bitcast(FP8X4),
                         rhs_scale=zq_s[:, d],
-                        start=(b == 0),
+                        start=opens,
                         stop=False,
                     )
                 nc.tensor.matmul_mx(
                     out=acc[n, h][:, c0:c1],
                     lhsT=wq[b][:, m].bitcast(FP8X4),
                     lhsT_scale=wq_s[b][:, m],
-                    rhs=zq[:].bitcast(FP8X4),
-                    rhs_scale=zq_s[:],
+                    rhs=zq.bitcast(FP8X4),
+                    rhs_scale=zq_s,
                     start=False,
                     stop=closes,
                 )
 
-        def store_early(h):
-            result = keep.tile([P, N_TILES, BANK], F32, name="early", tag=f"x{last}", align_bytes=64)
-            for n in range(N_TILES):
-                nc.scalar.copy(result[:, n, :], acc[n, h][:])
-                nc.sync.dma_start(out[n * P : (n + 1) * P, h * BANK : (h + 1) * BANK], result[:, n, :])
+        def scale_bank(u, t, scaled):
+            nc.scalar.activation(scaled, sim_bank[u, t][:], ACT.Copy, scale=g_sb[:, units[u][0], t : t + 1])
 
-        def store_last(h):
-            first = keep.tile([P, BANK], F32, name="first")
-            nc.scalar.copy(first[:], acc[0, h][:])
-            nc.sync.dma_start(out[0:P, h * BANK : (h + 1) * BANK], first[:])
-            second = keep.tile([P, BANK], F32, name="second")
-            for d0 in range(0, BANK, BANK // 2):
-                d = slice(d0, d0 + BANK // 2)
-                nc.vector.tensor_copy(second[:, d], acc[1, h][:, d])
-                nc.sync.dma_start(out[P : 2 * P, h * BANK + d0 : h * BANK + d0 + BANK // 2], second[:, d])
+        def subtract(u, t, scaled):
+            b, h = units[u]
+            nc.gpsimd.tensor_tensor(xs[u][:, t, :], scaled, gth[b, t, h], ALU.subtract)
 
-        for b in range(I_PASSES):
-            gather_scales(b)
-        for b in range(I_PASSES):
-            permute_scales(b)
-        for a in reversed(range(K_PASSES)):
-            for b in range(I_PASSES):
-                gather_words(a, b)
-        for h in range(J_HALVES):
-            nc.vector.tensor_copy(
-                v2[1][:, h * BANK : (h + 1) * BANK], t2[1][:].bitcast(U32).indirect(list2[:, h * cols : (h + 1) * cols])
+        def round_w_on_gpsimd(b, dst):
+            nc.gpsimd.tensor_scalar(
+                out=dst.rearrange("p (n t) -> p n t", t=PACK),
+                in0=w_raw[b].rearrange("p t n -> p n t"),
+                scalar1=1.0,
+                scalar2=0.0,
+                op0=ALU.mult,
+                op1=ALU.add,
             )
 
-        half = BANK // 2
-        pieces = [(b, h, 0, BANK) for b in range(I_PASSES) for h in range(J_HALVES)]
-        pieces[-1:] = [(I_PASSES - 1, J_HALVES - 1, 0, half), (I_PASSES - 1, J_HALVES - 1, half, BANK)]
-        pieces[0:2] = [pieces[1], pieces[0]]
-        last = len(pieces) - 1
-        xs = {}
-        zs = []
-
-        def open_piece(u):
-            b, h, c0, c1 = pieces[u]
-            x = keep.tile([P, PACK, c1 - c0], BF16, name=f"x{u}", align_bytes=64)
-            xs[u] = x
-            for t in range(SHARED[J_HALVES * b + h]):
-                excess(b, h, t, x, c0, c1)
-
-        def finish(u):
-            b, h, c0, c1 = pieces[u]
-            aggregate(b, h, zs[u], c0, c1)
-
-        open_piece(1)
-        open_piece(0)
-        for u, (b, h, c0, c1) in enumerate(pieces):
-            x = xs[u]
-            width = c1 - c0
-            tag = f"x{u - 2}" if u > 1 else ("gth0_1", "z1")[u]
-            z = keep.tile([P, width, PACK], BF16, name=f"z{u}", tag=tag, align_bytes=64)
-            zs.append(z)
-            for t in range(SHARED[J_HALVES * b + h], PACK):
-                excess(b, h, t, x, c0, c1)
-            if u == 0:
-                open_piece(2)
-            if 1 < u < last:
-                open_piece(u + 1)
-            if u == 2:
-                for c in range(I_PASSES):
-                    quantize_w(c)
-            if u >= 2:
-                finish(u - 2)
-            if u == 0:
-                round_w(I_PASSES - 1, "gth0_0")
-            rectify(x, z, 0, width if u < last else LAST_SPLIT, width)
-        finish(last - 1)
-        store_early(0)
-        finish(last)
-        store_last(1)
+        for u in (0, 3):
+            for t in range(PACK):
+                sim_pass(u, t, 1)
+        gather_rows(0, 0)
+        w_pair = keep.tile([P, 2 * N * PACK], BF16, name="w_pair", align_bytes=64)
+        nc.scalar.copy(
+            w_pair[:, : N * PACK].rearrange("p (c i t) -> p c t i", i=8, t=PACK),
+            w_raw[0].rearrange("p t (c i) -> p c t i", i=8),
+        )
+        held_first = keep.tile([P, 2, BANK], F32, name="held_first", align_bytes=64)
+        held = {
+            (0, 0): held_first[:, 0, :],
+            (3, 0): held_first[:, 1, :],
+            (3, 1): w_pair[:, N * PACK :].bitcast(F32),
+            (3, 2): keep.tile([P, BANK], F32, name="held3", tag="held3", align_bytes=64)[:],
+        }
+        for u, t in ((0, 0), (3, 0), (3, 1), (0, 1), (3, 2), (0, 2), (0, 3), (3, 3)):
+            sim_pass(u, t, 0)
+            if (u, t) in held:
+                scale_bank(u, t, held[u, t])
+        gather_rows(0, 1)
+        gather_rows(0, 2)
+        for u, t in held:
+            subtract(u, t, held[u, t])
+        round_w_on_gpsimd(1, w_pair[:, N * PACK :])
+        sim(1, 0)
+        sim(1, 1)
+        excess(0, 1)
+        sim(1, 2)
+        excess(0, 2)
+        sim(1, 3)
+        excess(0, 3)
+        for t in range(PACK - 1):
+            sim(2, t)
+        rectify(0, 0, BANK, slots(0, PACK), True)
+        excess(1, 0)
+        sim(2, 3)
+        for t in range(1, PACK):
+            excess(1, t)
+            sim(4, t - 1)
+        rectify(1, 0, BANK, slots(4, PACK), True)
+        excess(2, 0)
+        sim(4, 3)
+        for t in range(1, PACK):
+            excess(2, t)
+        sim(5, 3)
+        excess(3, 3)
+        sim(5, 0)
+        rectify(2, 0, BANK, slots(8, PACK), True)
+        sixth = keep.tile([P, BANK], F32, name="sixth", tag="sixth", align_bytes=64)
+        scale_bank(5, 3, sixth[:])
+        rectify(3, 0, BANK, slots(12, PACK), True)
+        zq, zq_s = quantize("zq01", slots(0, 2 * PACK), 2 * BANK, "w_raw1")
+        codes, scales = quantize("wq01", w_pair[:], 2 * N, "wq01")
+        for b in (0, 1):
+            wq[b] = codes[:, b * N : (b + 1) * N]
+            wq_s[b] = scales[:, b * N : (b + 1) * N]
+        aggregate(0, zq[:, :BANK], zq_s[:, :BANK], 0, BANK, True, False)
+        aggregate(1, zq[:, BANK:], zq_s[:, BANK:], 0, BANK, False, False)
+        w_last = slots(4, 2)
+        round_w_on_gpsimd(2, w_last)
+        excess(4, 0)
+        sim(5, 1)
+        excess(4, 1)
+        sim(5, 2)
+        excess(4, 2)
+        excess(4, 3)
+        rectify(4, 0, BANK, slots(16, PACK), True)
+        zq, zq_s = quantize("zq23", slots(8, 2 * PACK), 2 * BANK, "w_raw2")
+        wq[2], wq_s[2] = quantize("wq2", w_last, N, "wq2")
+        aggregate(2, zq[:, :BANK], zq_s[:, :BANK], 0, BANK, False, True)
+        aggregate(3, zq[:, BANK:], zq_s[:, BANK:], 0, BANK, True, False)
+        subtract(5, 3, sixth[:])
+        for t in range(PACK - 1):
+            excess(5, t)
+        rectify(5, 0, HALF, slots(20, 2), True)
+        zq, zq_s = quantize("zq4", slots(16, PACK), BANK, "sixth")
+        aggregate(4, zq, zq_s, 0, BANK, False, False)
+        rectify(5, HALF, BANK, slots(24, 2), False)
+        zq, zq_s = quantize("zq5b", slots(24, 2), HALF, "zq5b")
+        aggregate(5, zq, zq_s, HALF, BANK, False, False)
+        for n in range(N_TILES):
+            early = slots(8 + 2 * n, 2).bitcast(F32)
+            nc.scalar.copy(early, acc[n, 0][:])
+            nc.sync.dma_start(out[n * P : (n + 1) * P, 0:BANK], early)
+        zq, zq_s = quantize("zq5a", slots(20, 2), HALF, "zq5a")
+        aggregate(5, zq, zq_s, 0, HALF, False, True)
+        first = keep.tile([P, BANK], F32, name="first")
+        nc.scalar.copy(first[:], acc[0, 1][:])
+        nc.sync.dma_start(out[0:P, BANK:S2], first[:])
+        second = keep.tile([P, BANK], F32, name="second")
+        for d0 in range(0, BANK, HALF):
+            d = slice(d0, d0 + HALF)
+            nc.vector.tensor_copy(second[:, d], acc[1, 1][:, d])
+            nc.sync.dma_start(out[P : 2 * P, BANK + d0 : BANK + d0 + HALF], second[:, d])

@@ -70,7 +70,7 @@ def tile_list_similarity_join_aggregate_kernel(
         nc.sync.dma_start(t2[1][:], tab2_words[1].rearrange("p t i -> p (t i)").bitcast(I32))
         nc.sync.dma_start(t1[1][:], tab_words[1].rearrange("p t i -> p (t i)").bitcast(I32))
         nc.sync.dma_start(t1[0][:], tab_words[0].rearrange("p t i -> p (t i)").bitcast(I32))
-        arena = keep.tile([P, 26 * BANK], BF16, name="arena", align_bytes=64)
+        arena = keep.tile([P, 37 * BANK], BF16, name="arena", align_bytes=64)
 
         def slots(first, count):
             return arena[:, first * BANK : (first + count) * BANK]
@@ -136,10 +136,11 @@ def tile_list_similarity_join_aggregate_kernel(
 
         units = [(b, h) for h in range(J_HALVES) for b in range(I_PASSES)]
         sim_bank = {}
-        for u, row in enumerate(((4, 5, 6, 7), (4, 0, 5, 6), (7, 1, 2, 4), (0, 1, 2, 3), (0, 5, 6, 7), (3, 0, 5, 4))):
+        for u, row in enumerate(((0, 1, 2, 3), (4, 5, 6, 7), (0, 1, 2, 3), (4, 5, 6, 7), (0, 4, 5, 6), (3, 7, 0, 4))):
             for t in range(PACK):
                 sim_bank[u, t] = banks[row[t]]
-        acc = {(0, 0): banks[1], (1, 0): banks[2], (0, 1): banks[6], (1, 1): banks[7]}
+        acc = {(0, 0): banks[1], (1, 0): banks[2], (0, 1): banks[5], (1, 1): banks[6]}
+        acc_first = (banks[3], banks[7])
 
         def sim_pass(u, t, a):
             b, h = units[u]
@@ -158,7 +159,7 @@ def tile_list_similarity_join_aggregate_kernel(
             sim_pass(u, t, 1)
             sim_pass(u, t, 0)
 
-        xs = {u: slots(first, PACK).rearrange("p (t j) -> p t j", t=PACK) for u, first in ((0, 12), (1, 8), (2, 16), (3, 20), (4, 0), (5, 8))}
+        xs = {u: slots(first, PACK).rearrange("p (t j) -> p t j", t=PACK) for u, first in ((0, 23), (1, 15), (2, 19), (3, 31), (4, 11), (5, 15))}
 
         def excess(u, t):
             b, h = units[u]
@@ -188,32 +189,42 @@ def tile_list_similarity_join_aggregate_kernel(
             nc.vector.quantize_mx(out=codes[:].bitcast(FP8X4), scales=scales[:], in_=src)
             return codes[:], scales[:]
 
+        def add_product(dst, b, n, zq, zq_s, opens, closes):
+            width = zq.shape[1]
+            m = slice(n * P, (n + 1) * P)
+            fp4_width = BANK if width == BANK else P
+            for d0 in range(0, width, fp4_width):
+                d = slice(d0, d0 + fp4_width)
+                nc.tensor.matmul_mx(
+                    out=dst[:, d],
+                    lhsT=w4_c[:, b, :].bitcast(U8)[:, 2 * n * P : 2 * (n + 1) * P].bitcast(FP4X4),
+                    lhsT_scale=w4_s[:, b, :].bitcast(U8)[:, m],
+                    rhs=zq[:, d].bitcast(FP8X4),
+                    rhs_scale=zq_s[:, d],
+                    start=opens and d0 == 0,
+                    stop=False,
+                )
+            nc.tensor.matmul_mx(
+                out=dst,
+                lhsT=wq[b][:, m].bitcast(FP8X4),
+                lhsT_scale=wq_s[b][:, m],
+                rhs=zq.bitcast(FP8X4),
+                rhs_scale=zq_s,
+                start=False,
+                stop=closes,
+            )
+
         def aggregate(u, zq, zq_s, c0, c1, opens, closes):
             b, h = units[u]
-            width = c1 - c0
-            fp4_width = BANK if width == BANK else P
-            for n in range(N_TILES):
-                m = slice(n * P, (n + 1) * P)
-                for d0 in range(0, width, fp4_width):
-                    d = slice(d0, d0 + fp4_width)
-                    nc.tensor.matmul_mx(
-                        out=acc[n, h][:, c0 + d0 : c0 + d0 + fp4_width],
-                        lhsT=w4_c[:, b, :].bitcast(U8)[:, 2 * n * P : 2 * (n + 1) * P].bitcast(FP4X4),
-                        lhsT_scale=w4_s[:, b, :].bitcast(U8)[:, m],
-                        rhs=zq[:, d].bitcast(FP8X4),
-                        rhs_scale=zq_s[:, d],
-                        start=opens,
-                        stop=False,
-                    )
-                nc.tensor.matmul_mx(
-                    out=acc[n, h][:, c0:c1],
-                    lhsT=wq[b][:, m].bitcast(FP8X4),
-                    lhsT_scale=wq_s[b][:, m],
-                    rhs=zq.bitcast(FP8X4),
-                    rhs_scale=zq_s,
-                    start=False,
-                    stop=closes,
-                )
+            if h == 0:
+                for n in range(N_TILES):
+                    add_product(acc[n, 0][:], b, n, zq, zq_s, opens, closes)
+                return
+            for d0 in reversed(range(c0, c1, HALF)):
+                d = slice(d0 - c0, d0 - c0 + HALF)
+                for n in range(N_TILES):
+                    dst = acc[n, 1] if d0 else acc_first[n]
+                    add_product(dst[:, :HALF], b, n, zq[:, d], zq_s[:, d], opens, closes)
 
         def scale_bank(u, t, scaled):
             nc.scalar.activation(scaled, sim_bank[u, t][:], ACT.Copy, scale=g_sb[:, units[u][0], t : t + 1])
@@ -232,98 +243,102 @@ def tile_list_similarity_join_aggregate_kernel(
                 op1=ALU.add,
             )
 
-        for u in (0, 3):
+        def round_w(b):
+            nc.scalar.copy(
+                slots(7 + 2 * b, 2).rearrange("p (c i t) -> p c t i", i=8, t=PACK),
+                w_raw[b].rearrange("p t (c i) -> p c t i", i=8),
+            )
+
+        held = {u: keep.tile([P, BANK], F32, name=f"held{u}", tag=f"held{u}", align_bytes=64)[:] for u in range(6)}
+        for u in (0, 1):
             for t in range(PACK):
                 sim_pass(u, t, 1)
         gather_rows(0, 0)
-        w_pair = keep.tile([P, 2 * N * PACK], BF16, name="w_pair", align_bytes=64)
-        nc.scalar.copy(
-            w_pair[:, : N * PACK].rearrange("p (c i t) -> p c t i", i=8, t=PACK),
-            w_raw[0].rearrange("p t (c i) -> p c t i", i=8),
-        )
-        held_first = keep.tile([P, 2, BANK], F32, name="held_first", align_bytes=64)
-        held = {
-            (0, 0): held_first[:, 0, :],
-            (3, 0): held_first[:, 1, :],
-            (3, 1): w_pair[:, N * PACK :].bitcast(F32),
-            (3, 2): keep.tile([P, BANK], F32, name="held3", tag="held3", align_bytes=64)[:],
-        }
-        for u, t in ((0, 0), (3, 0), (3, 1), (0, 1), (3, 2), (0, 2), (0, 3), (3, 3)):
-            sim_pass(u, t, 0)
-            if (u, t) in held:
-                scale_bank(u, t, held[u, t])
+        round_w(0)
+        for t in range(PACK):
+            sim_pass(0, t, 0)
+        scale_bank(0, 0, held[0])
+        round_w(1)
         gather_rows(0, 1)
+        for t in range(PACK):
+            sim_pass(1, t, 0)
+        scale_bank(1, 0, held[1])
+        scale_bank(1, 1, held[2])
         gather_rows(0, 2)
-        for u, t in held:
-            subtract(u, t, held[u, t])
-        round_w_on_gpsimd(1, w_pair[:, N * PACK :])
-        sim(1, 0)
-        sim(1, 1)
-        excess(0, 1)
-        sim(1, 2)
-        excess(0, 2)
-        sim(1, 3)
-        excess(0, 3)
-        for t in range(PACK - 1):
-            sim(2, t)
-        rectify(0, 0, BANK, slots(0, PACK), True)
-        excess(1, 0)
-        sim(2, 3)
+        sim(2, 0)
+        subtract(0, 0, held[0])
+        subtract(1, 0, held[1])
+        subtract(1, 1, held[2])
+        w_last = slots(35, 2)
+        round_w_on_gpsimd(2, w_last)
         for t in range(1, PACK):
+            excess(0, t)
+            sim(2, t)
+        sim(3, 0)
+        sim(3, 1)
+        rectify(0, 0, BANK, slots(3, PACK), True)
+        scale_bank(3, 0, held[3])
+        subtract(3, 0, held[3])
+        for t in range(2, PACK):
             excess(1, t)
-            sim(4, t - 1)
-        rectify(1, 0, BANK, slots(4, PACK), True)
+            sim(3, t)
+        rectify(1, 0, BANK, slots(11, PACK), True)
         excess(2, 0)
-        sim(4, 3)
+        sim(4, 0)
         for t in range(1, PACK):
             excess(2, t)
-        sim(5, 3)
-        excess(3, 3)
         sim(5, 0)
-        rectify(2, 0, BANK, slots(8, PACK), True)
-        sixth = keep.tile([P, BANK], F32, name="sixth", tag="sixth", align_bytes=64)
-        scale_bank(5, 3, sixth[:])
-        rectify(3, 0, BANK, slots(12, PACK), True)
-        zq, zq_s = quantize("zq01", slots(0, 2 * PACK), 2 * BANK, "w_raw1")
-        codes, scales = quantize("wq01", w_pair[:], 2 * N, "wq01")
-        for b in (0, 1):
-            wq[b] = codes[:, b * N : (b + 1) * N]
-            wq_s[b] = scales[:, b * N : (b + 1) * N]
-        aggregate(0, zq[:, :BANK], zq_s[:, :BANK], 0, BANK, True, False)
-        aggregate(1, zq[:, BANK:], zq_s[:, BANK:], 0, BANK, False, False)
-        w_last = slots(4, 2)
-        round_w_on_gpsimd(2, w_last)
-        excess(4, 0)
-        sim(5, 1)
-        excess(4, 1)
+        scale_bank(4, 0, held[4])
+        rectify(2, 0, BANK, slots(15, PACK), True)
+        sim(4, 1)
         sim(5, 2)
+        scale_bank(5, 0, held[5])
+        excess(3, 1)
+        sim(4, 2)
+        excess(3, 2)
+        sim(4, 3)
+        excess(3, 3)
+        sim(5, 1)
+        codes, scales = quantize("zq0", slots(3, 2 * PACK), 2 * BANK, "held3")
+        for b in (0, 1):
+            wq[b] = codes[:, BANK + b * N : BANK + (b + 1) * N]
+            wq_s[b] = scales[:, BANK + b * N : BANK + (b + 1) * N]
+        aggregate(0, codes[:, :BANK], scales[:, :BANK], 0, BANK, True, False)
+        wq[2], wq_s[2] = quantize("wq2", w_last, N, "w_raw2")
+        zq, zq_s = quantize("zq1", slots(11, PACK), BANK, "zq1")
+        aggregate(1, zq, zq_s, 0, BANK, False, False)
+        subtract(4, 0, held[4])
+        rectify(3, 0, 256, slots(19, PACK)[:, : 1024], True)
+        excess(4, 1)
+        sim(5, 3)
         excess(4, 2)
         excess(4, 3)
-        rectify(4, 0, BANK, slots(16, PACK), True)
-        zq, zq_s = quantize("zq23", slots(8, 2 * PACK), 2 * BANK, "w_raw2")
-        wq[2], wq_s[2] = quantize("wq2", w_last, N, "wq2")
-        aggregate(2, zq[:, :BANK], zq_s[:, :BANK], 0, BANK, False, True)
-        aggregate(3, zq[:, BANK:], zq_s[:, BANK:], 0, BANK, True, False)
-        subtract(5, 3, sixth[:])
-        for t in range(PACK - 1):
-            excess(5, t)
-        rectify(5, 0, HALF, slots(20, 2), True)
-        zq, zq_s = quantize("zq4", slots(16, PACK), BANK, "sixth")
+        zq, zq_s = quantize("zq2", slots(15, PACK), BANK, "held4")
+        aggregate(2, zq, zq_s, 0, BANK, False, True)
+        rectify(3, 256, BANK, slots(19, PACK)[:, 1024 :], False)
+        subtract(5, 0, held[5])
+        rectify(4, 0, 512, slots(23, PACK)[:, : 2048], True)
+        excess(5, 1)
+        excess(5, 2)
+        zq, zq_s = quantize("zq3", slots(19, PACK), BANK, "held5")
+        aggregate(3, zq, zq_s, 0, BANK, True, False)
+        excess(5, 3)
+        rectify(5, 0, HALF, slots(27, 2), True)
+        zq, zq_s = quantize("zq4", slots(23, PACK), BANK, "zq4")
         aggregate(4, zq, zq_s, 0, BANK, False, False)
-        rectify(5, HALF, BANK, slots(24, 2), False)
-        zq, zq_s = quantize("zq5b", slots(24, 2), HALF, "zq5b")
-        aggregate(5, zq, zq_s, HALF, BANK, False, False)
+        rectify(5, HALF, BANK, slots(29, 2), False)
+        zq, zq_s = quantize("zq5b", slots(29, 2), HALF, "zq5b")
+        aggregate(5, zq, zq_s, HALF, BANK, False, True)
         for n in range(N_TILES):
-            early = slots(8 + 2 * n, 2).bitcast(F32)
+            early = slots(15 + 2 * n, 2).bitcast(F32)
             nc.scalar.copy(early, acc[n, 0][:])
             nc.sync.dma_start(out[n * P : (n + 1) * P, 0:BANK], early)
-        zq, zq_s = quantize("zq5a", slots(20, 2), HALF, "zq5a")
+        zq, zq_s = quantize("zq5a", slots(27, 2), HALF, "zq5a")
         aggregate(5, zq, zq_s, 0, HALF, False, True)
-        first = keep.tile([P, BANK], F32, name="first")
-        nc.scalar.copy(first[:], acc[0, 1][:])
-        nc.sync.dma_start(out[0:P, BANK:S2], first[:])
-        second = keep.tile([P, BANK], F32, name="second")
-        for d0 in range(0, BANK, HALF):
-            d = slice(d0, d0 + HALF)
-            nc.vector.tensor_copy(second[:, d], acc[1, 1][:, d])
-            nc.sync.dma_start(out[P : 2 * P, BANK + d0 : BANK + d0 + HALF], second[:, d])
+        result = keep.tile([P, 2, N_TILES, HALF], F32, name="result")
+        for half, pair in ((1, (acc[0, 1], acc[1, 1])), (0, acc_first)):
+            nc.scalar.copy(result[:, half, 0, :], pair[0][:, :HALF])
+            nc.vector.tensor_copy(result[:, half, 1, :], pair[1][:, :HALF])
+            for n in range(N_TILES):
+                c0 = BANK + half * HALF
+                nc.sync.dma_start(out[n * P : (n + 1) * P, c0 : c0 + HALF], result[:, half, n, :])

@@ -64,9 +64,10 @@ def tile_list_similarity_join_aggregate_kernel(
             )
         nc.sync.dma_start(t2[0][:], tab2_words[0].rearrange("p t i -> p (t i)").bitcast(I32))
         nc.sync.dma_start(list1[:], offs)
-        for r in range(4):
-            for a in range(K_PASSES):
-                nc.sync.dma_start(s1_tab[4 * a + r : P : 32, :], tab_scales[a, r:16:4, :].bitcast(I32))
+        for q in range(QUADRANTS):
+            nc.sync.dma_start(
+                s1_tab[32 * q : 32 * q + 4 * K_PASSES, :], tab_scales[:, 4 * q : 4 * q + 4, :].bitcast(I32)
+            )
         nc.sync.dma_start(t2[1][:], tab2_words[1].rearrange("p t i -> p (t i)").bitcast(I32))
         nc.sync.dma_start(t1[1][:], tab_words[1].rearrange("p t i -> p (t i)").bitcast(I32))
         nc.sync.dma_start(t1[0][:], tab_words[0].rearrange("p t i -> p (t i)").bitcast(I32))
@@ -84,8 +85,8 @@ def tile_list_similarity_join_aggregate_kernel(
             nc.sync.dma_start(w_raw[b], w[b * PASS : (b + 1) * PASS, :].rearrange("(p t) n -> p t n", t=PACK))
 
         load_w(0)
-        load_w(1)
         nc.sync.dma_start(w4_c[:], w4_words.rearrange("b p c -> p b c").bitcast(I32))
+        load_w(1)
         for q in range(QUADRANTS):
             nc.sync.dma_start(
                 w4_s[32 * q : 32 * q + 4, :, :],
@@ -249,12 +250,15 @@ def tile_list_similarity_join_aggregate_kernel(
                 w_raw[b].rearrange("p t (c i) -> p c t i", i=8),
             )
 
-        held = {u: keep.tile([P, BANK], F32, name=f"held{u}", tag=f"held{u}", align_bytes=64)[:] for u in range(6)}
+        held = {u: keep.tile([P, BANK], F32, name=f"held{u}", tag=f"held{u}", align_bytes=64)[:] for u in range(3, 6)}
         for u in (0, 1):
             for t in range(PACK):
                 sim_pass(u, t, 1)
         gather_rows(0, 0)
         round_w(0)
+        held_first = keep.tile([P, 3, BANK], F32, name="held_first", tag="w_raw0", align_bytes=64)
+        for u in range(3):
+            held[u] = held_first[:, u, :]
         for t in range(PACK):
             sim_pass(0, t, 0)
         scale_bank(0, 0, held[0])

@@ -64,10 +64,9 @@ def tile_list_similarity_join_aggregate_kernel(
             )
         nc.sync.dma_start(t2[0][:], tab2_words[0].rearrange("p t i -> p (t i)").bitcast(I32))
         nc.sync.dma_start(list1[:], offs)
-        for q in range(QUADRANTS):
-            nc.sync.dma_start(
-                s1_tab[32 * q : 32 * q + 4 * K_PASSES, :], tab_scales[:, 4 * q : 4 * q + 4, :].bitcast(I32)
-            )
+        for r in range(4):
+            for a in range(K_PASSES):
+                nc.sync.dma_start(s1_tab[4 * a + r : P : 32, :], tab_scales[a, r:16:4, :].bitcast(I32))
         nc.sync.dma_start(t2[1][:], tab2_words[1].rearrange("p t i -> p (t i)").bitcast(I32))
         nc.sync.dma_start(t1[1][:], tab_words[1].rearrange("p t i -> p (t i)").bitcast(I32))
         nc.sync.dma_start(t1[0][:], tab_words[0].rearrange("p t i -> p (t i)").bitcast(I32))

@@ -311,14 +311,14 @@ def tile_list_similarity_join_aggregate_kernel(
         zq, zq_s = quantize("zq1", slots(11, PACK), BANK, "zq1")
         aggregate(1, zq, zq_s, 0, BANK, False, False)
         subtract(4, 0, held[4])
-        rectify(3, 0, 256, slots(19, PACK)[:, : 1024], True)
+        rectify(3, 0, 192, slots(19, PACK)[:, : 768], True)
         excess(4, 1)
         sim(5, 3)
         excess(4, 2)
         excess(4, 3)
         zq, zq_s = quantize("zq2", slots(15, PACK), BANK, "held4")
         aggregate(2, zq, zq_s, 0, BANK, False, True)
-        rectify(3, 256, BANK, slots(19, PACK)[:, 1024 :], False)
+        rectify(3, 192, BANK, slots(19, PACK)[:, 768 :], False)
         subtract(5, 0, held[5])
         rectify(4, 0, 512, slots(23, PACK)[:, : 2048], True)
         excess(5, 1)
@@ -326,16 +326,16 @@ def tile_list_similarity_join_aggregate_kernel(
         zq, zq_s = quantize("zq3", slots(19, PACK), BANK, "held5")
         aggregate(3, zq, zq_s, 0, BANK, True, False)
         excess(5, 3)
+        for n in range(N_TILES):
+            early = slots(11 + 2 * n, 2).bitcast(F32)
+            nc.scalar.copy(early, acc[n, 0][:])
+            nc.sync.dma_start(out[n * P : (n + 1) * P, 0:BANK], early)
         rectify(5, 0, HALF, slots(27, 2), True)
         zq, zq_s = quantize("zq4", slots(23, PACK), BANK, "zq4")
         aggregate(4, zq, zq_s, 0, BANK, False, False)
         rectify(5, HALF, BANK, slots(29, 2), False)
         zq, zq_s = quantize("zq5b", slots(29, 2), HALF, "zq5b")
         aggregate(5, zq, zq_s, HALF, BANK, False, True)
-        for n in range(N_TILES):
-            early = slots(15 + 2 * n, 2).bitcast(F32)
-            nc.scalar.copy(early, acc[n, 0][:])
-            nc.sync.dma_start(out[n * P : (n + 1) * P, 0:BANK], early)
         zq, zq_s = quantize("zq5a", slots(27, 2), HALF, "zq5a")
         aggregate(5, zq, zq_s, 0, HALF, False, True)
         result = keep.tile([P, 2, N_TILES, HALF], F32, name="result")

@@ -28,6 +28,7 @@ N_TILES = N // P
 QUADRANTS = 4
 LIST_ROWS = 16
 HALF = BANK // 2
+STAGE = 96
 
 
 def tile_list_similarity_join_aggregate_kernel(
@@ -45,31 +46,53 @@ def tile_list_similarity_join_aggregate_kernel(
         s2_tab = keep.tile([P, T2 // 4], I32, name="s2_tab", align_bytes=64)
         s1_tab = keep.tile([P, T // 4], I32, name="s1_tab", align_bytes=64)
         w4_s = keep.tile([P, I_PASSES, N // 4], I32, name="w4_s", align_bytes=64)
-        nc.gpsimd.memset(s2_tab[:], 0)
-        nc.vector.memset(s1_tab[:], 0)
+        planes = keep.tile([P, K_PASSES * (S2 + S) // 4], I32, name="planes", align_bytes=64)
+        nc.vector.memset(s2_tab[:STAGE, :], 0)
+        nc.vector.memset(s1_tab[:STAGE, :], 0)
+        nc.gpsimd.memset(planes[:], 0)
         nc.vector.memset(w4_s[:], 0)
         ident = keep.tile([P, P], F32, name="ident")
         make_identity(nc, ident[:])
 
         list2 = keep.tile([P, S2 // LIST_ROWS], U16, name="list2")
         list1 = keep.tile([P, S // LIST_ROWS], U16, name="list1")
-        t2 = [keep.tile([P, T2], I32, name=f"t2_{a}", tag=f"t2_{a}", align_bytes=64) for a in range(K_PASSES)]
+        t2 = keep.tile([P, K_PASSES, T2], I32, name="t2", align_bytes=64)
         t1 = [keep.tile([P, T], I32, name=f"t1_{a}", tag=f"t1_{a}", align_bytes=64) for a in range(K_PASSES)]
         nc.sync.dma_start(list2[:], offs2)
         nc.scalar.dma_start(th_sb[:], th.rearrange("(p h c) -> p h c", h=J_HALVES, c=PACK))
-        nc.sync.dma_start(g_sb[:], g.rearrange("(b p t) -> p b t", b=I_PASSES, t=PACK))
-        for q in range(QUADRANTS):
-            nc.sync.dma_start(
-                s2_tab[32 * q : 32 * q + 4 * K_PASSES, :], tab2_scales[:, 4 * q : 4 * q + 4, :].bitcast(I32)
-            )
-        nc.sync.dma_start(t2[0][:], tab2_words[0].rearrange("p t i -> p (t i)").bitcast(I32))
+        nc.sync.dma_start(s2_tab[STAGE:, :], tab2_scales.rearrange("a q t -> (a q) t").bitcast(I32))
+        nc.scalar.dma_start(g_sb[:], g.rearrange("(b p t) -> p b t", b=I_PASSES, t=PACK))
         nc.sync.dma_start(list1[:], offs)
-        for r in range(4):
-            for a in range(K_PASSES):
-                nc.sync.dma_start(s1_tab[4 * a + r : P : 32, :], tab_scales[a, r:16:4, :].bitcast(I32))
-        nc.sync.dma_start(t2[1][:], tab2_words[1].rearrange("p t i -> p (t i)").bitcast(I32))
+        nc.sync.dma_start(s1_tab[STAGE:, :], tab_scales.rearrange("a q t -> (a q) t").bitcast(I32))
+        nc.sync.dma_start(t2[:], tab2_words.rearrange("a p t i -> p a (t i)").bitcast(I32))
         nc.sync.dma_start(t1[1][:], tab_words[1].rearrange("p t i -> p (t i)").bitcast(I32))
+
+        cols = PASS // LIST_ROWS
+        s2_raw = keep.tile([P, S2], U8, name="s2_raw", align_bytes=64)
+        s1_raw = [keep.tile([P, PASS], U8, name=f"s1_raw{b}", align_bytes=64) for b in range(I_PASSES)]
+        picked = keep.tile([P, S2 + S], U8, name="picked", align_bytes=64)
+        nc.vector.tensor_copy(s2_raw[:], s2_tab[:].bitcast(U8).indirect(list2[:]))
+        for b in range(I_PASSES):
+            nc.vector.tensor_copy(s1_raw[b][:], s1_tab[:].bitcast(U8).indirect(list1[:, b * cols : (b + 1) * cols]))
+        nc.vector.tensor_copy(picked[:, :S2].bitcast(I32), s2_raw[:].bitcast(I32))
+        for b in range(I_PASSES):
+            nc.vector.tensor_copy(
+                picked[:, S2 + b * PASS : S2 + (b + 1) * PASS].rearrange("p (t m) -> p t m", t=PACK),
+                s1_raw[b][:].rearrange("p (m t) -> p t m", t=PACK),
+            )
+        words = (S2 + S) // 4
+
+        def place_scales(a):
+            for q in range(QUADRANTS):
+                row = STAGE + 16 * a + 4 * q
+                nc.sync.dma_start(
+                    planes[32 * q : 32 * q + 4, a * words : (a + 1) * words], picked[row : row + 4, :].bitcast(I32)
+                )
+
+        place_scales(1)
         nc.sync.dma_start(t1[0][:], tab_words[0].rearrange("p t i -> p (t i)").bitcast(I32))
+        place_scales(0)
+        plane = [planes[:, a * words : (a + 1) * words].bitcast(U8) for a in range(K_PASSES)]
         arena = keep.tile([P, 37 * BANK], BF16, name="arena", align_bytes=64)
 
         def slots(first, count):
@@ -108,15 +131,8 @@ def tile_list_similarity_join_aggregate_kernel(
                 for h in range(J_HALVES):
                     gth[b, t, h] = tile[:, h * BANK : (h + 1) * BANK]
 
-        cols = PASS // LIST_ROWS
         v2 = [keep.tile([P, S2], U32, name=f"v2_{a}", align_bytes=64) for a in range(K_PASSES)]
-        v2_s = keep.tile([P, S2], U8, name="v2_s", align_bytes=64)
-        nc.vector.tensor_copy(v2_s[:], s2_tab[:].bitcast(U8).indirect(list2[:]))
-        nc.vector.tensor_copy(v2[0][:], t2[0][:].bitcast(U32).indirect(list2[:]))
-
         v1 = [[keep.tile([P, PASS], U32, name=f"v1_{a}_{b}", align_bytes=64) for b in range(I_PASSES)] for a in range(K_PASSES)]
-        s1_raw = [keep.tile([P, PASS], U8, name=f"s1_raw{b}", align_bytes=64) for b in range(I_PASSES)]
-        v1_s = [keep.tile([P, PASS], U8, name=f"v1_s{b}", align_bytes=64) for b in range(I_PASSES)]
 
         def gather_rows(a, b):
             nc.vector.tensor_copy(
@@ -124,13 +140,8 @@ def tile_list_similarity_join_aggregate_kernel(
                 t1[a][:].bitcast(U32).indirect(list1[:, b * cols : (b + 1) * cols]),
             )
 
-        for b in range(I_PASSES):
-            nc.vector.tensor_copy(s1_raw[b][:], s1_tab[:].bitcast(U8).indirect(list1[:, b * cols : (b + 1) * cols]))
-        for b in range(I_PASSES):
-            nc.vector.tensor_copy(
-                v1_s[b][:].rearrange("p (t m) -> p t m", t=PACK), s1_raw[b][:].rearrange("p (m t) -> p t m", t=PACK)
-            )
-        nc.vector.tensor_copy(v2[1][:], t2[1][:].bitcast(U32).indirect(list2[:]))
+        for a in (1, 0):
+            nc.vector.tensor_copy(v2[a][:], t2[:, a, :].bitcast(U32).indirect(list2[:]))
         for b in range(I_PASSES):
             gather_rows(1, b)
 
@@ -148,9 +159,9 @@ def tile_list_similarity_join_aggregate_kernel(
             nc.tensor.matmul_mx(
                 out=sim_bank[u, t][:],
                 lhsT=v1[a][b][:, m].bitcast(FP8X4),
-                lhsT_scale=v1_s[b][4 * a : P, m],
+                lhsT_scale=plane[a][:, S2 + b * PASS + t * P : S2 + b * PASS + (t + 1) * P],
                 rhs=v2[a][:, h * BANK : (h + 1) * BANK].bitcast(FP8X4),
-                rhs_scale=v2_s[4 * a : P, h * BANK : (h + 1) * BANK],
+                rhs_scale=plane[a][:, h * BANK : (h + 1) * BANK],
                 start=(a == 1),
                 stop=(a == 0),
             )

@@ -59,7 +59,7 @@ def tile_list_similarity_join_aggregate_kernel(
         t2 = keep.tile([P, K_PASSES, T2], I32, name="t2", align_bytes=64)
         t1 = [keep.tile([P, T], I32, name=f"t1_{a}", tag=f"t1_{a}", align_bytes=64) for a in range(K_PASSES)]
         nc.sync.dma_start(list2[:], offs2)
-        nc.scalar.dma_start(th_sb[:], th.rearrange("(p h c) -> p h c", h=J_HALVES, c=PACK))
+        nc.scalar.dma_start(th_sb[:], th.rearrange("(h p c) -> p h c", h=J_HALVES, c=PACK))
         nc.sync.dma_start(s2_tab[STAGE:, :], tab2_scales.rearrange("a q t -> (a q) t").bitcast(I32))
         nc.scalar.dma_start(g_sb[:], g.rearrange("(b p t) -> p b t", b=I_PASSES, t=PACK))
         nc.sync.dma_start(list1[:], offs)
@@ -91,24 +91,25 @@ def tile_list_similarity_join_aggregate_kernel(
 
         place_scales(1)
         nc.sync.dma_start(t1[0][:], tab_words[0].rearrange("p t i -> p (t i)").bitcast(I32))
-        place_scales(0)
-        plane = [planes[:, a * words : (a + 1) * words].bitcast(U8) for a in range(K_PASSES)]
-        arena = keep.tile([P, 37 * BANK], BF16, name="arena", align_bytes=64)
-
-        def slots(first, count):
-            return arena[:, first * BANK : (first + count) * BANK]
-
         w_raw = [
             keep.tile([P, PACK, N], F32, name=f"w_raw{b}", tag=f"w_raw{b}", align_bytes=64)[:] for b in range(I_PASSES)
         ]
-        w4_c = keep.tile([P, I_PASSES, 2 * N // 4], I32, name="w4_c", align_bytes=64)
 
         def load_w(b):
             nc.sync.dma_start(w_raw[b], w[b * PASS : (b + 1) * PASS, :].rearrange("(p t) n -> p t n", t=PACK))
 
         load_w(0)
-        nc.sync.dma_start(w4_c[:], w4_words.rearrange("b p c -> p b c").bitcast(I32))
+        place_scales(0)
+        plane = [planes[:, a * words : (a + 1) * words].bitcast(U8) for a in range(K_PASSES)]
+        arena = keep.tile([P, 30 * BANK], BF16, name="arena", align_bytes=64)
+
+        def slots(first, count):
+            return arena[:, first * BANK : (first + count) * BANK]
+
+        w4_c = keep.tile([P, I_PASSES, 2 * N // 4], I32, name="w4_c", align_bytes=64)
+
         load_w(1)
+        nc.sync.dma_start(w4_c[:], w4_words.rearrange("b p c -> p b c").bitcast(I32))
         for q in range(QUADRANTS):
             nc.sync.dma_start(
                 w4_s[32 * q : 32 * q + 4, :, :],
@@ -116,20 +117,21 @@ def tile_list_similarity_join_aggregate_kernel(
             )
         load_w(2)
 
-        th_all = keep.tile([P, P, J_HALVES, PACK], F32, name="th_all")
+        gth = {}
         for h in range(J_HALVES):
             spread = banks[6 + h][:].rearrange("m (c p) -> m c p", c=PACK)
             for c in range(PACK):
                 nc.tensor.transpose(spread[:, c, :], th_sb[:, h, c : c + 1].to_broadcast([P, P]), ident[:])
-            nc.scalar.copy(th_all[:, :, h, :], spread.rearrange("m c p -> m p c"))
-        th_row = th_all[:].rearrange("m p h c -> m (p h c)")
-        gth = {}
-        for b in range(I_PASSES):
-            for t in range(PACK):
-                tile = keep.tile([P, S2], F32, name=f"gth{b}_{t}", align_bytes=64)
-                nc.scalar.activation(tile[:], th_row, ACT.Copy, scale=g_sb[:, b, t : t + 1])
-                for h in range(J_HALVES):
-                    gth[b, t, h] = tile[:, h * BANK : (h + 1) * BANK]
+            for b in range(I_PASSES):
+                for t in range(PACK):
+                    tile = keep.tile([P, BANK], F32, name=f"gth{b}_{t}_{h}", align_bytes=64)
+                    nc.scalar.activation(
+                        tile[:].rearrange("m (p c) -> m p c", c=PACK),
+                        spread.rearrange("m c p -> m p c"),
+                        ACT.Copy,
+                        scale=g_sb[:, b, t : t + 1],
+                    )
+                    gth[b, t, h] = tile[:]
 
         v2 = [keep.tile([P, S2], U32, name=f"v2_{a}", align_bytes=64) for a in range(K_PASSES)]
         v1 = [[keep.tile([P, PASS], U32, name=f"v1_{a}_{b}", align_bytes=64) for b in range(I_PASSES)] for a in range(K_PASSES)]
@@ -170,7 +172,7 @@ def tile_list_similarity_join_aggregate_kernel(
             sim_pass(u, t, 1)
             sim_pass(u, t, 0)
 
-        xs = {u: slots(first, PACK).rearrange("p (t j) -> p t j", t=PACK) for u, first in ((0, 23), (1, 15), (2, 19), (3, 31), (4, 11), (5, 15))}
+        xs = {u: slots(first, PACK).rearrange("p (t j) -> p t j", t=PACK) for u, first in ((0, 22), (1, 14), (2, 18), (3, 26), (4, 10), (5, 25))}
 
         def excess(u, t):
             b, h = units[u]
@@ -225,7 +227,7 @@ def tile_list_similarity_join_aggregate_kernel(
                 stop=closes,
             )
 
-        def aggregate(u, zq, zq_s, c0, c1, opens, closes):
+        def aggregate(u, zq, zq_s, c0, c1, opens, closes, tiles=range(N_TILES)):
             b, h = units[u]
             if h == 0:
                 for n in range(N_TILES):
@@ -233,7 +235,7 @@ def tile_list_similarity_join_aggregate_kernel(
                 return
             for d0 in reversed(range(c0, c1, HALF)):
                 d = slice(d0 - c0, d0 - c0 + HALF)
-                for n in range(N_TILES):
+                for n in tiles:
                     dst = acc[n, 1] if d0 else acc_first[n]
                     add_product(dst[:, :HALF], b, n, zq[:, d], zq_s[:, d], opens, closes)
 
@@ -256,7 +258,7 @@ def tile_list_similarity_join_aggregate_kernel(
 
         def round_w(b):
             nc.scalar.copy(
-                slots(7 + 2 * b, 2).rearrange("p (c i t) -> p c t i", i=8, t=PACK),
+                slots(4 + 2 * b, 2).rearrange("p (c i t) -> p c t i", i=8, t=PACK),
                 w_raw[b].rearrange("p t (c i) -> p c t i", i=8),
             )
 
@@ -266,7 +268,7 @@ def tile_list_similarity_join_aggregate_kernel(
                 sim_pass(u, t, 1)
         gather_rows(0, 0)
         round_w(0)
-        held_first = keep.tile([P, 3, BANK], F32, name="held_first", tag="w_raw0", align_bytes=64)
+        held_first = keep.tile([P, 3, BANK], F32, name="held_first", align_bytes=64)
         for u in range(3):
             held[u] = held_first[:, u, :]
         for t in range(PACK):
@@ -283,27 +285,27 @@ def tile_list_similarity_join_aggregate_kernel(
         subtract(0, 0, held[0])
         subtract(1, 0, held[1])
         subtract(1, 1, held[2])
-        w_last = slots(35, 2)
+        w_last = slots(8, 2)
         round_w_on_gpsimd(2, w_last)
         for t in range(1, PACK):
             excess(0, t)
             sim(2, t)
         sim(3, 0)
         sim(3, 1)
-        rectify(0, 0, BANK, slots(3, PACK), True)
+        rectify(0, 0, BANK, slots(0, PACK), True)
         scale_bank(3, 0, held[3])
         subtract(3, 0, held[3])
         for t in range(2, PACK):
             excess(1, t)
             sim(3, t)
-        rectify(1, 0, BANK, slots(11, PACK), True)
+        rectify(1, 0, BANK, slots(10, PACK), True)
         excess(2, 0)
         sim(4, 0)
         for t in range(1, PACK):
             excess(2, t)
         sim(5, 0)
         scale_bank(4, 0, held[4])
-        rectify(2, 0, BANK, slots(15, PACK), True)
+        rectify(2, 0, BANK, slots(14, PACK), True)
         sim(4, 1)
         sim(5, 2)
         scale_bank(5, 0, held[5])
@@ -313,41 +315,44 @@ def tile_list_similarity_join_aggregate_kernel(
         sim(4, 3)
         excess(3, 3)
         sim(5, 1)
-        codes, scales = quantize("zq0", slots(3, 2 * PACK), 2 * BANK, "held3")
+        codes, scales = quantize("zq0", slots(0, 2 * PACK), 2 * BANK, "held3")
         for b in (0, 1):
             wq[b] = codes[:, BANK + b * N : BANK + (b + 1) * N]
             wq_s[b] = scales[:, BANK + b * N : BANK + (b + 1) * N]
         aggregate(0, codes[:, :BANK], scales[:, :BANK], 0, BANK, True, False)
         wq[2], wq_s[2] = quantize("wq2", w_last, N, "w_raw2")
-        zq, zq_s = quantize("zq1", slots(11, PACK), BANK, "zq1")
+        zq, zq_s = quantize("zq1", slots(10, PACK), BANK, "zq1")
         aggregate(1, zq, zq_s, 0, BANK, False, False)
+        rectify(3, 256, BANK, slots(22, PACK)[:, 1024:], False)
         subtract(4, 0, held[4])
-        rectify(3, 0, 192, slots(19, PACK)[:, : 768], True)
+        rectify(3, 0, 256, slots(22, PACK)[:, :1024], True)
         excess(4, 1)
         sim(5, 3)
         excess(4, 2)
         excess(4, 3)
-        zq, zq_s = quantize("zq2", slots(15, PACK), BANK, "held4")
+        zq, zq_s = quantize("zq2", slots(14, PACK), BANK, "held4")
         aggregate(2, zq, zq_s, 0, BANK, False, True)
-        rectify(3, 192, BANK, slots(19, PACK)[:, 768 :], False)
+        zq, zq_s = quantize("zq3", slots(22, PACK), BANK, "zq3")
+        aggregate(3, zq[:, HALF:], zq_s[:, HALF:], HALF, BANK, True, False)
+        aggregate(3, zq[:, :HALF], zq_s[:, :HALF], 0, HALF, True, False, tiles=(0,))
         subtract(5, 0, held[5])
-        rectify(4, 0, 512, slots(23, PACK)[:, : 2048], True)
+        rectify(4, 0, BANK, slots(18, PACK), True)
         excess(5, 1)
+        aggregate(3, zq[:, :HALF], zq_s[:, :HALF], 0, HALF, True, False, tiles=(1,))
         excess(5, 2)
-        zq, zq_s = quantize("zq3", slots(19, PACK), BANK, "held5")
-        aggregate(3, zq, zq_s, 0, BANK, True, False)
         excess(5, 3)
         for n in range(N_TILES):
-            early = slots(11 + 2 * n, 2).bitcast(F32)
+            early = slots(10 + 2 * n, 2).bitcast(F32)
             nc.scalar.copy(early, acc[n, 0][:])
             nc.sync.dma_start(out[n * P : (n + 1) * P, 0:BANK], early)
-        rectify(5, 0, HALF, slots(27, 2), True)
-        zq, zq_s = quantize("zq4", slots(23, PACK), BANK, "zq4")
+        rectify(5, 0, 160, slots(0, 2)[:, :640], True)
+        zq, zq_s = quantize("zq4", slots(18, PACK), BANK, "held5")
         aggregate(4, zq, zq_s, 0, BANK, False, False)
-        rectify(5, HALF, BANK, slots(29, 2), False)
-        zq, zq_s = quantize("zq5b", slots(29, 2), HALF, "zq5b")
+        rectify(5, HALF, BANK, slots(2, 2), False)
+        rectify(5, 160, HALF, slots(0, 2)[:, 640:], False)
+        zq, zq_s = quantize("zq5b", slots(2, 2), HALF, "zq5b")
         aggregate(5, zq, zq_s, HALF, BANK, False, True)
-        zq, zq_s = quantize("zq5a", slots(27, 2), HALF, "zq5a")
+        zq, zq_s = quantize("zq5a", slots(0, 2), HALF, "zq5a")
         aggregate(5, zq, zq_s, 0, HALF, False, True)
         result = keep.tile([P, 2, N_TILES, HALF], F32, name="result")
         for half, pair in ((1, (acc[0, 1], acc[1, 1])), (0, acc_first)):

@@ -69,24 +69,26 @@ def tile_list_similarity_join_aggregate_kernel(
 
         cols = PASS // LIST_ROWS
         s2_raw = keep.tile([P, S2], U8, name="s2_raw", align_bytes=64)
-        s1_raw = [keep.tile([P, PASS], U8, name=f"s1_raw{b}", align_bytes=64) for b in range(I_PASSES)]
+        pieces = ((0, 2), (2, 3))
+        s1_raw = [keep.tile([P, (b1 - b0) * PASS], U8, name=f"s1_raw{b0}", align_bytes=64) for b0, b1 in pieces]
         picked = keep.tile([P, S2 + S], U8, name="picked", align_bytes=64)
         nc.vector.tensor_copy(s2_raw[:], s2_tab[:].bitcast(U8).indirect(list2[:]))
-        for b in range(I_PASSES):
-            nc.vector.tensor_copy(s1_raw[b][:], s1_tab[:].bitcast(U8).indirect(list1[:, b * cols : (b + 1) * cols]))
+        for raw, (b0, b1) in zip(s1_raw, pieces):
+            nc.vector.tensor_copy(raw[:], s1_tab[:].bitcast(U8).indirect(list1[:, b0 * cols : b1 * cols]))
         nc.vector.tensor_copy(picked[:, :S2].bitcast(I32), s2_raw[:].bitcast(I32))
-        for b in range(I_PASSES):
+        for raw, (b0, b1) in zip(s1_raw, pieces):
             nc.vector.tensor_copy(
-                picked[:, S2 + b * PASS : S2 + (b + 1) * PASS].rearrange("p (t m) -> p t m", t=PACK),
-                s1_raw[b][:].rearrange("p (m t) -> p t m", t=PACK),
+                picked[:, S2 + b0 * PASS : S2 + b1 * PASS].rearrange("p (b t m) -> p t b m", t=PACK, m=P),
+                raw[:].rearrange("p (b m t) -> p t b m", t=PACK, m=P),
             )
         words = (S2 + S) // 4
 
         def place_scales(a):
-            for q in range(QUADRANTS):
-                row = STAGE + 16 * a + 4 * q
+            for r in range(4):
+                row = STAGE + 16 * a + r
                 nc.sync.dma_start(
-                    planes[32 * q : 32 * q + 4, a * words : (a + 1) * words], picked[row : row + 4, :].bitcast(I32)
+                    planes[4 * a + r : P : 32, a * words : (a + 1) * words],
+                    picked[row : STAGE + 16 * (a + 1) : 4, :].bitcast(I32),
                 )
 
         place_scales(1)
@@ -100,7 +102,7 @@ def tile_list_similarity_join_aggregate_kernel(
 
         load_w(0)
         place_scales(0)
-        plane = [planes[:, a * words : (a + 1) * words].bitcast(U8) for a in range(K_PASSES)]
+        plane = [planes[:, a * words : (a + 1) * words].bitcast(U8)[4 * a : P, :] for a in range(K_PASSES)]
         arena = keep.tile([P, 30 * BANK], BF16, name="arena", align_bytes=64)
 
         def slots(first, count):
@@ -134,18 +136,21 @@ def tile_list_similarity_join_aggregate_kernel(
                     gth[b, t, h] = tile[:]
 
         v2 = [keep.tile([P, S2], U32, name=f"v2_{a}", align_bytes=64) for a in range(K_PASSES)]
-        v1 = [[keep.tile([P, PASS], U32, name=f"v1_{a}_{b}", align_bytes=64) for b in range(I_PASSES)] for a in range(K_PASSES)]
+        v1 = {}
 
-        def gather_rows(a, b):
+        def gather_rows(a, b0, count=1):
+            tile = keep.tile([P, count * PASS], U32, name=f"v1_{a}_{b0}", align_bytes=64)
             nc.vector.tensor_copy(
-                v1[a][b][:].rearrange("p (t m) -> p m t", t=PACK),
-                t1[a][:].bitcast(U32).indirect(list1[:, b * cols : (b + 1) * cols]),
+                tile[:].rearrange("p (b t m) -> p b m t", t=PACK, m=P),
+                t1[a][:].bitcast(U32).indirect(list1[:, b0 * cols : (b0 + count) * cols]),
             )
+            for b in range(count):
+                v1[a, b0 + b] = tile[:, b * PASS : (b + 1) * PASS]
 
         for a in (1, 0):
             nc.vector.tensor_copy(v2[a][:], t2[:, a, :].bitcast(U32).indirect(list2[:]))
-        for b in range(I_PASSES):
-            gather_rows(1, b)
+        gather_rows(1, 0)
+        gather_rows(1, 1, 2)
 
         units = [(b, h) for h in range(J_HALVES) for b in range(I_PASSES)]
         sim_bank = {}
@@ -160,7 +165,7 @@ def tile_list_similarity_join_aggregate_kernel(
             m = slice(t * P, (t + 1) * P)
             nc.tensor.matmul_mx(
                 out=sim_bank[u, t][:],
-                lhsT=v1[a][b][:, m].bitcast(FP8X4),
+                lhsT=v1[a, b][:, m].bitcast(FP8X4),
                 lhsT_scale=plane[a][:, S2 + b * PASS + t * P : S2 + b * PASS + (t + 1) * P],
                 rhs=v2[a][:, h * BANK : (h + 1) * BANK].bitcast(FP8X4),
                 rhs_scale=plane[a][:, h * BANK : (h + 1) * BANK],
@@ -172,7 +177,7 @@ def tile_list_similarity_join_aggregate_kernel(
             sim_pass(u, t, 1)
             sim_pass(u, t, 0)
 
-        xs = {u: slots(first, PACK).rearrange("p (t j) -> p t j", t=PACK) for u, first in ((0, 22), (1, 14), (2, 18), (3, 26), (4, 10), (5, 25))}
+        xs = {u: slots(first, PACK).rearrange("p (t j) -> p t j", t=PACK) for u, first in ((0, 22), (1, 18), (2, 14), (3, 26), (4, 10), (5, 25))}
 
         def excess(u, t):
             b, h = units[u]
@@ -305,10 +310,9 @@ def tile_list_similarity_join_aggregate_kernel(
             excess(2, t)
         sim(5, 0)
         scale_bank(4, 0, held[4])
-        rectify(2, 0, BANK, slots(14, PACK), True)
+        rectify(2, 0, BANK, slots(18, PACK), True)
         sim(4, 1)
         sim(5, 2)
-        scale_bank(5, 0, held[5])
         excess(3, 1)
         sim(4, 2)
         excess(3, 2)
@@ -326,33 +330,34 @@ def tile_list_similarity_join_aggregate_kernel(
         rectify(3, 256, BANK, slots(22, PACK)[:, 1024:], False)
         subtract(4, 0, held[4])
         rectify(3, 0, 256, slots(22, PACK)[:, :1024], True)
+        scale_bank(5, 0, held[5])
         excess(4, 1)
         sim(5, 3)
         excess(4, 2)
         excess(4, 3)
-        zq, zq_s = quantize("zq2", slots(14, PACK), BANK, "held4")
+        zq, zq_s = quantize("zq2", slots(18, PACK), BANK, "held4")
         aggregate(2, zq, zq_s, 0, BANK, False, True)
         zq, zq_s = quantize("zq3", slots(22, PACK), BANK, "zq3")
         aggregate(3, zq[:, HALF:], zq_s[:, HALF:], HALF, BANK, True, False)
         aggregate(3, zq[:, :HALF], zq_s[:, :HALF], 0, HALF, True, False, tiles=(0,))
         subtract(5, 0, held[5])
-        rectify(4, 0, BANK, slots(18, PACK), True)
+        rectify(4, 0, BANK, slots(14, PACK), True)
         excess(5, 1)
         aggregate(3, zq[:, :HALF], zq_s[:, :HALF], 0, HALF, True, False, tiles=(1,))
         excess(5, 2)
         excess(5, 3)
         for n in range(N_TILES):
-            early = slots(10 + 2 * n, 2).bitcast(F32)
+            early = slots(2 * n, 2).bitcast(F32)
             nc.scalar.copy(early, acc[n, 0][:])
             nc.sync.dma_start(out[n * P : (n + 1) * P, 0:BANK], early)
-        rectify(5, 0, 160, slots(0, 2)[:, :640], True)
-        zq, zq_s = quantize("zq4", slots(18, PACK), BANK, "held5")
+        rectify(5, 0, 192, slots(10, 2)[:, :768], True)
+        zq, zq_s = quantize("zq4", slots(14, PACK), BANK, "held5")
         aggregate(4, zq, zq_s, 0, BANK, False, False)
-        rectify(5, HALF, BANK, slots(2, 2), False)
-        rectify(5, 160, HALF, slots(0, 2)[:, 640:], False)
-        zq, zq_s = quantize("zq5b", slots(2, 2), HALF, "zq5b")
+        rectify(5, HALF, BANK, slots(12, 2), False)
+        rectify(5, 192, HALF, slots(10, 2)[:, 768:], False)
+        zq, zq_s = quantize("zq5b", slots(12, 2), HALF, "zq5b")
         aggregate(5, zq, zq_s, HALF, BANK, False, True)
-        zq, zq_s = quantize("zq5a", slots(0, 2), HALF, "zq5a")
+        zq, zq_s = quantize("zq5a", slots(10, 2), HALF, "zq5a")
         aggregate(5, zq, zq_s, 0, HALF, False, True)
         result = keep.tile([P, 2, N_TILES, HALF], F32, name="result")
         for half, pair in ((1, (acc[0, 1], acc[1, 1])), (0, acc_first)):

@@ -46,10 +46,11 @@ def tile_list_similarity_join_aggregate_kernel(
         s2_tab = keep.tile([P, T2 // 4], I32, name="s2_tab", align_bytes=64)
         s1_tab = keep.tile([P, T // 4], I32, name="s1_tab", align_bytes=64)
         w4_s = keep.tile([P, I_PASSES, N // 4], I32, name="w4_s", align_bytes=64)
-        planes = keep.tile([P, K_PASSES * (S2 + S) // 4], I32, name="planes", align_bytes=64)
+        planes = [keep.tile([P, (S2 + S) // 4], I32, name=f"plane{a}", align_bytes=64) for a in range(K_PASSES)]
         nc.vector.memset(s2_tab[:STAGE, :], 0)
         nc.vector.memset(s1_tab[:STAGE, :], 0)
-        nc.gpsimd.memset(planes[:], 0)
+        for a in range(K_PASSES):
+            nc.gpsimd.memset(planes[a][:], 0)
         nc.vector.memset(w4_s[:], 0)
         ident = keep.tile([P, P], F32, name="ident")
         make_identity(nc, ident[:])
@@ -66,6 +67,8 @@ def tile_list_similarity_join_aggregate_kernel(
         nc.sync.dma_start(s1_tab[STAGE:, :], tab_scales.rearrange("a q t -> (a q) t").bitcast(I32))
         nc.sync.dma_start(t2[:], tab2_words.rearrange("a p t i -> p a (t i)").bitcast(I32))
         nc.sync.dma_start(t1[1][:], tab_words[1].rearrange("p t i -> p (t i)").bitcast(I32))
+        last_words = tab_words[0].rearrange("p t i -> p (t i)").bitcast(I32)
+        nc.sync.dma_start(t1[0][:, :1024], last_words[:, :1024])
 
         cols = PASS // LIST_ROWS
         s2_raw = keep.tile([P, S2], U8, name="s2_raw", align_bytes=64)
@@ -81,18 +84,17 @@ def tile_list_similarity_join_aggregate_kernel(
                 picked[:, S2 + b0 * PASS : S2 + b1 * PASS].rearrange("p (b t m) -> p t b m", t=PACK, m=P),
                 raw[:].rearrange("p (b m t) -> p t b m", t=PACK, m=P),
             )
-        words = (S2 + S) // 4
 
         def place_scales(a):
             for r in range(4):
                 row = STAGE + 16 * a + r
                 nc.sync.dma_start(
-                    planes[4 * a + r : P : 32, a * words : (a + 1) * words],
+                    planes[a][4 * a + r : P : 32, :],
                     picked[row : STAGE + 16 * (a + 1) : 4, :].bitcast(I32),
                 )
 
         place_scales(1)
-        nc.sync.dma_start(t1[0][:], tab_words[0].rearrange("p t i -> p (t i)").bitcast(I32))
+        nc.sync.dma_start(t1[0][:, 1024:], last_words[:, 1024:])
         w_raw = [
             keep.tile([P, PACK, N], F32, name=f"w_raw{b}", tag=f"w_raw{b}", align_bytes=64)[:] for b in range(I_PASSES)
         ]
@@ -102,7 +104,7 @@ def tile_list_similarity_join_aggregate_kernel(
 
         load_w(0)
         place_scales(0)
-        plane = [planes[:, a * words : (a + 1) * words].bitcast(U8)[4 * a : P, :] for a in range(K_PASSES)]
+        plane = [planes[a][:].bitcast(U8)[4 * a : P, :] for a in range(K_PASSES)]
         arena = keep.tile([P, 30 * BANK], BF16, name="arena", align_bytes=64)
 
         def slots(first, count):

@@ -21,14 +21,33 @@ P = 128
 PACK = 4
 PASS = P * PACK
 BANK = 512
+HALF = BANK // 2
 K_PASSES = K // PASS
 I_PASSES = S // PASS
 J_HALVES = S2 // BANK
 N_TILES = N // P
 QUADRANTS = 4
+ROWS = 4
+BLOCKS = QUADRANTS * ROWS
 LIST_ROWS = 16
-HALF = BANK // 2
-STAGE = 96
+STAGE = P - K_PASSES * BLOCKS
+RESERVE = T // 4
+RUN = 8
+UNIT3_ON_SCALAR = 288
+UNIT5_ON_SCALAR = 192
+
+UNITS = [(b, h) for h in range(J_HALVES) for b in range(I_PASSES)]
+SIM_BANKS = ((0, 1, 2, 3), (4, 5, 6, 7), (0, 1, 2, 3), (4, 5, 6, 7), (0, 4, 5, 6), (3, 7, 0, 4))
+FIRST_HALF_BANKS = (1, 2)
+LOW_QUARTER_BANKS = (3, 7)
+HIGH_QUARTER_BANKS = (5, 6)
+THRESHOLD_BANKS = (6, 7)
+
+SLOTS = 30
+EXCESS_SLOT = (22, 18, 14, 26, 10, 25)
+RECTIFIED_SLOT = (0, 10, 18, 22, 14, 10)
+ROUNDED_W_SLOT = (4, 6, 8)
+EARLY_RESULT_SLOT = (0, 2)
 
 
 def tile_list_similarity_join_aggregate_kernel(
@@ -43,58 +62,51 @@ def tile_list_similarity_join_aggregate_kernel(
         th_sb = keep.tile([P, J_HALVES, PACK], F32, name="th_sb")
         g_sb = keep.tile([P, I_PASSES, PACK], F32, name="g_sb")
 
-        s2_tab = keep.tile([P, T2 // 4], I32, name="s2_tab", align_bytes=64)
-        s1_tab = keep.tile([P, T // 4], I32, name="s1_tab", align_bytes=64)
+        probe_scales = keep.tile([P, T2 // 4], I32, name="probe_scales", align_bytes=64)
+        row_scales = keep.tile([P, T // 4], I32, name="row_scales", tag="row_scales", align_bytes=64)
         w4_s = keep.tile([P, I_PASSES, N // 4], I32, name="w4_s", align_bytes=64)
         planes = [keep.tile([P, (S2 + S) // 4], I32, name=f"plane{a}", align_bytes=64) for a in range(K_PASSES)]
-        nc.vector.memset(s2_tab[:STAGE, :], 0)
-        nc.vector.memset(s1_tab[:STAGE, :], 0)
-        for a in range(K_PASSES):
-            nc.gpsimd.memset(planes[a][:], 0)
-        nc.vector.memset(w4_s[:], 0)
+        nc.vector.memset(probe_scales[:STAGE, :], 0)
+        nc.vector.memset(row_scales[:STAGE, :], 0)
         ident = keep.tile([P, P], F32, name="ident")
         make_identity(nc, ident[:])
 
-        list2 = keep.tile([P, S2 // LIST_ROWS], U16, name="list2")
-        list1 = keep.tile([P, S // LIST_ROWS], U16, name="list1")
-        t2 = keep.tile([P, K_PASSES, T2], I32, name="t2", align_bytes=64)
-        t1 = [keep.tile([P, T], I32, name=f"t1_{a}", tag=f"t1_{a}", align_bytes=64) for a in range(K_PASSES)]
-        nc.sync.dma_start(list2[:], offs2)
+        probe_list = keep.tile([P, S2 // LIST_ROWS], U16, name="probe_list")
+        row_list = keep.tile([P, S // LIST_ROWS], U16, name="row_list")
+        probe_table = keep.tile([P, K_PASSES, T2], I32, name="probe_table", align_bytes=64)
+        row_table = [keep.tile([P, T], I32, name=f"row_table{a}", align_bytes=64) for a in range(K_PASSES)]
+        nc.sync.dma_start(probe_list[:], offs2)
         nc.scalar.dma_start(th_sb[:], th.rearrange("(h p c) -> p h c", h=J_HALVES, c=PACK))
-        nc.sync.dma_start(s2_tab[STAGE:, :], tab2_scales.rearrange("a q t -> (a q) t").bitcast(I32))
+        nc.sync.dma_start(probe_scales[STAGE:, :], tab2_scales.rearrange("a q t -> (a q) t").bitcast(I32))
         nc.scalar.dma_start(g_sb[:], g.rearrange("(b p t) -> p b t", b=I_PASSES, t=PACK))
-        nc.sync.dma_start(list1[:], offs)
-        nc.sync.dma_start(s1_tab[STAGE:, :], tab_scales.rearrange("a q t -> (a q) t").bitcast(I32))
-        nc.sync.dma_start(t2[:], tab2_words.rearrange("a p t i -> p a (t i)").bitcast(I32))
-        nc.sync.dma_start(t1[1][:], tab_words[1].rearrange("p t i -> p (t i)").bitcast(I32))
+        nc.sync.dma_start(row_list[:], offs)
+        nc.sync.dma_start(row_scales[STAGE:, :], tab_scales.rearrange("a q t -> (a q) t").bitcast(I32))
+        nc.sync.dma_start(probe_table[:], tab2_words.rearrange("a p t i -> p a (t i)").bitcast(I32))
+        nc.sync.dma_start(row_table[1][:], tab_words[1].rearrange("p t i -> p (t i)").bitcast(I32))
         last_words = tab_words[0].rearrange("p t i -> p (t i)").bitcast(I32)
-        nc.sync.dma_start(t1[0][:, :1024], last_words[:, :1024])
+        nc.sync.dma_start(row_table[0][:, :RESERVE], last_words[:, :RESERVE])
 
-        cols = PASS // LIST_ROWS
-        s2_raw = keep.tile([P, S2], U8, name="s2_raw", align_bytes=64)
-        pieces = ((0, 2), (2, 3))
-        s1_raw = [keep.tile([P, (b1 - b0) * PASS], U8, name=f"s1_raw{b0}", align_bytes=64) for b0, b1 in pieces]
-        picked = keep.tile([P, S2 + S], U8, name="picked", align_bytes=64)
-        nc.vector.tensor_copy(s2_raw[:], s2_tab[:].bitcast(U8).indirect(list2[:]))
-        for raw, (b0, b1) in zip(s1_raw, pieces):
-            nc.vector.tensor_copy(raw[:], s1_tab[:].bitcast(U8).indirect(list1[:, b0 * cols : b1 * cols]))
-        nc.vector.tensor_copy(picked[:, :S2].bitcast(I32), s2_raw[:].bitcast(I32))
-        for raw, (b0, b1) in zip(s1_raw, pieces):
-            nc.vector.tensor_copy(
-                picked[:, S2 + b0 * PASS : S2 + b1 * PASS].rearrange("p (b t m) -> p t b m", t=PACK, m=P),
-                raw[:].rearrange("p (b m t) -> p t b m", t=PACK, m=P),
-            )
+        probe_bytes = keep.tile([P, S2], U8, name="probe_bytes", align_bytes=64)
+        row_bytes = keep.tile([P, S], U8, name="row_bytes", align_bytes=64)
+        nc.vector.tensor_copy(probe_bytes[:], probe_scales[:].bitcast(U8).indirect(probe_list[:]))
+        nc.vector.tensor_copy(row_bytes[:], row_scales[:].bitcast(U8).indirect(row_list[:]))
+        joined = keep.tile([P, S2 + S], U8, name="joined", tag="row_scales", align_bytes=64)
+        nc.vector.tensor_copy(joined[:, :S2].bitcast(I32), probe_bytes[:].bitcast(I32))
+        nc.vector.tensor_copy(
+            joined[:, S2:].rearrange("p (b t m) -> p t b m", t=PACK, m=P),
+            row_bytes[:].rearrange("p (b m t) -> p t b m", t=PACK, m=P),
+        )
 
-        def place_scales(a):
-            for r in range(4):
-                row = STAGE + 16 * a + r
+        def carry_scales(a):
+            for r in range(ROWS):
+                first = STAGE + BLOCKS * a + r
                 nc.sync.dma_start(
-                    planes[a][4 * a + r : P : 32, :],
-                    picked[row : STAGE + 16 * (a + 1) : 4, :].bitcast(I32),
+                    planes[a][ROWS * a + r : P : 32, :],
+                    joined[first : STAGE + BLOCKS * (a + 1) : ROWS, :].bitcast(I32),
                 )
 
-        place_scales(1)
-        nc.sync.dma_start(t1[0][:, 1024:], last_words[:, 1024:])
+        carry_scales(1)
+        nc.sync.dma_start(row_table[0][:, RESERVE:], last_words[:, RESERVE:])
         w_raw = [
             keep.tile([P, PACK, N], F32, name=f"w_raw{b}", tag=f"w_raw{b}", align_bytes=64)[:] for b in range(I_PASSES)
         ]
@@ -103,27 +115,26 @@ def tile_list_similarity_join_aggregate_kernel(
             nc.sync.dma_start(w_raw[b], w[b * PASS : (b + 1) * PASS, :].rearrange("(p t) n -> p t n", t=PACK))
 
         load_w(0)
-        place_scales(0)
-        plane = [planes[a][:].bitcast(U8)[4 * a : P, :] for a in range(K_PASSES)]
-        arena = keep.tile([P, 30 * BANK], BF16, name="arena", align_bytes=64)
+        carry_scales(0)
+        plane = [planes[a][:].bitcast(U8)[ROWS * a : P, :] for a in range(K_PASSES)]
+        work = keep.tile([P, SLOTS * BANK], BF16, name="work", align_bytes=64)
 
         def slots(first, count):
-            return arena[:, first * BANK : (first + count) * BANK]
+            return work[:, first * BANK : (first + count) * BANK]
 
         w4_c = keep.tile([P, I_PASSES, 2 * N // 4], I32, name="w4_c", align_bytes=64)
-
         load_w(1)
         nc.sync.dma_start(w4_c[:], w4_words.rearrange("b p c -> p b c").bitcast(I32))
         for q in range(QUADRANTS):
             nc.sync.dma_start(
-                w4_s[32 * q : 32 * q + 4, :, :],
-                w4_scales[:, 4 * q : 4 * q + 4, :].rearrange("b r n -> r b n").bitcast(I32),
+                w4_s[32 * q : 32 * q + ROWS, :, :],
+                w4_scales[:, ROWS * q : ROWS * (q + 1), :].rearrange("b r n -> r b n").bitcast(I32),
             )
         load_w(2)
 
         gth = {}
         for h in range(J_HALVES):
-            spread = banks[6 + h][:].rearrange("m (c p) -> m c p", c=PACK)
+            spread = banks[THRESHOLD_BANKS[h]][:].rearrange("m (c p) -> m c p", c=PACK)
             for c in range(PACK):
                 nc.tensor.transpose(spread[:, c, :], th_sb[:, h, c : c + 1].to_broadcast([P, P]), ident[:])
             for b in range(I_PASSES):
@@ -137,39 +148,31 @@ def tile_list_similarity_join_aggregate_kernel(
                     )
                     gth[b, t, h] = tile[:]
 
-        v2 = [keep.tile([P, S2], U32, name=f"v2_{a}", align_bytes=64) for a in range(K_PASSES)]
-        v1 = {}
+        probes = [keep.tile([P, S2], U32, name=f"probes{a}", align_bytes=64) for a in range(K_PASSES)]
+        rows = {}
+        list_cols = PASS // LIST_ROWS
 
-        def gather_rows(a, b0, count=1):
-            tile = keep.tile([P, count * PASS], U32, name=f"v1_{a}_{b0}", align_bytes=64)
+        def gather_rows(a, first, count=1):
+            tile = keep.tile([P, count * PASS], U32, name=f"rows{a}_{first}", align_bytes=64)
             nc.vector.tensor_copy(
                 tile[:].rearrange("p (b t m) -> p b m t", t=PACK, m=P),
-                t1[a][:].bitcast(U32).indirect(list1[:, b0 * cols : (b0 + count) * cols]),
+                row_table[a][:].bitcast(U32).indirect(row_list[:, first * list_cols : (first + count) * list_cols]),
             )
             for b in range(count):
-                v1[a, b0 + b] = tile[:, b * PASS : (b + 1) * PASS]
+                rows[a, first + b] = tile[:, b * PASS : (b + 1) * PASS]
 
         for a in (1, 0):
-            nc.vector.tensor_copy(v2[a][:], t2[:, a, :].bitcast(U32).indirect(list2[:]))
+            nc.vector.tensor_copy(probes[a][:], probe_table[:, a, :].bitcast(U32).indirect(probe_list[:]))
         gather_rows(1, 0)
-        gather_rows(1, 1, 2)
-
-        units = [(b, h) for h in range(J_HALVES) for b in range(I_PASSES)]
-        sim_bank = {}
-        for u, row in enumerate(((0, 1, 2, 3), (4, 5, 6, 7), (0, 1, 2, 3), (4, 5, 6, 7), (0, 4, 5, 6), (3, 7, 0, 4))):
-            for t in range(PACK):
-                sim_bank[u, t] = banks[row[t]]
-        acc = {(0, 0): banks[1], (1, 0): banks[2], (0, 1): banks[5], (1, 1): banks[6]}
-        acc_first = (banks[3], banks[7])
+        gather_rows(1, 1, I_PASSES - 1)
 
         def sim_pass(u, t, a):
-            b, h = units[u]
-            m = slice(t * P, (t + 1) * P)
+            b, h = UNITS[u]
             nc.tensor.matmul_mx(
-                out=sim_bank[u, t][:],
-                lhsT=v1[a, b][:, m].bitcast(FP8X4),
+                out=banks[SIM_BANKS[u][t]][:],
+                lhsT=rows[a, b][:, t * P : (t + 1) * P].bitcast(FP8X4),
                 lhsT_scale=plane[a][:, S2 + b * PASS + t * P : S2 + b * PASS + (t + 1) * P],
-                rhs=v2[a][:, h * BANK : (h + 1) * BANK].bitcast(FP8X4),
+                rhs=probes[a][:, h * BANK : (h + 1) * BANK].bitcast(FP8X4),
                 rhs_scale=plane[a][:, h * BANK : (h + 1) * BANK],
                 start=(a == 1),
                 stop=(a == 0),
@@ -179,35 +182,44 @@ def tile_list_similarity_join_aggregate_kernel(
             sim_pass(u, t, 1)
             sim_pass(u, t, 0)
 
-        xs = {u: slots(first, PACK).rearrange("p (t j) -> p t j", t=PACK) for u, first in ((0, 22), (1, 18), (2, 14), (3, 26), (4, 10), (5, 25))}
+        excess = [slots(first, PACK).rearrange("p (t j) -> p t j", t=PACK) for first in EXCESS_SLOT]
+        rectified = [slots(first, PACK) for first in RECTIFIED_SLOT]
 
-        def excess(u, t):
-            b, h = units[u]
+        def read_bank(u, t):
+            b, h = UNITS[u]
             nc.vector.scalar_tensor_tensor(
-                out=xs[u][:, t, :],
-                in0=sim_bank[u, t][:],
+                out=excess[u][:, t, :],
+                in0=banks[SIM_BANKS[u][t]][:],
                 scalar=g_sb[:, b, t : t + 1],
                 in1=gth[b, t, h],
                 op0=ALU.mult,
                 op1=ALU.subtract,
             )
 
-        def rectify(u, c0, c1, z, on_scalar):
-            dst = z.rearrange("p (c i t) -> p c t i", i=8, t=PACK)
-            src = xs[u][:, :, c0:c1].rearrange("p t (c i) -> p c t i", i=8)
+        def scale_bank(u, t, scaled):
+            nc.scalar.activation(scaled, banks[SIM_BANKS[u][t]][:], ACT.Copy, scale=g_sb[:, UNITS[u][0], t : t + 1])
+
+        def subtract(u, t, scaled):
+            b, h = UNITS[u]
+            nc.gpsimd.tensor_tensor(excess[u][:, t, :], scaled, gth[b, t, h], ALU.subtract)
+
+        def rectify(u, c0, c1, on_scalar):
+            dst = rectified[u][:, PACK * c0 : PACK * c1].rearrange("p (c i t) -> p c t i", i=RUN, t=PACK)
+            src = excess[u][:, :, c0:c1].rearrange("p t (c i) -> p c t i", i=RUN)
             if on_scalar:
                 nc.scalar.activation(dst, src, ACT.Relu)
             else:
                 nc.vector.tensor_scalar(out=dst, in0=src, scalar1=0.0, scalar2=None, op0=ALU.max)
 
-        wq = {}
-        wq_s = {}
-
-        def quantize(name, src, width, tag):
+        def quantize(name, src, tag):
+            width = src.shape[1] // PACK
             codes = keep.tile([P, width], U32, name=name, tag=tag, align_bytes=64)
             scales = keep.tile([P, width], U8, name=name + "_s", align_bytes=64)
             nc.vector.quantize_mx(out=codes[:].bitcast(FP8X4), scales=scales[:], in_=src)
             return codes[:], scales[:]
+
+        wq = {}
+        wq_s = {}
 
         def add_product(dst, b, n, zq, zq_s, opens, closes):
             width = zq.shape[1]
@@ -234,28 +246,20 @@ def tile_list_similarity_join_aggregate_kernel(
                 stop=closes,
             )
 
-        def aggregate(u, zq, zq_s, c0, c1, opens, closes, tiles=range(N_TILES)):
-            b, h = units[u]
-            if h == 0:
-                for n in range(N_TILES):
-                    add_product(acc[n, 0][:], b, n, zq, zq_s, opens, closes)
-                return
-            for d0 in reversed(range(c0, c1, HALF)):
-                d = slice(d0 - c0, d0 - c0 + HALF)
-                for n in tiles:
-                    dst = acc[n, 1] if d0 else acc_first[n]
-                    add_product(dst[:, :HALF], b, n, zq[:, d], zq_s[:, d], opens, closes)
+        def aggregate(u, sums, zq, zq_s, tiles=range(N_TILES)):
+            b = UNITS[u][0]
+            for n in tiles:
+                add_product(banks[sums[n]][:, : zq.shape[1]], b, n, zq, zq_s, b == 0, b == I_PASSES - 1)
 
-        def scale_bank(u, t, scaled):
-            nc.scalar.activation(scaled, sim_bank[u, t][:], ACT.Copy, scale=g_sb[:, units[u][0], t : t + 1])
+        def round_w_on_scalar(b):
+            nc.scalar.copy(
+                slots(ROUNDED_W_SLOT[b], 2).rearrange("p (c i t) -> p c t i", i=RUN, t=PACK),
+                w_raw[b].rearrange("p t (c i) -> p c t i", i=RUN),
+            )
 
-        def subtract(u, t, scaled):
-            b, h = units[u]
-            nc.gpsimd.tensor_tensor(xs[u][:, t, :], scaled, gth[b, t, h], ALU.subtract)
-
-        def round_w_on_gpsimd(b, dst):
+        def round_w_on_gpsimd(b):
             nc.gpsimd.tensor_scalar(
-                out=dst.rearrange("p (n t) -> p n t", t=PACK),
+                out=slots(ROUNDED_W_SLOT[b], 2).rearrange("p (n t) -> p n t", t=PACK),
                 in0=w_raw[b].rearrange("p t n -> p n t"),
                 scalar1=1.0,
                 scalar2=0.0,
@@ -263,108 +267,101 @@ def tile_list_similarity_join_aggregate_kernel(
                 op1=ALU.add,
             )
 
-        def round_w(b):
-            nc.scalar.copy(
-                slots(4 + 2 * b, 2).rearrange("p (c i t) -> p c t i", i=8, t=PACK),
-                w_raw[b].rearrange("p t (c i) -> p c t i", i=8),
-            )
-
-        held = {u: keep.tile([P, BANK], F32, name=f"held{u}", tag=f"held{u}", align_bytes=64)[:] for u in range(3, 6)}
+        held = {u: keep.tile([P, BANK], F32, name=f"held{u}", tag=f"held{u}", align_bytes=64)[:] for u in (3, 4, 5)}
         for u in (0, 1):
             for t in range(PACK):
                 sim_pass(u, t, 1)
         gather_rows(0, 0)
-        round_w(0)
+        round_w_on_scalar(0)
         held_first = keep.tile([P, 3, BANK], F32, name="held_first", align_bytes=64)
-        for u in range(3):
-            held[u] = held_first[:, u, :]
         for t in range(PACK):
             sim_pass(0, t, 0)
-        scale_bank(0, 0, held[0])
-        round_w(1)
+        scale_bank(0, 0, held_first[:, 0, :])
+        round_w_on_scalar(1)
         gather_rows(0, 1)
         for t in range(PACK):
             sim_pass(1, t, 0)
-        scale_bank(1, 0, held[1])
-        scale_bank(1, 1, held[2])
+        scale_bank(1, 0, held_first[:, 1, :])
+        scale_bank(1, 1, held_first[:, 2, :])
         gather_rows(0, 2)
+
         sim(2, 0)
-        subtract(0, 0, held[0])
-        subtract(1, 0, held[1])
-        subtract(1, 1, held[2])
-        w_last = slots(8, 2)
-        round_w_on_gpsimd(2, w_last)
+        subtract(0, 0, held_first[:, 0, :])
+        subtract(1, 0, held_first[:, 1, :])
+        subtract(1, 1, held_first[:, 2, :])
+        round_w_on_gpsimd(2)
         for t in range(1, PACK):
-            excess(0, t)
+            read_bank(0, t)
             sim(2, t)
         sim(3, 0)
         sim(3, 1)
-        rectify(0, 0, BANK, slots(0, PACK), True)
+        rectify(0, 0, BANK, True)
         scale_bank(3, 0, held[3])
         subtract(3, 0, held[3])
         for t in range(2, PACK):
-            excess(1, t)
+            read_bank(1, t)
             sim(3, t)
-        rectify(1, 0, BANK, slots(10, PACK), True)
-        excess(2, 0)
+        rectify(1, 0, BANK, True)
+        read_bank(2, 0)
         sim(4, 0)
         for t in range(1, PACK):
-            excess(2, t)
+            read_bank(2, t)
         sim(5, 0)
         scale_bank(4, 0, held[4])
-        rectify(2, 0, BANK, slots(18, PACK), True)
+        rectify(2, 0, BANK, True)
         sim(4, 1)
         sim(5, 2)
-        excess(3, 1)
+        read_bank(3, 1)
         sim(4, 2)
-        excess(3, 2)
+        read_bank(3, 2)
         sim(4, 3)
-        excess(3, 3)
+        read_bank(3, 3)
         sim(5, 1)
-        codes, scales = quantize("zq0", slots(0, 2 * PACK), 2 * BANK, "held3")
+
+        codes, scales = quantize("zq0", slots(RECTIFIED_SLOT[0], 2 * PACK), "held3")
         for b in (0, 1):
             wq[b] = codes[:, BANK + b * N : BANK + (b + 1) * N]
             wq_s[b] = scales[:, BANK + b * N : BANK + (b + 1) * N]
-        aggregate(0, codes[:, :BANK], scales[:, :BANK], 0, BANK, True, False)
-        wq[2], wq_s[2] = quantize("wq2", w_last, N, "w_raw2")
-        zq, zq_s = quantize("zq1", slots(10, PACK), BANK, "zq1")
-        aggregate(1, zq, zq_s, 0, BANK, False, False)
-        rectify(3, 256, BANK, slots(22, PACK)[:, 1024:], False)
+        aggregate(0, FIRST_HALF_BANKS, codes[:, :BANK], scales[:, :BANK])
+        wq[2], wq_s[2] = quantize("wq2", slots(ROUNDED_W_SLOT[2], 2), "w_raw2")
+        aggregate(1, FIRST_HALF_BANKS, *quantize("zq1", rectified[1], "zq1"))
+        rectify(3, UNIT3_ON_SCALAR, BANK, False)
+
         subtract(4, 0, held[4])
-        rectify(3, 0, 256, slots(22, PACK)[:, :1024], True)
+        rectify(3, 0, UNIT3_ON_SCALAR, True)
         scale_bank(5, 0, held[5])
-        excess(4, 1)
+        read_bank(4, 1)
         sim(5, 3)
-        excess(4, 2)
-        excess(4, 3)
-        zq, zq_s = quantize("zq2", slots(18, PACK), BANK, "held4")
-        aggregate(2, zq, zq_s, 0, BANK, False, True)
-        zq, zq_s = quantize("zq3", slots(22, PACK), BANK, "zq3")
-        aggregate(3, zq[:, HALF:], zq_s[:, HALF:], HALF, BANK, True, False)
-        aggregate(3, zq[:, :HALF], zq_s[:, :HALF], 0, HALF, True, False, tiles=(0,))
+        read_bank(4, 2)
+        read_bank(4, 3)
+        aggregate(2, FIRST_HALF_BANKS, *quantize("zq2", rectified[2], "held4"))
+        zq, zq_s = quantize("zq3", rectified[3], "zq3")
+        aggregate(3, HIGH_QUARTER_BANKS, zq[:, HALF:], zq_s[:, HALF:])
+        aggregate(3, LOW_QUARTER_BANKS, zq[:, :HALF], zq_s[:, :HALF], tiles=(0,))
+
         subtract(5, 0, held[5])
-        rectify(4, 0, BANK, slots(14, PACK), True)
-        excess(5, 1)
-        aggregate(3, zq[:, :HALF], zq_s[:, :HALF], 0, HALF, True, False, tiles=(1,))
-        excess(5, 2)
-        excess(5, 3)
+        rectify(4, 0, BANK, True)
+        read_bank(5, 1)
+        aggregate(3, LOW_QUARTER_BANKS, zq[:, :HALF], zq_s[:, :HALF], tiles=(1,))
+        read_bank(5, 2)
+        read_bank(5, 3)
         for n in range(N_TILES):
-            early = slots(2 * n, 2).bitcast(F32)
-            nc.scalar.copy(early, acc[n, 0][:])
+            early = slots(EARLY_RESULT_SLOT[n], 2).bitcast(F32)
+            nc.scalar.copy(early, banks[FIRST_HALF_BANKS[n]][:])
             nc.sync.dma_start(out[n * P : (n + 1) * P, 0:BANK], early)
-        rectify(5, 0, 192, slots(10, 2)[:, :768], True)
-        zq, zq_s = quantize("zq4", slots(14, PACK), BANK, "held5")
-        aggregate(4, zq, zq_s, 0, BANK, False, False)
-        rectify(5, HALF, BANK, slots(12, 2), False)
-        rectify(5, 192, HALF, slots(10, 2)[:, 768:], False)
-        zq, zq_s = quantize("zq5b", slots(12, 2), HALF, "zq5b")
-        aggregate(5, zq, zq_s, HALF, BANK, False, True)
-        zq, zq_s = quantize("zq5a", slots(10, 2), HALF, "zq5a")
-        aggregate(5, zq, zq_s, 0, HALF, False, True)
+
+        rectify(5, 0, UNIT5_ON_SCALAR, True)
+        zq, zq_s = quantize("zq4", rectified[4], "held5")
+        aggregate(4, HIGH_QUARTER_BANKS, zq[:, HALF:], zq_s[:, HALF:])
+        aggregate(4, LOW_QUARTER_BANKS, zq[:, :HALF], zq_s[:, :HALF])
+        rectify(5, HALF, BANK, False)
+        rectify(5, UNIT5_ON_SCALAR, HALF, False)
+        aggregate(5, HIGH_QUARTER_BANKS, *quantize("zq5_high", rectified[5][:, PACK * HALF :], "zq5_high"))
+        aggregate(5, LOW_QUARTER_BANKS, *quantize("zq5_low", rectified[5][:, : PACK * HALF], "zq5_low"))
         result = keep.tile([P, 2, N_TILES, HALF], F32, name="result")
-        for half, pair in ((1, (acc[0, 1], acc[1, 1])), (0, acc_first)):
-            nc.scalar.copy(result[:, half, 0, :], pair[0][:, :HALF])
-            nc.vector.tensor_copy(result[:, half, 1, :], pair[1][:, :HALF])
+        for quarter, sums in ((1, HIGH_QUARTER_BANKS), (0, LOW_QUARTER_BANKS)):
+            nc.scalar.copy(result[:, quarter, 0, :], banks[sums[0]][:, :HALF])
+            nc.vector.tensor_copy(result[:, quarter, 1, :], banks[sums[1]][:, :HALF])
+            c0 = BANK + quarter * HALF
             for n in range(N_TILES):
-                c0 = BANK + half * HALF
-                nc.sync.dma_start(out[n * P : (n + 1) * P, c0 : c0 + HALF], result[:, half, n, :])
+                nc.sync.dma_start(out[n * P : (n + 1) * P, c0 : c0 + HALF], result[:, quarter, n, :])

@@ -32,15 +32,17 @@ BLOCKS = QUADRANTS * ROWS
 LIST_ROWS = 16
 STAGE = P - K_PASSES * BLOCKS
 RESERVE = T // 4
+NO_LIMIT = 3.4e38
 RUN = 8
+UNIT1_ON_GPSIMD = 128
 UNIT3_ON_SCALAR = 288
 UNIT5_ON_SCALAR = 192
 
 UNITS = [(b, h) for h in range(J_HALVES) for b in range(I_PASSES)]
-SIM_BANKS = ((0, 1, 2, 3), (4, 5, 6, 7), (0, 1, 2, 3), (4, 5, 6, 7), (0, 4, 5, 6), (3, 7, 0, 4))
-FIRST_HALF_BANKS = (1, 2)
-LOW_QUARTER_BANKS = (3, 7)
-HIGH_QUARTER_BANKS = (5, 6)
+SIM_BANKS = ((0, 1, 2, 3), (4, 5, 6, 7), (0, 4, 5, 1), (2, 3, 6, 7), (0, 4, 5, 2), (1, 3, 0, 4))
+FIRST_HALF_BANKS = (6, 7)
+LOW_QUARTER_BANKS = (1, 3)
+HIGH_QUARTER_BANKS = (5, 2)
 THRESHOLD_BANKS = (6, 7)
 
 SLOTS = 30
@@ -59,8 +61,8 @@ def tile_list_similarity_join_aggregate_kernel(
         psum = ctx.enter_context(tc.psum_pool(name="psum", bufs=1))
         banks = [psum.tile([P, BANK], F32, name=f"bank{i}") for i in range(8)]
 
-        th_sb = keep.tile([P, J_HALVES, PACK], F32, name="th_sb")
-        g_sb = keep.tile([P, I_PASSES, PACK], F32, name="g_sb")
+        th_sb = keep.tile([P, J_HALVES, 2 * PACK], F32, name="th_sb")
+        g_sb = keep.tile([P, I_PASSES, 2 * PACK], F32, name="g_sb")
 
         probe_scales = keep.tile([P, T2 // 4], I32, name="probe_scales", align_bytes=64)
         row_scales = keep.tile([P, T // 4], I32, name="row_scales", tag="row_scales", align_bytes=64)
@@ -76,11 +78,11 @@ def tile_list_similarity_join_aggregate_kernel(
         probe_table = keep.tile([P, K_PASSES, T2], I32, name="probe_table", align_bytes=64)
         row_table = [keep.tile([P, T], I32, name=f"row_table{a}", align_bytes=64) for a in range(K_PASSES)]
         nc.sync.dma_start(probe_list[:], offs2)
-        nc.scalar.dma_start(th_sb[:], th.rearrange("(h p c) -> p h c", h=J_HALVES, c=PACK))
         nc.sync.dma_start(probe_scales[STAGE:, :], tab2_scales.rearrange("a q t -> (a q) t").bitcast(I32))
-        nc.scalar.dma_start(g_sb[:], g.rearrange("(b p t) -> p b t", b=I_PASSES, t=PACK))
         nc.sync.dma_start(row_list[:], offs)
         nc.sync.dma_start(row_scales[STAGE:, :], tab_scales.rearrange("a q t -> (a q) t").bitcast(I32))
+        nc.sync.dma_start(th_sb[:, :, :PACK], th.rearrange("(h p c) -> p h c", h=J_HALVES, c=PACK))
+        nc.sync.dma_start(g_sb[:, :, :PACK], g.rearrange("(b p t) -> p b t", b=I_PASSES, t=PACK))
         nc.sync.dma_start(probe_table[:], tab2_words.rearrange("a p t i -> p a (t i)").bitcast(I32))
         nc.sync.dma_start(row_table[1][:], tab_words[1].rearrange("p t i -> p (t i)").bitcast(I32))
         last_words = tab_words[0].rearrange("p t i -> p (t i)").bitcast(I32)
@@ -114,8 +116,9 @@ def tile_list_similarity_join_aggregate_kernel(
         def load_w(b):
             nc.sync.dma_start(w_raw[b], w[b * PASS : (b + 1) * PASS, :].rearrange("(p t) n -> p t n", t=PACK))
 
-        load_w(0)
         carry_scales(0)
+        for b in range(I_PASSES):
+            load_w(b)
         plane = [planes[a][:].bitcast(U8)[ROWS * a : P, :] for a in range(K_PASSES)]
         work = keep.tile([P, SLOTS * BANK], BF16, name="work", align_bytes=64)
 
@@ -123,14 +126,12 @@ def tile_list_similarity_join_aggregate_kernel(
             return work[:, first * BANK : (first + count) * BANK]
 
         w4_c = keep.tile([P, I_PASSES, 2 * N // 4], I32, name="w4_c", align_bytes=64)
-        load_w(1)
         nc.sync.dma_start(w4_c[:], w4_words.rearrange("b p c -> p b c").bitcast(I32))
         for q in range(QUADRANTS):
             nc.sync.dma_start(
                 w4_s[32 * q : 32 * q + ROWS, :, :],
                 w4_scales[:, ROWS * q : ROWS * (q + 1), :].rearrange("b r n -> r b n").bitcast(I32),
             )
-        load_w(2)
 
         gth = {}
         for h in range(J_HALVES):
@@ -139,16 +140,19 @@ def tile_list_similarity_join_aggregate_kernel(
                 nc.tensor.transpose(spread[:, c, :], th_sb[:, h, c : c + 1].to_broadcast([P, P]), ident[:])
             for b in range(I_PASSES):
                 for t in range(PACK):
-                    tile = keep.tile([P, BANK], F32, name=f"gth{b}_{t}_{h}", align_bytes=64)
+                    if (b, t, h) == (0, 0, 0):
+                        tile = slots(ROUNDED_W_SLOT[1], 2).bitcast(F32)
+                    else:
+                        tile = keep.tile([P, BANK], F32, name=f"gth{b}_{t}_{h}", align_bytes=64)[:]
                     nc.scalar.activation(
-                        tile[:].rearrange("m (p c) -> m p c", c=PACK),
+                        tile.rearrange("m (p c) -> m p c", c=PACK),
                         spread.rearrange("m c p -> m p c"),
                         ACT.Copy,
                         scale=g_sb[:, b, t : t + 1],
                     )
-                    gth[b, t, h] = tile[:]
+                    gth[b, t, h] = tile
 
-        probes = [keep.tile([P, S2], U32, name=f"probes{a}", align_bytes=64) for a in range(K_PASSES)]
+        probes = {}
         rows = {}
         list_cols = PASS // LIST_ROWS
 
@@ -161,8 +165,17 @@ def tile_list_similarity_join_aggregate_kernel(
             for b in range(count):
                 rows[a, first + b] = tile[:, b * PASS : (b + 1) * PASS]
 
-        for a in (1, 0):
-            nc.vector.tensor_copy(probes[a][:], probe_table[:, a, :].bitcast(U32).indirect(probe_list[:]))
+        def gather_probes(a, first, count, tag):
+            tile = keep.tile([P, count * BANK], U32, name=f"probes{a}_{first}", tag=tag, align_bytes=64)
+            nc.vector.tensor_copy(
+                tile[:],
+                probe_table[:, a, :].bitcast(U32).indirect(probe_list[:, first * list_cols : (first + count) * list_cols]),
+            )
+            for h in range(count):
+                probes[a, first + h] = tile[:, h * BANK : (h + 1) * BANK]
+
+        gather_probes(1, 0, J_HALVES, "probes1")
+        gather_probes(0, 0, J_HALVES, "probes0")
         gather_rows(1, 0)
         gather_rows(1, 1, I_PASSES - 1)
 
@@ -172,7 +185,7 @@ def tile_list_similarity_join_aggregate_kernel(
                 out=banks[SIM_BANKS[u][t]][:],
                 lhsT=rows[a, b][:, t * P : (t + 1) * P].bitcast(FP8X4),
                 lhsT_scale=plane[a][:, S2 + b * PASS + t * P : S2 + b * PASS + (t + 1) * P],
-                rhs=probes[a][:, h * BANK : (h + 1) * BANK].bitcast(FP8X4),
+                rhs=probes[a, h].bitcast(FP8X4),
                 rhs_scale=plane[a][:, h * BANK : (h + 1) * BANK],
                 start=(a == 1),
                 stop=(a == 0),
@@ -203,11 +216,14 @@ def tile_list_similarity_join_aggregate_kernel(
             b, h = UNITS[u]
             nc.gpsimd.tensor_tensor(excess[u][:, t, :], scaled, gth[b, t, h], ALU.subtract)
 
-        def rectify(u, c0, c1, on_scalar):
-            dst = rectified[u][:, PACK * c0 : PACK * c1].rearrange("p (c i t) -> p c t i", i=RUN, t=PACK)
-            src = excess[u][:, :, c0:c1].rearrange("p t (c i) -> p c t i", i=RUN)
-            if on_scalar:
+        def rectify(u, c0, c1, engine):
+            run = 1 if engine == "gpsimd" else RUN
+            dst = rectified[u][:, PACK * c0 : PACK * c1].rearrange("p (c i t) -> p c t i", i=run, t=PACK)
+            src = excess[u][:, :, c0:c1].rearrange("p t (c i) -> p c t i", i=run)
+            if engine == "scalar":
                 nc.scalar.activation(dst, src, ACT.Relu)
+            elif engine == "gpsimd":
+                nc.gpsimd.tensor_scalar(out=dst, in0=src, scalar1=NO_LIMIT, scalar2=0.0, op0=ALU.min, op1=ALU.max)
             else:
                 nc.vector.tensor_scalar(out=dst, in0=src, scalar1=0.0, scalar2=None, op0=ALU.max)
 
@@ -222,20 +238,16 @@ def tile_list_similarity_join_aggregate_kernel(
         wq_s = {}
 
         def add_product(dst, b, n, zq, zq_s, opens, closes):
-            width = zq.shape[1]
             m = slice(n * P, (n + 1) * P)
-            fp4_width = BANK if width == BANK else P
-            for d0 in range(0, width, fp4_width):
-                d = slice(d0, d0 + fp4_width)
-                nc.tensor.matmul_mx(
-                    out=dst[:, d],
-                    lhsT=w4_c[:, b, :].bitcast(U8)[:, 2 * n * P : 2 * (n + 1) * P].bitcast(FP4X4),
-                    lhsT_scale=w4_s[:, b, :].bitcast(U8)[:, m],
-                    rhs=zq[:, d].bitcast(FP8X4),
-                    rhs_scale=zq_s[:, d],
-                    start=opens and d0 == 0,
-                    stop=False,
-                )
+            nc.tensor.matmul_mx(
+                out=dst,
+                lhsT=w4_c[:, b, :].bitcast(U8)[:, 2 * n * P : 2 * (n + 1) * P].bitcast(FP4X4),
+                lhsT_scale=w4_s[:, b, :].bitcast(U8)[:, m],
+                rhs=zq.bitcast(FP8X4),
+                rhs_scale=zq_s,
+                start=opens,
+                stop=False,
+            )
             nc.tensor.matmul_mx(
                 out=dst,
                 lhsT=wq[b][:, m].bitcast(FP8X4),
@@ -267,80 +279,79 @@ def tile_list_similarity_join_aggregate_kernel(
                 op1=ALU.add,
             )
 
-        held = {u: keep.tile([P, BANK], F32, name=f"held{u}", tag=f"held{u}", align_bytes=64)[:] for u in (3, 4, 5)}
+        shared = ((0, 0), (1, 0), (1, 1), (3, 0), (4, 0), (5, 0))
+        held = {(u, t): keep.tile([P, BANK], F32, name=f"held{u}_{t}", align_bytes=64)[:] for u, t in shared}
+
+        def share(u, t):
+            scale_bank(u, t, held[u, t])
+            subtract(u, t, held[u, t])
+
         for u in (0, 1):
             for t in range(PACK):
                 sim_pass(u, t, 1)
-        gather_rows(0, 0)
-        round_w_on_scalar(0)
-        held_first = keep.tile([P, 3, BANK], F32, name="held_first", align_bytes=64)
-        for t in range(PACK):
-            sim_pass(0, t, 0)
-        scale_bank(0, 0, held_first[:, 0, :])
-        round_w_on_scalar(1)
-        gather_rows(0, 1)
-        for t in range(PACK):
-            sim_pass(1, t, 0)
-        scale_bank(1, 0, held_first[:, 1, :])
-        scale_bank(1, 1, held_first[:, 2, :])
-        gather_rows(0, 2)
-
-        sim(2, 0)
-        subtract(0, 0, held_first[:, 0, :])
-        subtract(1, 0, held_first[:, 1, :])
-        subtract(1, 1, held_first[:, 2, :])
-        round_w_on_gpsimd(2)
-        for t in range(1, PACK):
-            read_bank(0, t)
+        for b in range(I_PASSES):
+            gather_rows(0, b)
+        round_w_on_gpsimd(0)
+        for u in (0, 1):
+            for t in range(PACK):
+                sim_pass(u, t, 0)
+        share(0, 0)
+        share(1, 0)
+        share(1, 1)
+        for t in range(3):
             sim(2, t)
-        sim(3, 0)
-        sim(3, 1)
-        rectify(0, 0, BANK, True)
-        scale_bank(3, 0, held[3])
-        subtract(3, 0, held[3])
-        for t in range(2, PACK):
-            read_bank(1, t)
-            sim(3, t)
-        rectify(1, 0, BANK, True)
-        read_bank(2, 0)
-        sim(4, 0)
-        for t in range(1, PACK):
-            read_bank(2, t)
-        sim(5, 0)
-        scale_bank(4, 0, held[4])
-        rectify(2, 0, BANK, True)
-        sim(4, 1)
-        sim(5, 2)
-        read_bank(3, 1)
-        sim(4, 2)
-        read_bank(3, 2)
-        sim(4, 3)
-        read_bank(3, 3)
-        sim(5, 1)
 
-        codes, scales = quantize("zq0", slots(RECTIFIED_SLOT[0], 2 * PACK), "held3")
+        read_bank(0, 1)
+        round_w_on_scalar(1)
+        round_w_on_gpsimd(2)
+        sim(2, 3)
+        read_bank(0, 2)
+        read_bank(0, 3)
+        rectify(0, 0, BANK, "scalar")
+        read_bank(1, 2)
+        read_bank(1, 3)
+        for t in range(PACK):
+            sim(3, t)
+        scale_bank(3, 0, held[3, 0])
+        rectify(1, 0, UNIT1_ON_GPSIMD, "gpsimd")
+        subtract(3, 0, held[3, 0])
+        rectify(1, UNIT1_ON_GPSIMD, BANK, "scalar")
+        for t in range(PACK):
+            read_bank(2, t)
+        for t in range(PACK):
+            sim(4, t)
+        scale_bank(4, 0, held[4, 0])
+        rectify(2, 0, BANK, "scalar")
+        sim(5, 0)
+        read_bank(3, 1)
+        sim(5, 1)
+        read_bank(3, 2)
+        read_bank(3, 3)
+        sim(5, 2)
+
+        codes, scales = quantize("zq0", slots(RECTIFIED_SLOT[0], 2 * PACK), "gth0_2_1")
         for b in (0, 1):
             wq[b] = codes[:, BANK + b * N : BANK + (b + 1) * N]
             wq_s[b] = scales[:, BANK + b * N : BANK + (b + 1) * N]
         aggregate(0, FIRST_HALF_BANKS, codes[:, :BANK], scales[:, :BANK])
-        wq[2], wq_s[2] = quantize("wq2", slots(ROUNDED_W_SLOT[2], 2), "w_raw2")
+        wq[2], wq_s[2] = quantize("wq2", slots(ROUNDED_W_SLOT[2], 2), "gth0_3_1")
         aggregate(1, FIRST_HALF_BANKS, *quantize("zq1", rectified[1], "zq1"))
-        rectify(3, UNIT3_ON_SCALAR, BANK, False)
+        rectify(3, UNIT3_ON_SCALAR, BANK, "vector")
 
-        subtract(4, 0, held[4])
-        rectify(3, 0, UNIT3_ON_SCALAR, True)
-        scale_bank(5, 0, held[5])
+        subtract(4, 0, held[4, 0])
+        rectify(3, 0, UNIT3_ON_SCALAR, "scalar")
+        scale_bank(5, 0, held[5, 0])
         read_bank(4, 1)
         sim(5, 3)
         read_bank(4, 2)
         read_bank(4, 3)
-        aggregate(2, FIRST_HALF_BANKS, *quantize("zq2", rectified[2], "held4"))
+        aggregate(2, FIRST_HALF_BANKS, *quantize("zq2", rectified[2], "held4_0"))
         zq, zq_s = quantize("zq3", rectified[3], "zq3")
         aggregate(3, HIGH_QUARTER_BANKS, zq[:, HALF:], zq_s[:, HALF:])
         aggregate(3, LOW_QUARTER_BANKS, zq[:, :HALF], zq_s[:, :HALF], tiles=(0,))
 
-        subtract(5, 0, held[5])
-        rectify(4, 0, BANK, True)
+        subtract(5, 0, held[5, 0])
+        rectify(4, 0, BANK, "scalar")
         read_bank(5, 1)
         aggregate(3, LOW_QUARTER_BANKS, zq[:, :HALF], zq_s[:, :HALF], tiles=(1,))
         read_bank(5, 2)
@@ -350,12 +361,12 @@ def tile_list_similarity_join_aggregate_kernel(
             nc.scalar.copy(early, banks[FIRST_HALF_BANKS[n]][:])
             nc.sync.dma_start(out[n * P : (n + 1) * P, 0:BANK], early)
 
-        rectify(5, 0, UNIT5_ON_SCALAR, True)
-        zq, zq_s = quantize("zq4", rectified[4], "held5")
+        rectify(5, 0, UNIT5_ON_SCALAR, "scalar")
+        zq, zq_s = quantize("zq4", rectified[4], "held5_0")
         aggregate(4, HIGH_QUARTER_BANKS, zq[:, HALF:], zq_s[:, HALF:])
         aggregate(4, LOW_QUARTER_BANKS, zq[:, :HALF], zq_s[:, :HALF])
-        rectify(5, HALF, BANK, False)
-        rectify(5, UNIT5_ON_SCALAR, HALF, False)
+        rectify(5, HALF, BANK, "vector")
+        rectify(5, UNIT5_ON_SCALAR, HALF, "vector")
         aggregate(5, HIGH_QUARTER_BANKS, *quantize("zq5_high", rectified[5][:, PACK * HALF :], "zq5_high"))
         aggregate(5, LOW_QUARTER_BANKS, *quantize("zq5_low", rectified[5][:, : PACK * HALF], "zq5_low"))
         result = keep.tile([P, 2, N_TILES, HALF], F32, name="result")

@@ -35,13 +35,13 @@ RESERVE = T // 4
 NO_LIMIT = 3.4e38
 RUN = 8
 UNIT1_ON_GPSIMD = 128
-UNIT3_ON_SCALAR = 288
+UNIT3_ON_SCALAR = 256
 UNIT5_ON_SCALAR = 192
 
 UNITS = [(b, h) for h in range(J_HALVES) for b in range(I_PASSES)]
 SIM_BANKS = ((0, 1, 2, 3), (4, 5, 6, 7), (0, 4, 5, 1), (2, 3, 6, 7), (0, 4, 5, 2), (1, 3, 0, 4))
 FIRST_HALF_BANKS = (6, 7)
-LOW_QUARTER_BANKS = (1, 3)
+LOW_QUARTER_BANKS = (0, 4)
 HIGH_QUARTER_BANKS = (5, 2)
 THRESHOLD_BANKS = (6, 7)
 
@@ -65,12 +65,12 @@ def tile_list_similarity_join_aggregate_kernel(
         g_sb = keep.tile([P, I_PASSES, 2 * PACK], F32, name="g_sb")
 
         probe_scales = keep.tile([P, T2 // 4], I32, name="probe_scales", align_bytes=64)
-        row_scales = keep.tile([P, T // 4], I32, name="row_scales", tag="row_scales", align_bytes=64)
+        row_scales = keep.tile([P, T // 4], I32, name="row_scales", align_bytes=64)
         w4_s = keep.tile([P, I_PASSES, N // 4], I32, name="w4_s", align_bytes=64)
         planes = [keep.tile([P, (S2 + S) // 4], I32, name=f"plane{a}", align_bytes=64) for a in range(K_PASSES)]
         nc.vector.memset(probe_scales[:STAGE, :], 0)
         nc.vector.memset(row_scales[:STAGE, :], 0)
-        ident = keep.tile([P, P], F32, name="ident")
+        ident = keep.tile([P, P], F32, name="ident", align_bytes=64)
         make_identity(nc, ident[:])
 
         probe_list = keep.tile([P, S2 // LIST_ROWS], U16, name="probe_list")
@@ -78,7 +78,7 @@ def tile_list_similarity_join_aggregate_kernel(
         probe_table = keep.tile([P, K_PASSES, T2], I32, name="probe_table", align_bytes=64)
         row_table = [keep.tile([P, T], I32, name=f"row_table{a}", align_bytes=64) for a in range(K_PASSES)]
         nc.sync.dma_start(probe_list[:], offs2)
-        nc.sync.dma_start(probe_scales[STAGE:, :], tab2_scales.rearrange("a q t -> (a q) t").bitcast(I32))
+        nc.scalar.dma_start(probe_scales[STAGE:, :], tab2_scales.rearrange("a q t -> (a q) t").bitcast(I32))
         nc.sync.dma_start(row_list[:], offs)
         nc.sync.dma_start(row_scales[STAGE:, :], tab_scales.rearrange("a q t -> (a q) t").bitcast(I32))
         nc.sync.dma_start(th_sb[:, :, :PACK], th.rearrange("(h p c) -> p h c", h=J_HALVES, c=PACK))
@@ -92,7 +92,7 @@ def tile_list_similarity_join_aggregate_kernel(
         row_bytes = keep.tile([P, S], U8, name="row_bytes", align_bytes=64)
         nc.vector.tensor_copy(probe_bytes[:], probe_scales[:].bitcast(U8).indirect(probe_list[:]))
         nc.vector.tensor_copy(row_bytes[:], row_scales[:].bitcast(U8).indirect(row_list[:]))
-        joined = keep.tile([P, S2 + S], U8, name="joined", tag="row_scales", align_bytes=64)
+        joined = keep.tile([P, S2 + S], U8, name="joined", tag="ident", align_bytes=64)
         nc.vector.tensor_copy(joined[:, :S2].bitcast(I32), probe_bytes[:].bitcast(I32))
         nc.vector.tensor_copy(
             joined[:, S2:].rearrange("p (b t m) -> p t b m", t=PACK, m=P),
@@ -140,10 +140,7 @@ def tile_list_similarity_join_aggregate_kernel(
                 nc.tensor.transpose(spread[:, c, :], th_sb[:, h, c : c + 1].to_broadcast([P, P]), ident[:])
             for b in range(I_PASSES):
                 for t in range(PACK):
-                    if (b, t, h) == (0, 0, 0):
-                        tile = slots(ROUNDED_W_SLOT[1], 2).bitcast(F32)
-                    else:
-                        tile = keep.tile([P, BANK], F32, name=f"gth{b}_{t}_{h}", align_bytes=64)[:]
+                    tile = keep.tile([P, BANK], F32, name=f"gth{b}_{t}_{h}", align_bytes=64)[:]
                     nc.scalar.activation(
                         tile.rearrange("m (p c) -> m p c", c=PACK),
                         spread.rearrange("m c p -> m p c"),
@@ -348,20 +345,19 @@ def tile_list_similarity_join_aggregate_kernel(
         aggregate(2, FIRST_HALF_BANKS, *quantize("zq2", rectified[2], "held4_0"))
         zq, zq_s = quantize("zq3", rectified[3], "zq3")
         aggregate(3, HIGH_QUARTER_BANKS, zq[:, HALF:], zq_s[:, HALF:])
-        aggregate(3, LOW_QUARTER_BANKS, zq[:, :HALF], zq_s[:, :HALF], tiles=(0,))
 
         subtract(5, 0, held[5, 0])
         rectify(4, 0, BANK, "scalar")
         read_bank(5, 1)
-        aggregate(3, LOW_QUARTER_BANKS, zq[:, :HALF], zq_s[:, :HALF], tiles=(1,))
-        read_bank(5, 2)
-        read_bank(5, 3)
+        for n in range(N_TILES):
+            read_bank(5, 2 + n)
+            aggregate(3, LOW_QUARTER_BANKS, zq[:, :HALF], zq_s[:, :HALF], tiles=(n,))
+        rectify(5, 0, UNIT5_ON_SCALAR, "scalar")
         for n in range(N_TILES):
             early = slots(EARLY_RESULT_SLOT[n], 2).bitcast(F32)
             nc.scalar.copy(early, banks[FIRST_HALF_BANKS[n]][:])
             nc.sync.dma_start(out[n * P : (n + 1) * P, 0:BANK], early)
 
-        rectify(5, 0, UNIT5_ON_SCALAR, "scalar")
         zq, zq_s = quantize("zq4", rectified[4], "held5_0")
         aggregate(4, HIGH_QUARTER_BANKS, zq[:, HALF:], zq_s[:, HALF:])
         aggregate(4, LOW_QUARTER_BANKS, zq[:, :HALF], zq_s[:, :HALF])

@@ -33,9 +33,9 @@ LIST_ROWS = 16
 STAGE = P - K_PASSES * BLOCKS
 RESERVE = T // 4
 NO_LIMIT = 3.4e38
-RUN = 8
+RUN = 4
 UNIT1_ON_GPSIMD = 128
-UNIT3_ON_SCALAR = 256
+UNIT3_ON_SCALAR = 288
 UNIT5_ON_SCALAR = 192
 
 UNITS = [(b, h) for h in range(J_HALVES) for b in range(I_PASSES)]
@@ -78,7 +78,7 @@ def tile_list_similarity_join_aggregate_kernel(
         probe_table = keep.tile([P, K_PASSES, T2], I32, name="probe_table", align_bytes=64)
         row_table = [keep.tile([P, T], I32, name=f"row_table{a}", align_bytes=64) for a in range(K_PASSES)]
         nc.sync.dma_start(probe_list[:], offs2)
-        nc.scalar.dma_start(probe_scales[STAGE:, :], tab2_scales.rearrange("a q t -> (a q) t").bitcast(I32))
+        nc.sync.dma_start(probe_scales[STAGE:, :], tab2_scales.rearrange("a q t -> (a q) t").bitcast(I32))
         nc.sync.dma_start(row_list[:], offs)
         nc.sync.dma_start(row_scales[STAGE:, :], tab_scales.rearrange("a q t -> (a q) t").bitcast(I32))
         nc.sync.dma_start(th_sb[:, :, :PACK], th.rearrange("(h p c) -> p h c", h=J_HALVES, c=PACK))
@@ -352,12 +352,12 @@ def tile_list_similarity_join_aggregate_kernel(
         for n in range(N_TILES):
             read_bank(5, 2 + n)
             aggregate(3, LOW_QUARTER_BANKS, zq[:, :HALF], zq_s[:, :HALF], tiles=(n,))
-        rectify(5, 0, UNIT5_ON_SCALAR, "scalar")
         for n in range(N_TILES):
             early = slots(EARLY_RESULT_SLOT[n], 2).bitcast(F32)
             nc.scalar.copy(early, banks[FIRST_HALF_BANKS[n]][:])
             nc.sync.dma_start(out[n * P : (n + 1) * P, 0:BANK], early)
 
+        rectify(5, 0, UNIT5_ON_SCALAR, "scalar")
         zq, zq_s = quantize("zq4", rectified[4], "held5_0")
         aggregate(4, HIGH_QUARTER_BANKS, zq[:, HALF:], zq_s[:, HALF:])
         aggregate(4, LOW_QUARTER_BANKS, zq[:, :HALF], zq_s[:, :HALF])

@@ -32,10 +32,8 @@ BLOCKS = QUADRANTS * ROWS
 LIST_ROWS = 16
 STAGE = P - K_PASSES * BLOCKS
 RESERVE = T // 4
-NO_LIMIT = 3.4e38
 RUN = 4
-UNIT1_ON_GPSIMD = 128
-UNIT3_ON_SCALAR = 288
+UNIT3_ON_SCALAR = 256
 UNIT5_ON_SCALAR = 192
 
 UNITS = [(b, h) for h in range(J_HALVES) for b in range(I_PASSES)]
@@ -214,13 +212,10 @@ def tile_list_similarity_join_aggregate_kernel(
             nc.gpsimd.tensor_tensor(excess[u][:, t, :], scaled, gth[b, t, h], ALU.subtract)
 
         def rectify(u, c0, c1, engine):
-            run = 1 if engine == "gpsimd" else RUN
-            dst = rectified[u][:, PACK * c0 : PACK * c1].rearrange("p (c i t) -> p c t i", i=run, t=PACK)
-            src = excess[u][:, :, c0:c1].rearrange("p t (c i) -> p c t i", i=run)
+            dst = rectified[u][:, PACK * c0 : PACK * c1].rearrange("p (c i t) -> p c t i", i=RUN, t=PACK)
+            src = excess[u][:, :, c0:c1].rearrange("p t (c i) -> p c t i", i=RUN)
             if engine == "scalar":
                 nc.scalar.activation(dst, src, ACT.Relu)
-            elif engine == "gpsimd":
-                nc.gpsimd.tensor_scalar(out=dst, in0=src, scalar1=NO_LIMIT, scalar2=0.0, op0=ALU.min, op1=ALU.max)
             else:
                 nc.vector.tensor_scalar(out=dst, in0=src, scalar1=0.0, scalar2=None, op0=ALU.max)
 
@@ -310,9 +305,8 @@ def tile_list_similarity_join_aggregate_kernel(
         for t in range(PACK):
             sim(3, t)
         scale_bank(3, 0, held[3, 0])
-        rectify(1, 0, UNIT1_ON_GPSIMD, "gpsimd")
         subtract(3, 0, held[3, 0])
-        rectify(1, UNIT1_ON_GPSIMD, BANK, "scalar")
+        rectify(1, 0, BANK, "scalar")
         for t in range(PACK):
             read_bank(2, t)
         for t in range(PACK):

from contextlib import ExitStack

import concourse.mybir as mybir
from concourse.masks import make_identity

K, T, S, T2, S2, N = 1024, 4096, 1536, 2048, 1024, 256
FLOPS = 2 * K * S * S2 + 2 * 2 * S * N * S2

F32 = mybir.dt.float32
BF16 = mybir.dt.bfloat16
I32 = mybir.dt.int32
U32 = mybir.dt.uint32
U16 = mybir.dt.uint16
U8 = mybir.dt.uint8
FP8X4 = mybir.dt.float8_e4m3fn_x4
FP4X4 = mybir.dt.float4_e2m1fn_x4
ACT = mybir.ActivationFunctionType
ALU = mybir.AluOpType

P = 128
PACK = 4
PASS = P * PACK
BANK = 512
HALF = BANK // 2
K_PASSES = K // PASS
I_PASSES = S // PASS
J_HALVES = S2 // BANK
N_TILES = N // P
QUADRANTS = 4
ROWS = 4
BLOCKS = QUADRANTS * ROWS
LIST_ROWS = 16
STAGE = P - K_PASSES * BLOCKS
RESERVE = T // 4
RUN = 4
UNIT3_ON_SCALAR = 256
UNIT5_ON_SCALAR = 192

UNITS = [(b, h) for h in range(J_HALVES) for b in range(I_PASSES)]
SIM_BANKS = ((0, 1, 2, 3), (4, 5, 6, 7), (0, 4, 5, 1), (2, 3, 6, 7), (0, 4, 5, 2), (1, 3, 0, 4))
FIRST_HALF_BANKS = (6, 7)
LOW_QUARTER_BANKS = (0, 4)
HIGH_QUARTER_BANKS = (5, 2)
THRESHOLD_BANKS = (6, 7)

SLOTS = 30
EXCESS_SLOT = (22, 18, 14, 26, 10, 25)
RECTIFIED_SLOT = (0, 10, 18, 22, 14, 10)
ROUNDED_W_SLOT = (4, 6, 8)
EARLY_RESULT_SLOT = (0, 2)


def tile_list_similarity_join_aggregate_kernel(
    tc, tab_words, tab_scales, offs, tab2_words, tab2_scales, offs2, th, g, w4_words, w4_scales, w, out
):
    nc = tc.nc
    with ExitStack() as ctx:
        keep = ctx.enter_context(tc.tile_pool(name="keep", bufs=1))
        psum = ctx.enter_context(tc.psum_pool(name="psum", bufs=1))
        banks = [psum.tile([P, BANK], F32, name=f"bank{i}") for i in range(8)]

        th_sb = keep.tile([P, J_HALVES, 2 * PACK], F32, name="th_sb")
        g_sb = keep.tile([P, I_PASSES, 2 * PACK], F32, name="g_sb")

        probe_scales = keep.tile([P, T2 // 4], I32, name="probe_scales", align_bytes=64)
        row_scales = keep.tile([P, T // 4], I32, name="row_scales", align_bytes=64)
        w4_s = keep.tile([P, I_PASSES, N // 4], I32, name="w4_s", align_bytes=64)
        planes = [keep.tile([P, (S2 + S) // 4], I32, name=f"plane{a}", align_bytes=64) for a in range(K_PASSES)]
        nc.vector.memset(probe_scales[:STAGE, :], 0)
        nc.vector.memset(row_scales[:STAGE, :], 0)
        ident = keep.tile([P, P], F32, name="ident", align_bytes=64)
        make_identity(nc, ident[:])

        probe_list = keep.tile([P, S2 // LIST_ROWS], U16, name="probe_list")
        row_list = keep.tile([P, S // LIST_ROWS], U16, name="row_list")
        probe_table = keep.tile([P, K_PASSES, T2], I32, name="probe_table", align_bytes=64)
        row_table = [keep.tile([P, T], I32, name=f"row_table{a}", align_bytes=64) for a in range(K_PASSES)]
        nc.sync.dma_start(probe_list[:], offs2)
        nc.sync.dma_start(probe_scales[STAGE:, :], tab2_scales.rearrange("a q t -> (a q) t").bitcast(I32))
        nc.sync.dma_start(row_list[:], offs)
        nc.sync.dma_start(row_scales[STAGE:, :], tab_scales.rearrange("a q t -> (a q) t").bitcast(I32))
        nc.sync.dma_start(th_sb[:, :, :PACK], th.rearrange("(h p c) -> p h c", h=J_HALVES, c=PACK))
        nc.sync.dma_start(g_sb[:, :, :PACK], g.rearrange("(b p t) -> p b t", b=I_PASSES, t=PACK))
        nc.sync.dma_start(probe_table[:], tab2_words.rearrange("a p t i -> p a (t i)").bitcast(I32))
        nc.sync.dma_start(row_table[1][:], tab_words[1].rearrange("p t i -> p (t i)").bitcast(I32))
        last_words = tab_words[0].rearrange("p t i -> p (t i)").bitcast(I32)
        nc.sync.dma_start(row_table[0][:, :RESERVE], last_words[:, :RESERVE])

        probe_bytes = keep.tile([P, S2], U8, name="probe_bytes", align_bytes=64)
        row_bytes = keep.tile([P, S], U8, name="row_bytes", align_bytes=64)
        nc.vector.tensor_copy(probe_bytes[:], probe_scales[:].bitcast(U8).indirect(probe_list[:]))
        nc.vector.tensor_copy(row_bytes[:], row_scales[:].bitcast(U8).indirect(row_list[:]))
        joined = keep.tile([P, S2 + S], U8, name="joined", tag="ident", align_bytes=64)
        nc.vector.tensor_copy(joined[:, :S2].bitcast(I32), probe_bytes[:].bitcast(I32))
        nc.vector.tensor_copy(
            joined[:, S2:].rearrange("p (b t m) -> p t b m", t=PACK, m=P),
            row_bytes[:].rearrange("p (b m t) -> p t b m", t=PACK, m=P),
        )

        def carry_scales(a):
            for r in range(ROWS):
                first = STAGE + BLOCKS * a + r
                nc.sync.dma_start(
                    planes[a][ROWS * a + r : P : 32, :],
                    joined[first : STAGE + BLOCKS * (a + 1) : ROWS, :].bitcast(I32),
                )

        carry_scales(1)
        nc.sync.dma_start(row_table[0][:, RESERVE:], last_words[:, RESERVE:])
        w_raw = [
            keep.tile([P, PACK, N], F32, name=f"w_raw{b}", tag=f"w_raw{b}", align_bytes=64)[:] for b in range(I_PASSES)
        ]

        def load_w(b):
            nc.sync.dma_start(w_raw[b], w[b * PASS : (b + 1) * PASS, :].rearrange("(p t) n -> p t n", t=PACK))

        carry_scales(0)
        for b in range(I_PASSES):
            load_w(b)
        plane = [planes[a][:].bitcast(U8)[ROWS * a : P, :] for a in range(K_PASSES)]
        work = keep.tile([P, SLOTS * BANK], BF16, name="work", align_bytes=64)

        def slots(first, count):
            return work[:, first * BANK : (first + count) * BANK]

        w4_c = keep.tile([P, I_PASSES, 2 * N // 4], I32, name="w4_c", align_bytes=64)
        nc.sync.dma_start(w4_c[:], w4_words.rearrange("b p c -> p b c").bitcast(I32))
        for q in range(QUADRANTS):
            nc.sync.dma_start(
                w4_s[32 * q : 32 * q + ROWS, :, :],
                w4_scales[:, ROWS * q : ROWS * (q + 1), :].rearrange("b r n -> r b n").bitcast(I32),
            )

        gth = {}
        for h in range(J_HALVES):
            spread = banks[THRESHOLD_BANKS[h]][:].rearrange("m (c p) -> m c p", c=PACK)
            for c in range(PACK):
                nc.tensor.transpose(spread[:, c, :], th_sb[:, h, c : c + 1].to_broadcast([P, P]), ident[:])
            for b in range(I_PASSES):
                for t in range(PACK):
                    tile = keep.tile([P, BANK], F32, name=f"gth{b}_{t}_{h}", align_bytes=64)[:]
                    nc.scalar.activation(
                        tile.rearrange("m (p c) -> m p c", c=PACK),
                        spread.rearrange("m c p -> m p c"),
                        ACT.Copy,
                        scale=g_sb[:, b, t : t + 1],
                    )
                    gth[b, t, h] = tile

        probes = {}
        rows = {}
        list_cols = PASS // LIST_ROWS

        def gather_rows(a, first, count=1):
            tile = keep.tile([P, count * PASS], U32, name=f"rows{a}_{first}", align_bytes=64)
            nc.vector.tensor_copy(
                tile[:].rearrange("p (b t m) -> p b m t", t=PACK, m=P),
                row_table[a][:].bitcast(U32).indirect(row_list[:, first * list_cols : (first + count) * list_cols]),
            )
            for b in range(count):
                rows[a, first + b] = tile[:, b * PASS : (b + 1) * PASS]

        def gather_probes(a, first, count, tag):
            tile = keep.tile([P, count * BANK], U32, name=f"probes{a}_{first}", tag=tag, align_bytes=64)
            nc.vector.tensor_copy(
                tile[:],
                probe_table[:, a, :].bitcast(U32).indirect(probe_list[:, first * list_cols : (first + count) * list_cols]),
            )
            for h in range(count):
                probes[a, first + h] = tile[:, h * BANK : (h + 1) * BANK]

        gather_probes(1, 0, J_HALVES, "probes1")
        gather_probes(0, 0, J_HALVES, "probes0")
        gather_rows(1, 0)
        gather_rows(1, 1, I_PASSES - 1)

        def sim_pass(u, t, a):
            b, h = UNITS[u]
            nc.tensor.matmul_mx(
                out=banks[SIM_BANKS[u][t]][:],
                lhsT=rows[a, b][:, t * P : (t + 1) * P].bitcast(FP8X4),
                lhsT_scale=plane[a][:, S2 + b * PASS + t * P : S2 + b * PASS + (t + 1) * P],
                rhs=probes[a, h].bitcast(FP8X4),
                rhs_scale=plane[a][:, h * BANK : (h + 1) * BANK],
                start=(a == 1),
                stop=(a == 0),
            )

        def sim(u, t):
            sim_pass(u, t, 1)
            sim_pass(u, t, 0)

        excess = [slots(first, PACK).rearrange("p (t j) -> p t j", t=PACK) for first in EXCESS_SLOT]
        rectified = [slots(first, PACK) for first in RECTIFIED_SLOT]

        def read_bank(u, t):
            b, h = UNITS[u]
            nc.vector.scalar_tensor_tensor(
                out=excess[u][:, t, :],
                in0=banks[SIM_BANKS[u][t]][:],
                scalar=g_sb[:, b, t : t + 1],
                in1=gth[b, t, h],
                op0=ALU.mult,
                op1=ALU.subtract,
            )

        def scale_bank(u, t, scaled):
            nc.scalar.activation(scaled, banks[SIM_BANKS[u][t]][:], ACT.Copy, scale=g_sb[:, UNITS[u][0], t : t + 1])

        def subtract(u, t, scaled):
            b, h = UNITS[u]
            nc.gpsimd.tensor_tensor(excess[u][:, t, :], scaled, gth[b, t, h], ALU.subtract)

        def rectify(u, c0, c1, engine):
            dst = rectified[u][:, PACK * c0 : PACK * c1].rearrange("p (c i t) -> p c t i", i=RUN, t=PACK)
            src = excess[u][:, :, c0:c1].rearrange("p t (c i) -> p c t i", i=RUN)
            if engine == "scalar":
                nc.scalar.activation(dst, src, ACT.Relu)
            else:
                nc.vector.tensor_scalar(out=dst, in0=src, scalar1=0.0, scalar2=None, op0=ALU.max)

        def quantize(name, src, tag):
            width = src.shape[1] // PACK
            codes = keep.tile([P, width], U32, name=name, tag=tag, align_bytes=64)
            scales = keep.tile([P, width], U8, name=name + "_s", align_bytes=64)
            nc.vector.quantize_mx(out=codes[:].bitcast(FP8X4), scales=scales[:], in_=src)
            return codes[:], scales[:]

        wq = {}
        wq_s = {}

        def add_product(dst, b, n, zq, zq_s, opens, closes):
            m = slice(n * P, (n + 1) * P)
            nc.tensor.matmul_mx(
                out=dst,
                lhsT=w4_c[:, b, :].bitcast(U8)[:, 2 * n * P : 2 * (n + 1) * P].bitcast(FP4X4),
                lhsT_scale=w4_s[:, b, :].bitcast(U8)[:, m],
                rhs=zq.bitcast(FP8X4),
                rhs_scale=zq_s,
                start=opens,
                stop=False,
            )
            nc.tensor.matmul_mx(
                out=dst,
                lhsT=wq[b][:, m].bitcast(FP8X4),
                lhsT_scale=wq_s[b][:, m],
                rhs=zq.bitcast(FP8X4),
                rhs_scale=zq_s,
                start=False,
                stop=closes,
            )

        def aggregate(u, sums, zq, zq_s, tiles=range(N_TILES)):
            b = UNITS[u][0]
            for n in tiles:
                add_product(banks[sums[n]][:, : zq.shape[1]], b, n, zq, zq_s, b == 0, b == I_PASSES - 1)

        def round_w_on_scalar(b):
            nc.scalar.copy(
                slots(ROUNDED_W_SLOT[b], 2).rearrange("p (c i t) -> p c t i", i=RUN, t=PACK),
                w_raw[b].rearrange("p t (c i) -> p c t i", i=RUN),
            )

        def round_w_on_gpsimd(b):
            nc.gpsimd.tensor_scalar(
                out=slots(ROUNDED_W_SLOT[b], 2).rearrange("p (n t) -> p n t", t=PACK),
                in0=w_raw[b].rearrange("p t n -> p n t"),
                scalar1=1.0,
                scalar2=0.0,
                op0=ALU.mult,
                op1=ALU.add,
            )

        shared = ((0, 0), (1, 0), (1, 1), (3, 0), (4, 0), (5, 0))
        held = {(u, t): keep.tile([P, BANK], F32, name=f"held{u}_{t}", align_bytes=64)[:] for u, t in shared}

        def share(u, t):
            scale_bank(u, t, held[u, t])
            subtract(u, t, held[u, t])

        for u in (0, 1):
            for t in range(PACK):
                sim_pass(u, t, 1)
        for b in range(I_PASSES):
            gather_rows(0, b)
        round_w_on_gpsimd(0)
        for u in (0, 1):
            for t in range(PACK):
                sim_pass(u, t, 0)
        share(0, 0)
        share(1, 0)
        share(1, 1)
        for t in range(3):
            sim(2, t)

        read_bank(0, 1)
        round_w_on_scalar(1)
        round_w_on_gpsimd(2)
        sim(2, 3)
        read_bank(0, 2)
        read_bank(0, 3)
        rectify(0, 0, BANK, "scalar")
        read_bank(1, 2)
        read_bank(1, 3)
        for t in range(PACK):
            sim(3, t)
        scale_bank(3, 0, held[3, 0])
        subtract(3, 0, held[3, 0])
        rectify(1, 0, BANK, "scalar")
        for t in range(PACK):
            read_bank(2, t)
        for t in range(PACK):
            sim(4, t)
        scale_bank(4, 0, held[4, 0])
        rectify(2, 0, BANK, "scalar")
        sim(5, 0)
        read_bank(3, 1)
        sim(5, 1)
        read_bank(3, 2)
        read_bank(3, 3)
        sim(5, 2)

        codes, scales = quantize("zq0", slots(RECTIFIED_SLOT[0], 2 * PACK), "gth0_2_1")
        for b in (0, 1):
            wq[b] = codes[:, BANK + b * N : BANK + (b + 1) * N]
            wq_s[b] = scales[:, BANK + b * N : BANK + (b + 1) * N]
        aggregate(0, FIRST_HALF_BANKS, codes[:, :BANK], scales[:, :BANK])
        wq[2], wq_s[2] = quantize("wq2", slots(ROUNDED_W_SLOT[2], 2), "gth0_3_1")
        aggregate(1, FIRST_HALF_BANKS, *quantize("zq1", rectified[1], "zq1"))
        rectify(3, UNIT3_ON_SCALAR, BANK, "vector")

        subtract(4, 0, held[4, 0])
        rectify(3, 0, UNIT3_ON_SCALAR, "scalar")
        scale_bank(5, 0, held[5, 0])
        read_bank(4, 1)
        sim(5, 3)
        read_bank(4, 2)
        read_bank(4, 3)
        aggregate(2, FIRST_HALF_BANKS, *quantize("zq2", rectified[2], "held4_0"))
        zq, zq_s = quantize("zq3", rectified[3], "zq3")
        aggregate(3, HIGH_QUARTER_BANKS, zq[:, HALF:], zq_s[:, HALF:])

        subtract(5, 0, held[5, 0])
        rectify(4, 0, BANK, "scalar")
        read_bank(5, 1)
        for n in range(N_TILES):
            read_bank(5, 2 + n)
            aggregate(3, LOW_QUARTER_BANKS, zq[:, :HALF], zq_s[:, :HALF], tiles=(n,))
        for n in range(N_TILES):
            early = slots(EARLY_RESULT_SLOT[n], 2).bitcast(F32)
            nc.scalar.copy(early, banks[FIRST_HALF_BANKS[n]][:])
            nc.sync.dma_start(out[n * P : (n + 1) * P, 0:BANK], early)

        rectify(5, 0, UNIT5_ON_SCALAR, "scalar")
        zq, zq_s = quantize("zq4", rectified[4], "held5_0")
        aggregate(4, HIGH_QUARTER_BANKS, zq[:, HALF:], zq_s[:, HALF:])
        aggregate(4, LOW_QUARTER_BANKS, zq[:, :HALF], zq_s[:, :HALF])
        rectify(5, HALF, BANK, "vector")
        rectify(5, UNIT5_ON_SCALAR, HALF, "vector")
        aggregate(5, HIGH_QUARTER_BANKS, *quantize("zq5_high", rectified[5][:, PACK * HALF :], "zq5_high"))
        aggregate(5, LOW_QUARTER_BANKS, *quantize("zq5_low", rectified[5][:, : PACK * HALF], "zq5_low"))
        result = keep.tile([P, 2, N_TILES, HALF], F32, name="result")
        for quarter, sums in ((1, HIGH_QUARTER_BANKS), (0, LOW_QUARTER_BANKS)):
            nc.scalar.copy(result[:, quarter, 0, :], banks[sums[0]][:, :HALF])
            nc.vector.tensor_copy(result[:, quarter, 1, :], banks[sums[1]][:, :HALF])
            c0 = BANK + quarter * HALF
            for n in range(N_TILES):
                nc.sync.dma_start(out[n * P : (n + 1) * P, c0 : c0 + HALF], result[:, quarter, n, :])
